import numpy as np, ml_dtypes
CORES = [3,7,11,15,131,135,139,143]
N = 8
BF = ml_dtypes.bfloat16
W, Q, TV, HOP, M = 2048, 256, 6, 5, 10
def parts(rng):
    hi = rng.choice(np.array([64, 128, 192, 256]), (N, 8, 1, W)); p = np.floor(hi * rng.random((N, 8, 16, W)))
    lo = rng.choice(np.array([0, 32, 64, 128, 192]), (N, 8, 1, Q)); y = lo + np.floor((256 - lo) * rng.random((N, 8, 16, Q)))
    L = rng.integers(0, W, (N, 8, 16, Q)); share = rng.choice(np.array([0.0, 0.1, 0.3, 0.7, 1.0]), (N, 8, 1, Q))
    C = np.where(rng.random((N, 8, 16, Q)) < share, rng.integers(0, W, (N, 8, 16, Q)), -1)
    o = rng.integers(0, 16, (N, 8, 16, Q)); b = np.minimum(rng.integers(0, 8, (N, 8, 16, Q)), rng.integers(0, 8, (N, 8, 16, Q)))
    return p, y, L, C, o, b, rng.integers(0, 4, (N, 8, 16, TV))
def pack(p, y, L, C, o, b, lim):
    def half(a): return np.ascontiguousarray(np.asarray(a, np.float32).reshape(N, 128, -1)).astype(BF)
    def whole(a): return np.ascontiguousarray(np.asarray(a).reshape(N, 128, -1)).astype(np.int32)
    return {"prop": half(p), "lem": whole(L), "con": whole(C), "org": half(o), "cnt": half(b), "ex": half(y), "lim": whole(lim)}
def setup_inputs(rng):
    return pack(*parts(rng))
def setup_inputs_spread(rng):
    p, y, L, C, o, b, lim = parts(rng)
    p = np.minimum(np.floor(np.exp2(8 * rng.random((N, 8, 1, W))) * rng.random((N, 8, 16, W))), 255)
    y = np.minimum(np.floor(np.exp2(2 + 6 * rng.random((N, 8, 1, Q))) * rng.random((N, 8, 16, Q))), 255)
    y = np.where(rng.random((N, 8, 1, Q)) < 0.5, 255 - y, y)
    L = np.minimum(np.floor(W * rng.random((N, 8, 16, Q)) ** 3), W - 1)
    C = np.where(C >= 0, W - 1 - np.minimum(np.floor(W * rng.random((N, 8, 16, Q)) ** 3), W - 1), -1)
    o = np.minimum(np.floor(16 * rng.random((N, 8, 16, Q)) ** 2), 15); b = rng.integers(0, 8, (N, 8, 16, Q))
    return pack(p, y, L, C, o, b, lim)
def setup_inputs_ends(rng):
    p = 255 * (rng.random((N, 8, 16, W)) < rng.choice(np.array([0.0, 0.5, 1.0]), (N, 8, 1, W))).astype(np.int64)
    y = 255 * (rng.random((N, 8, 16, Q)) < rng.choice(np.array([0.0, 0.5, 1.0]), (N, 8, 1, Q))).astype(np.int64)
    just = np.argsort(rng.random((N, 8, 16, Q)), axis=2) < 16 - M
    y = np.where(rng.random((N, 8, 1, Q)) < 0.25, 255 * just, y)
    L = (W - 1) * rng.integers(0, 2, (N, 8, 16, Q)); share = rng.choice(np.array([0.0, 0.5, 1.0]), (N, 8, 1, Q))
    C = np.where(rng.random((N, 8, 16, Q)) < share, W - 1, -1)
    o = 15 * rng.integers(0, 2, (N, 8, 16, Q)); b = 7 * rng.integers(0, 2, (N, 8, 16, Q)); lim = 3 * rng.integers(0, 2, (N, 8, 16, TV))
    turn = int(rng.integers(0, 4))
    for r in range(N):
        for g in range(8):
            w = (r + g + turn) % 4
            if (r, g) in ((0, 0), (N - 1, 7)): w = 3
            if (r, g) in ((0, 7), (N - 1, 6)): w = 1
            pm = rng.permutation(16)
            p[r, g, :, 0] = (0 * pm, 0 * pm + 255, 255 * (pm < M), 0 * pm)[w]
            p[r, g, :, W - 1] = (0 * pm + 255, 0 * pm, 255 * (pm < M - 1), 0 * pm)[w]
            for c in (0, Q - 1):
                if w == 3: y[r, g, :, c] = 255
                if w == 1:
                    y[r, g, :, c] = 0; L[r, g, :, c] = W - 1; L[r, g, 15, c] = 0; C[r, g, :, c] = W - 1; C[r, g, 15, c] = -1
                if w == 0:
                    y[r, g, :, c] = 254 + (pm < 16 - M); L[r, g, :, c] = 0; L[r, g, 15, c] = W - 1; C[r, g, :, c] = 0
    return pack(p, y, L, C, o, b, lim)
def setup_inputs_corners(rng):
    p, y, L, C, o, b, lim = parts(rng)
    p[..., :W // 4] = np.floor(0.125 * p[..., :W // 4]); p[..., W // 2:] = 96 + np.floor(160 * rng.random((N, 8, 16, W - W // 2))); p[..., W - 1] = 255
    y = 32 + np.floor(224 * rng.random((N, 8, 16, Q))); y = np.where(rng.random((N, 8, 1, Q)) < 0.125, 255, y)
    e = (np.arange(Q).reshape(1, 1, 1, Q) + rng.integers(0, 6, (N, 8, 1, 1))) % 6; k = np.arange(16).reshape(1, 1, 16, 1)
    name = np.where(rng.random((N, 8, 1, Q)) < 0.6, rng.integers(0, W // 4, (N, 8, 16, Q)), rng.integers(0, W, (N, 8, 16, Q)))
    hole = rng.choice(np.array([0, 15, 15, 6]), (N, 8, 1, Q))
    has = np.where(e == 0, False, np.where(e == 2, k != hole, np.where(e == 3, k == 15, True)))
    C = np.where(has, name, -1)
    L = np.where(rng.random((N, 8, 1, Q)) < 0.5, rng.integers(W // 2, W, (N, 8, 16, Q)), L)
    mode = rng.integers(0, 4, (N, 8, 1, Q)); o = np.where(mode == 0, k, np.where(mode == 1, 0, np.where(mode == 2, 15, o)))
    b = rng.choice(np.array([0, 0, 1, 3, 6, 7]), (N, 8, 16, Q)); b = np.where(e == 4, 7, np.where(e == 5, 7 * (k == 15), b))
    lim = 3 * rng.integers(0, 2, (N, 8, 16, TV))
    for c in (Q - 2, Q - 1):
        y[:, :, :, c] = 0; C[:, :, :, c] = -1; C[:, :, 15, c] = W - 1; b[:, :, 15, c] = 0
    y[:, 0, :, Q - 2] = 255; C[:, 0, :, Q - 2] = -1
    return pack(p, y, L, C, o, b, lim)
def setup_inputs_ties(rng):
    p, y, L, C, o, b, lim = parts(rng)
    base = rng.integers(2, 254, (1, 8, 16, 1))
    m = np.where(rng.random((N, 8, 1, W)) < 0.06, M + rng.integers(0, 2, (N, 8, 1, W)), rng.choice(np.array([M - 1, M - 1, M - 2, 0]), (N, 8, 1, W)))
    up = np.argsort(rng.random((N, 8, 16, W)), axis=2) < m
    p = base + np.where(m == 0, 0, np.where(up, 1, 0 - rng.integers(0, 2, (N, 8, 16, W))))
    y = base + np.where(rng.random((N, 8, 1, Q)) < 0.6, 0, rng.integers(-1, 2, (N, 8, 16, Q)))
    b = rng.integers(0, 3, (N, 8, 16, Q))
    p[..., :80] = (np.arange(80).reshape(1, 80) + np.arange(16).reshape(16, 1)) >> 4
    y[..., Q - 16:] = 255; L[..., Q - 16:] = rng.integers(0, 80, (N, 8, 16, 16)); L[..., Q - 8:] = rng.integers(0, 2, (N, 8, 16, 8))
    L[:, :, 0, Q - 16:] = 0; L[:, :, 15, Q - 8:] = 1
    us = np.arange(2048, 4081 - M).reshape(-1, 1); names = np.arange(2048, W).reshape(1, -1); x = us * names
    iu, ia = np.nonzero(((x & 63) == 32) & (x > 2 ** 23) & ((((x >> 5) + names + 97) & 255) == 0) & ((names & 255) < Q - 16))
    if len(iu) > 0:
        for g in range(8):
            s = int(rng.integers(0, len(iu))); u = int(us[iu[s], 0]); a = int(names[0, ia[s]]); c = a & 255
            p[:, g, :, a] = 255; y[:, g, :, c] = (u + np.argsort(rng.random((N, 16)), axis=1)) >> 4
            C[:, g, :, c] = -1; C[:, g, 0, c] = a; o[:, g, 0, c] = 0; b[:, g, 0, c] = 7
    return pack(p, y, L, C, o, b, lim)
def setup_inputs_alike(rng):
    p, y, L, C, o, b, lim = parts(rng); c = np.arange(Q).reshape(1, 1, 1, Q)
    few = np.array([0, W - 1, W // 2, 3])
    L[:, 0::4] = rng.choice(few, (N, 2, 16, Q))
    L[:, 1::4] = np.repeat(L[:, 1::4, :1], 16, axis=2)
    L[:, 2::4] = 256 * rng.integers(0, W // 256, (N, 2, 16, Q)) + c
    L[:, 3::4] = 256 * rng.integers(0, W // 256, (N, 2, 16, Q)) + (c + 1) % Q
    own = rng.random((N, 8, 1, Q)) < 0.5
    C = np.where((C >= 0) & own, L[:, :, ::-1], C); b[:, ::2] = 2
    return pack(p, y, L, C, o, b, lim)
def check_inputs(d):
    bad = []
    for k, lo, hi in (("prop", 0, 255), ("lem", 0, W - 1), ("con", -1, W - 1), ("org", 0, 15), ("cnt", 0, 7), ("ex", 0, 255), ("lim", 0, 3)):
        a = np.asarray(d[k]).astype(np.float64)
        if not (np.min(a) >= lo and np.max(a) <= hi): bad.append("range of " + k)
        elif not np.all(a == np.floor(a)): bad.append("whole numbers in " + k)
    return bad
def pick(p, a):
    return np.take_along_axis(p, a.reshape(N, 8, 1, 16 * Q), 3).reshape(N, 8, 16, 16, Q)
def at(a, k):
    return np.take_along_axis(a, k[:, :, None, :], 2)[:, :, 0]
def reference(prop, lem, con, org, cnt, ex, lim):
    p = prop.astype(np.float32).astype(np.int16).reshape(N, 8, 16, W); y = ex.astype(np.float32).astype(np.int16).reshape(N, 8, 16, Q)
    L = lem.astype(np.int64).reshape(N, 8, 16, Q); C = con.astype(np.int64).reshape(N, 8, 16, Q)
    o = org.astype(np.float32).astype(np.int64).reshape(N, 8, 16, Q); b = cnt.astype(np.float32).astype(np.int64).reshape(N, 8, 16, Q)
    lm = lim.astype(np.int64).reshape(N, 8, 16, TV); w = np.zeros((N, Q), np.int64)
    rows = np.arange(16).reshape(1, 1, 16, 1); lane = np.arange(Q).reshape(1, 1, Q)
    for t in range(TV):
        y5 = y[:, :, :, None, :]; pl = pick(p, L); pc = pick(p, np.maximum(C, 0))
        bar = (np.add.reduce(pc > y5, axis=2, dtype=np.int64) >= M) & (C >= 0)
        gui = np.add.reduce(pl > y5, axis=2, dtype=np.int64) >= M
        score = np.add.reduce(np.abs(pl - y5), axis=2, dtype=np.int64); u = np.add.reduce(y, axis=2, dtype=np.int64)
        barred = np.any(bar, axis=2); some = np.any(gui, axis=2); guilty = ~barred & some; clear = ~barred & ~some
        kb = np.argmax(bar, axis=2); hit = barred[:, :, None] & (rows == kb[:, :, None]); b1 = b + hit
        over = hit & (b1 > lm[:, :, :, t:t + 1] + w[:, None, None, :]); back = np.any(over, axis=2)
        L1 = np.where(back[:, :, None] & (rows == at(o, kb)[:, :, None]), at(C, kb)[:, :, None], L)
        C1 = np.where(over, -1, C); b1 = np.where(over, 0, b1)
        kg = np.argmax(gui, axis=2); old = at(L, kg); empty = C < 0
        slot = np.where(np.any(empty, axis=2), np.argmax(empty, axis=2), np.argmax(b, axis=2)); put = guilty[:, :, None] & (rows == slot[:, :, None])
        n = ((((u * old) >> 5) + old + 97 * t) & (W - 256)) + lane
        C1 = np.where(put, old[:, :, None], C1); o1 = np.where(put, kg[:, :, None], o); b1 = np.where(put, 0, b1)
        L1 = np.where(guilty[:, :, None] & (rows == kg[:, :, None]), n[:, :, None], L1)
        pv = np.take_along_axis(pl, kg[:, :, None, None, :], 3)[:, :, :, 0]
        np.put_along_axis(p, n[:, :, None, :], np.where(guilty[:, :, None], np.minimum(pv, y), np.take_along_axis(p, n[:, :, None, :], 3)), 3)
        y = np.where(guilty[:, :, None], np.abs(y - pv), y)
        ks = np.argmin(score, axis=2); new = (((u * u) >> 5) + 37 * u + t) & (W - 1)
        L1 = np.where(clear[:, :, None] & (rows == ks[:, :, None]), new[:, :, None], L1)
        w = np.add.reduce(barred, axis=1, dtype=np.int64) & 3
        L, C, o, b = L1, C1, o1, b1
        if t < TV - 1: L, C, o, b = [np.roll(a, HOP, axis=0) for a in (L, C, o, b)]
    def half(a): return a.reshape(N, 128, -1).astype(np.float32).astype(BF)
    return {"zp": half(p), "zl": L.reshape(N, 128, Q).astype(np.float32), "zc": C.reshape(N, 128, Q).astype(np.float32), "zo": half(o), "zb": half(b), "zy": half(y)}

@@ -1,0 +1,564 @@
+from concourse.mybir import AluOpType as A, ActivationFunctionType as AF, AxisListType as AX
+
+TV, HOP = 6, 5
+BIG = float(2 ** 26)
+CAP = float(2 ** 24)
+W = 256
+SCRATCH = {
+    "P": ("sbuf", [128, 4352], "bfloat16"), "NID": ("sbuf", [128, 128], "bfloat16"),
+    "PC": ("sbuf", [128, 16, 256], "bfloat16"), "PL": ("sbuf", [128, 16, 256], "bfloat16"),
+    "XC": ("sbuf", [128, 16, 256], "bfloat16"), "XL": ("sbuf", [128, 16, 256], "bfloat16"),
+    "DL": ("sbuf", [128, 16, 256], "bfloat16"), "AB": ("sbuf", [128, 16, 256], "bfloat16"),
+    "yv": ("sbuf", [128, 256], "bfloat16"), "dv": ("sbuf", [128, 256], "bfloat16"), "mn": ("sbuf", [128, 256], "bfloat16"),
+    "C16": ("sbuf", [128, 256 * TV], "uint16"), "L16": ("sbuf", [128, 256 * TV], "uint16"),
+    "PK": ("sbuf", [128, 256 * TV], "int32"), "LK": ("sbuf", [128, 256 * TV], "int32"),
+    "oC16": ("sbuf", [128, 256 * TV], "uint16"), "oL16": ("sbuf", [128, 256 * TV], "uint16"),
+    "oPK": ("sbuf", [128, 256 * TV], "int32"), "oLK": ("sbuf", [128, 256 * TV], "int32"),
+    "lemA": ("sbuf", [128, 256], "int32"), "conA": ("sbuf", [128, 256], "int32"), "limA": ("sbuf", [128, TV], "int32"),
+    "orgA": ("sbuf", [128, 256], "bfloat16"), "cntA": ("sbuf", [128, 256], "bfloat16"),
+    "f0": ("sbuf", [128, 256], "float32"), "f1": ("sbuf", [128, 256], "float32"), "f2": ("sbuf", [128, 256], "float32"),
+    "f3": ("sbuf", [128, 256], "float32"), "f4": ("sbuf", [128, 256], "float32"), "zPK": ("sbuf", [128, 256], "float32"), "zLK": ("sbuf", [128, 256], "float32"),
+    "i0": ("sbuf", [128, 256], "int32"), "i1": ("sbuf", [128, 256], "int32"),
+    "i2": ("sbuf", [128, 256], "int32"), "h0": ("sbuf", [128, 256], "bfloat16"), "h1": ("sbuf", [128, 256], "bfloat16"),
+    "KC": ("sbuf", [128, 256], "float32"), "key": ("sbuf", [128, 256], "float32"),
+    "keyS": ("sbuf", [128, 256], "float32"), "SS": ("sbuf", [128, 256], "float32"),
+    "SB": ("sbuf", [128, 256], "float32"), "SG": ("sbuf", [128, 256], "float32"), "SC": ("sbuf", [128, 256], "float32"),
+    "RC": ("sbuf", [128, 256], "bfloat16"), "RL": ("sbuf", [128, 256], "bfloat16"),
+    "eC": ("sbuf", [128, 256], "bfloat16"), "eL": ("sbuf", [128, 256], "bfloat16"),
+    "EVC": ("sbuf", [128, 256], "float32"), "EVL": ("sbuf", [128, 256], "float32"),
+    "ERC": ("sbuf", [128, 256], "bfloat16"), "ERL": ("sbuf", [128, 256], "bfloat16"),
+    "Yp": ("sbuf", [128, 16, 32], "float32"), "Yl": ("sbuf", [128, 16, 32], "float32"), "Z": ("sbuf", [128, 16, 32], "float32"),
+    "ones": ("sbuf", [128, 256], "bfloat16"), "ID": ("sbuf", [128, 128], "bfloat16"), "BT": ("sbuf", [128, 128], "bfloat16"),
+    "BLK": ("sbuf", [128, 128], "bfloat16"), "RK": ("sbuf", [128, 256], "bfloat16"), "mt": ("sbuf", [128, 128], "bfloat16"),
+    "SELC": ("sbuf", [128, 2048], "bfloat16"), "SELS": ("sbuf", [128, 2048], "bfloat16"),
+    "THR": ("sbuf", [128, 256], "bfloat16"), "KI": ("sbuf", [128, 256], "float32"), "KB": ("sbuf", [128, 256], "bfloat16"),
+    "D0": ("sbuf", [128, 256], "float32"), "D1": ("sbuf", [128, 256], "float32"), "D1h": ("sbuf", [128, 256], "bfloat16"),
+    "fb": ("sbuf", [128, 256], "float32"), "RLM": ("sbuf", [128, 256 * TV], "bfloat16"), "limf": ("sbuf", [128, TV], "float32"),
+    "col": ("sbuf", [128, 8], "float32"), "cb": ("sbuf", [128, 16], "float32"), "kq": ("sbuf", [128, 16], "float32"),
+    "LF": ("sbuf", [128, 16 * 64], "float32"), "LI": ("sbuf", [128, 16 * 64], "int32"), "bfl": ("sbuf", [128, 16], "bfloat16"),
+    "U16": ("sbuf", [128, 32], "uint16"),
+    "pC": ("psum", [128, 512], "float32"), "pL": ("psum", [128, 512], "float32"), "pS": ("psum", [128, 512], "float32"),
+    "pM": ("psum", [128, 512], "float32"), "pY": ("psum", [128, 32, 16], "float32"), "pT": ("psum", [128, 512], "float32"),
+    "pD0": ("psum", [128, 16, 32], "float32"), "pD1": ("psum", [128, 16, 32], "float32"),
+}
+_LOADS = ["prop", "lem", "con", "ex", "lim", "org", "cnt"]
+_KINDS = ["C16", "PK", "L16", "LK"]
+SEMAPHORES = (["qV", "qS", "qP", "qG", "sent", "outs"] + ["ld_" + n for n in _LOADS]
+              + ["a%s_%d" % (k, t) for k in _KINDS for t in range(1, TV)])
+
+
+def rank_program(g, core, T, topo):
+    rank = T.rank_of(core)
+    if rank is None:
+        return
+    eng = {"V": g.vector, "S": g.scalar, "P": g.tensor, "G": g, "Y": g.sync}
+    cnt = {}
+    seen = {q: {} for q in eng}
+    snap = {}
+    ops, wrote, read, run = [], {}, {}, {}
+
+    def require(q, dep):
+        s, n = dep
+        if seen[q].get(s, 0) >= n:
+            return
+        eng[q].wait_ge(T.sem[s], n)
+        for a, b in list(snap.get(dep, {}).items()) + [dep]:
+            if seen[q].get(a, 0) < b:
+                seen[q][a] = b
+
+    banks = {"pC", "pL", "pS", "pM", "pY", "pT", "pD0", "pD1"}
+
+    def do(q, reads, writes, calls, us=0.06, kind="call"):
+        i, deps = len(ops), set()
+        for t in reads + writes:
+            deps |= wrote.get(t, set())
+        for t in writes:
+            deps |= read.get(t, set())
+        for b in {t.split(":")[0] for t in reads + writes} & banks:
+            r = run.setdefault(b, [q, [], []])
+            if r[0] != q:
+                run[b] = r = [q, [], r[1]]
+            r[1].append(i)
+            deps |= set(r[2])
+        for t in writes:
+            wrote[t], read[t] = {i}, set()
+        for t in reads:
+            read.setdefault(t, set()).add(i)
+        deps.discard(i)
+        ops.append({"q": q, "deps": deps, "calls": calls, "us": us, "kind": kind})
+        return ops[-1]
+
+    def emit():
+        lat, slack = 0.12, 0.1
+        n = len(ops)
+        succ, left = [[] for _ in ops], [len(o["deps"]) for o in ops]
+        for i, o in enumerate(ops):
+            for d in o["deps"]:
+                succ[d].append(i)
+        prio, start, end, rdy = [0.0] * n, [0.0] * n, [0.0] * n, [0.0] * n
+        for i in range(n - 1, -1, -1):
+            prio[i] = -i
+        free, pool = {q: 0.0 for q in "VSPGYN"}, {q: set() for q in "VSPGYN"}
+        for i in range(n):
+            if not left[i]:
+                pool[ops[i]["q"]].add(i)
+        done = []
+        while len(done) < n:
+            best = None
+            for q, c in pool.items():
+                if not c:
+                    continue
+                f = free[q] if q != "N" else 0.0
+                top = max(c, key=lambda i: (prio[i], -i))
+                lim = max(f, rdy[top]) + slack
+                fit = [i for i in c if q == "V" and i < top + 30 and max(f, rdy[i]) + ops[i]["us"] <= lim]
+                pick = min(fit, key=lambda i: (max(f, rdy[i]), -prio[i], i)) if fit and rdy[top] > f else top
+                s = max(f, rdy[pick])
+                if best is None or s < best[0]:
+                    best = (s, q, pick)
+            s, q, i = best
+            pool[q].discard(i)
+            start[i], end[i] = s, s + ops[i]["us"]
+            free[q] = end[i]
+            done.append(i)
+            for j in succ[i]:
+                left[j] -= 1
+                rdy[j] = max(rdy[j], end[i] + lat)
+                if not left[j]:
+                    pool[ops[j]["q"]].add(j)
+        for i in done:
+            o = ops[i]
+            q = o["q"]
+            if o["kind"] == "land":
+                continue
+            deps = {}
+            for d in o["deps"]:
+                a, b = ops[d]["sig"]
+                deps[a] = max(deps.get(a, 0), b)
+            for a in sorted(deps, key=lambda a: a == "q" + q):
+                require(q, (a, deps[a]))
+            if o["kind"] == "call":
+                a = "q" + q
+                for c in o["calls"]:
+                    c().then_inc(T.sem[a], 1)
+                    cnt[a] = cnt.get(a, 0) + 1
+                o["sig"] = (a, cnt[a])
+                snap[o["sig"]] = dict(seen[q])
+            else:
+                o["calls"]()
+
+    def X(name, idx=None, tok=None, n=256):
+        return (T[name][:] if idx is None else T[name][idx], tok or name, n)
+
+    def cols(name, a, b, tok=None):
+        return X(name, (slice(None), slice(a, b)), tok, b - a)
+
+    lanes = {"LF": {}, "LI": {}}
+
+    def lane(buf, n):
+        j = lanes[buf].setdefault(n, len(lanes[buf]))
+        return cols(buf, 16 * j, 16 * j + 16, buf + ":" + n)
+
+    def F(n):
+        return lane("LF", n)
+
+    def I(n):
+        return lane("LI", n)
+
+    def first(name):
+        return X(name, (slice(None), slice(0, 256, 16)), None, 16)
+
+    def final(name):
+        return X(name, (slice(None), slice(15, 256, 16)), None, 16)
+
+    def cyc(n):
+        return max(64, n) * 0.83e-3
+
+    v, s_, p = g.vector, g.scalar, g.tensor
+
+    def tt(o, a, b, op):
+        do("V", [a[1], b[1]], [o[1]], [lambda: v.tensor_tensor(out=o[0], in0=a[0], in1=b[0], op=op)],
+           cyc(o[2] * (1 if {a[1].split(":")[0], b[1].split(":")[0]} & banks else 2)))
+
+    def ts(o, a, s1, op0, s2=None, op1=None, extra=()):
+        kw = {"op1": op1} if op1 is not None else {}
+        do("V", [a[1]] + list(extra), [o[1]],
+           [lambda: v.tensor_scalar(out=o[0], in0=a[0], scalar1=s1, scalar2=s2, op0=op0, **kw)], cyc(o[2]))
+
+    def cp(o, a):
+        do("V", [a[1]], [o[1]], [lambda: v.tensor_copy(out=o[0], in_=a[0])], cyc(o[2]))
+
+    def fill(o, c):
+        do("V", [], [o[1]], [lambda: v.memset(o[0], c)], 0.2 if o[1] != "SELC" else 0.9)
+
+    def scan(o, d0, d1, op0, op1):
+        do("V", [d0[1], d1[1]], [o[1]],
+           [lambda: v.tensor_tensor_scan(out=o[0], data0=d0[0], data1=d1[0], initial=0.0, op0=op0, op1=op1)], cyc(o[2]))
+
+    def act(o, a, func, scale=1.0, bias=0.0, extra=()):
+        do("S", [a[1]] + list(extra), [o[1]], [lambda: s_.activation(out=o[0], in_=a[0], func=func, scale=scale, bias=bias)],
+           cyc(o[2]) if o[1] != "SELS" else 1.7)
+
+    def mm(o, pairs):
+        reads = [t[1] for pr in pairs for t in pr]
+        n = len(pairs)
+        do("P", reads, [o[1]], [(lambda i=i, l=l, r=r: p.matmul(o[0], l[0], r[0], i == 0, i == n - 1)) for i, (l, r) in enumerate(pairs)],
+           n * max(64, o[2]) * 0.42e-3)
+
+    SHR, AND = A.logical_shift_right, A.bitwise_and
+
+    def load(q, name, dst):
+        s = "ld_" + name
+        cnt[s] = 16
+        eng[q].dma_start(dst[0], T[name][:]).then_inc(T.sem[s], 16)
+        do("N", [], [dst[1]], [], 4.5 if name == "prop" else 2.3, "land")["sig"] = (s, 16)
+    load("Y", "con", X("conA"))
+    load("S", "prop", cols("P", 0, 2048))
+    load("Y", "ex", X("yv"))
+    load("Y", "lem", X("lemA"))
+    load("Y", "org", X("orgA"))
+    load("Y", "cnt", X("cntA"))
+    load("Y", "lim", X("limA"))
+
+    def sel(o, a, pat, cmp, fillv, base, cm):
+        do("G", [a[1]], [o[1]], [lambda: g.affine_select(o[0], a[0], pat, cmp, fillv, base, cm)], 0.17 + 2 * cyc(o[2]))
+
+    def iota(o, pat, base, cm):
+        do("G", [], [o[1]], [lambda: g.iota(o[0], pat, base, cm, allow_small_or_imprecise_dtypes=True)], 0.13 + 2 * cyc(o[2]))
+    fill(X("ones"), 1.0)
+    one128 = cols("ones", 0, 128)
+    sel(X("ID"), one128, [[-1, 128]], A.is_equal, 0.0, 0, 1)
+    sel(X("BT"), one128, [[-16, 8], [0, 16]], A.is_ge, 0.0, 0, 1)
+    sel(X("BLK"), X("BT"), [[16, 8], [0, 16]], A.is_ge, 0.0, 15, -1)
+    fill(cols("P", 2048, 2304, "Pz"), 0.0)
+    fill(X("THR"), 9.5 * BIG)
+    fill(X("SELC"), 0.0)
+    fill(X("EVC"), 0.0)
+    fill(X("EVL"), 0.0)
+    fill(X("ERC"), -1.0)
+    fill(X("ERL"), -1.0)
+    fill(X("fb"), -float(2 ** 30))
+    fill(X("SC"), 1.0)
+    fill(I("w"), 0)
+    emp = X("f0")
+    ts(emp, X("conA"), 0.0, A.is_lt)
+    ts(X("f1"), emp, 2049.0, A.mult)
+    tt(X("f1"), X("f1"), X("conA"), A.add)
+    cp(cols("C16", 0, 256, "C16_0"), X("f1"))
+    mm(X("pY", (slice(None), slice(0, 16))), [(X("ID"), X("yv"))])
+    cp(cols("L16", 0, 256, "L16_0"), X("lemA"))
+    do("V", ["BLK"], ["SELC"],
+       [(lambda i=i: v.tensor_scalar(out=T.SELC[:, 129 * i:128 * i + 128:16], in0=T.BLK[:, 0:128:16], scalar1=-BIG, scalar2=None,
+                                     op0=A.mult)) for i in range(16)], 0.9)
+
+    def selq(nm, q):
+        return cols(nm, 128 * q, 128 * q + 128, nm)
+    yr = [X("yv", (slice(None), slice(q, 256, 16))) for q in range(16)]
+
+    def gather(t, lst, dst, m, q="S"):
+        tok = "%s_%d" % (lst, t)
+        win = T.P[:, 0:2064].indirect(T[lst][:, 256 * t + 16 * m:256 * t + 16 * m + 16])
+        out = T[dst][:, m, :]
+        do(q, [tok, "P", "Pz"], ["%s:%d" % (dst, m)],
+           [(lambda: s_.activation(out=out, in_=win, func=AF.Copy)) if q == "S" else (lambda: v.tensor_copy(out=out, in_=win))], 0.39)
+
+    def rows_of(t, k):
+        return slice(k, 256, 16) if t == 0 else slice(16 * k, 16 * k + 16)
+
+    def lanes_of(t, q):
+        return slice(16 * q, 16 * q + 16) if t == 0 else slice(q, 256, 16)
+
+    def toks(b, m0, m1):
+        return ["%s:%d" % (b, m) for m in range(m0, m1)]
+
+    def compare(t, src, dst, op, m0, m1):
+        ms = slice(m0, m1)
+        do("V", toks(src, m0, m1) + ["pY"], toks(dst, m0, m1),
+           [(lambda k=k: v.tensor_tensor(out=T[dst][:, ms, rows_of(t, k)], in0=T[src][:, ms, rows_of(t, k)], in1=T.pY[:, ms, :], op=op))
+            for k in range(16)], 16 * cyc(16 * (m1 - m0)))
+
+    def sums(t, src, bank, sl, const, m0, m1, made=None):
+        ms, cs = slice(m0, m1), slice(16 * m0, 16 * m1)
+        out = T[bank][:, cs]
+        calls = [lambda: p.matmul(out, T.ID[:], T[const][:, cs], True, False)]
+        calls += [(lambda q=q: p.matmul(out, T[sl][:, 128 * q:128 * q + 128], T[src][:, ms, lanes_of(t, q)], False, q == 15)) for q in range(16)]
+        do("P", ["ID", const, sl] + (made or toks(src, m0, m1)), ["%s:%d" % (bank, m) for m in range(m0, m1)], calls,
+           17 * max(64, 16 * (m1 - m0)) * 0.42e-3)
+
+    def whole(bank):
+        return [("%s:%d" % (bank, m)) for m in range(16)]
+
+    def keyed(o, bank, b):
+        do("V", whole(bank) + [b[1]], [o[1]], [lambda: v.tensor_tensor(out=o[0], in0=T[bank][:, 0:256], in1=b[0], op=A.max)], cyc(256))
+
+    cpieces = [(0, 8), (8, 16)]
+    HB = 4
+    lpieces = [(0, 4), (4, 8), (8, 12), (12, 16)]
+    VG = 3
+    dst = T.cores[(rank + HOP) % len(T.cores)]
+    rid, pid = topo.addr(dst, core)
+    msk = topo.mask(core, dst)
+    neng = len(topo.engines(core, dst))
+    sent = [0]
+
+    def send(kind, t):
+        c = slice(256 * t, 256 * t + 256)
+        d = slice(256 * t + 256, 256 * t + 512)
+        a = "a%s_%d" % (kind, t + 1)
+        do("G", ["o%s_%d" % (kind, t)], ["net" + a],
+           lambda: g.remote_dma(T[kind][:, d], T["o" + kind][:, c], T.sem[a], T.sem.sent, pid, rid, msk), 0.8, "send")
+        do("N", ["net" + a], ["%s_%d" % (kind, t + 1)], [], 3.0, "land")["sig"] = (a, neng)
+        sent[0] += neng
+
+    def masks(src, y):
+        for e in range(2):
+            act(X(y, (slice(None), slice(None), slice(16 * e, 16 * e + 16)), "%s%d" % (y, e)), src, AF.Copy, T.col[:, e:e + 1], extra=["col"])
+
+    def turn(y, dst):
+        do("V", [y + "0", y + "1"], ["Z"], [(lambda m=m: v.transpose(out=T.Z[:, m, :], in_=T[y][:, m, :])) for m in range(16)], 0.85)
+        tt(dst, X("Z", (slice(None), slice(None), slice(0, 16))), X("Z", (slice(None), slice(None), slice(16, 32))), A.add)
+
+    def consts():
+        tt(cols("mt", 0, 64), cols("ID", 0, 64), cols("ID", 64, 128), A.add)
+        tt(cols("mt", 64, 96), cols("mt", 0, 32), cols("mt", 32, 64), A.add)
+        tt(cols("RK", 0, 16), cols("mt", 64, 80), cols("mt", 80, 96), A.add)
+        for w in (16, 32, 64, 128):
+            cp(cols("RK", w, 2 * w), cols("RK", 0, w))
+        tt(X("kq"), cols("RK", 0, 16), cols("KI", 0, 16), A.mult)
+        do("V", ["kq"], ["col"], [lambda: v.tensor_reduce(out=T.col[:, 2:3], in_=T.kq[:], axis=AX.X, op=A.add)])
+        do("V", ["BLK"], ["col"], [lambda: v.tensor_reduce(out=T.col[:, 0:1], in_=T.BLK[:, 0:128:32], axis=AX.X, op=A.add)])
+        ts(X("col", (slice(None), slice(1, 2))), X("col", (slice(None), slice(0, 1))), -1.0, A.mult, 1.0, A.add)
+        ts(X("col", (slice(None), slice(3, 4))), X("col", (slice(None), slice(2, 3))), float(2 ** 20), A.mult)
+        ts(X("col", (slice(None), slice(4, 5))), X("col", (slice(None), slice(2, 3))), 65536.0, A.mult, 65536.0, A.add)
+        ts(X("cb"), X("cb"), T.col[:, 2:3], A.add, extra=["col"])
+        ts(X("pY", (slice(None), slice(16, 32)), "pY:k"), X("KI"), 0.0625, A.mult)
+        ts(X("NID"), X("ID"), -1.0, A.mult)
+        cp(X("D1h"), X("D1"))
+        ts(X("limf"), X("limA"), 16384.0, A.mult)
+
+    def pack():
+        ts(X("f2"), X("f1"), 8.0, A.mult, T.col[:, 3:4], A.add, extra=["col"])
+        ts(X("f4"), X("orgA"), 65536.0, A.mult)
+        ts(X("f3"), emp, 7.0, A.mult, 1.0, A.add)
+        tt(X("f2"), X("f2"), X("f4"), A.add)
+        tt(X("f4"), X("f3"), X("cntA"), A.mult)
+        ts(X("f3"), X("lemA"), 8.0, A.mult, T.col[:, 4:5], A.add, extra=["col"])
+        tt(X("f2"), X("f2"), X("f4"), A.add)
+
+    iota(cols("KI", 0, 256), [[0, 16], [1, 16]], 0, 0)
+    iota(X("KB"), [[0, 16], [1, 16]], 0, 0)
+    iota(X("cb"), [[16, 16]], 0, 0)
+    sel(X("D0"), X("fb"), [[0, 16], [1, 16]], A.is_gt, float(2 ** 30), 0, 0)
+    sel(X("D1"), X("SC"), [[0, 16], [1, 16]], A.is_gt, 0.0, 0, 0)
+
+    def u_sum(t):
+        mm(cols("pM", 0, 16, "pM:u"), [(selq("SELS", q), yr[q]) for q in range(16)])
+        act(F("u"), cols("pM", 0, 16, "pM:u"), AF.Copy, 1.0 / 16)
+        act(F("u32"), cols("pM", 0, 16, "pM:u"), AF.Identity, 1.0 / 512, 1.0)
+        act(F("v37"), cols("pM", 0, 16, "pM:u"), AF.Identity, 37.0 / 16, float(t))
+
+    def update(e_row, e_val, R, e, at, old, new):
+        pa, pb = cols("pT", 0, 256, "pT:a"), cols("pT", 256, 512, "pT:b")
+        scan(X(R), X("D1h"), X(e_row), A.mult, A.add)
+        scan(pa, X("D1"), X(e_val), A.mult, A.add)
+        ts(X(e), X(R), at, A.is_equal)
+        tt(pb, pa, old, A.subtract)
+        tt(pa, pb, X(e), A.mult)
+        tt(new, pa, old, A.add)
+
+    stores = [0]
+
+    def store(q, name, src):
+        do(q, [src[1]], [], lambda: eng[q].dma_start(T[name][:], src[0]).then_inc(T.sem.outs, 16), 0.1, "store")
+        stores[0] += 16
+
+    for t in range(TV):
+        last = t == TV - 1
+        c0, c1 = 256 * t, 256 * t + 256
+        pk, lk = cols("PK", c0, c1, "PK_%d" % t), cols("LK", c0, c1, "LK_%d" % t)
+        opk, olk = cols("oPK", c0, c1, "oPK_%d" % t), cols("oLK", c0, c1, "oLK_%d" % t)
+        if last:
+            opk, olk = X("zPK"), X("zLK")
+        if t == 0:
+            consts()
+            ts(cols("RLM", 0, 256, "RLM_0"), X("RK"), T.limf[:, 0:1], A.mult, extra=["limf"])
+        for m in range(16):
+            gather(t, "C16", "PC", m, "V" if m < VG else "S")
+        def conditions(m0, m1):
+            compare(t, "PC", "XC", A.is_gt, m0, m1)
+            sums(t, "XC", "pC", "SELC", "THR", m0, m1)
+
+        def lemma(m0, m1):
+            if m0 < HB:
+                compare(t, "PL", "DL", A.subtract, m0, m1)
+                do("V", toks("DL", m0, m1), toks("XL", m0, m1),
+                   [lambda: v.tensor_scalar(out=T.XL[:, m0:m1, :], in0=T.DL[:, m0:m1, :], scalar1=0.0, scalar2=None, op0=A.is_gt)],
+                   cyc(128 * (m1 - m0)))
+            else:
+                compare(t, "PL", "XL", A.is_gt, m0, m1)
+            sums(t, "XL", "pL", "SELC", "THR", m0, m1)
+        for m in range(16 if t else 8):
+            gather(t, "L16", "PL", m)
+        if t == 0:
+            conditions(*cpieces[0])
+            pack()
+            masks(X("f2"), "Yp")
+            masks(X("f3"), "Yl")
+            for m in range(8, 16):
+                gather(t, "L16", "PL", m)
+            act(X("SELS"), X("SELC"), AF.Copy, -16.0 / BIG)
+            conditions(*cpieces[1])
+            turn("Yp", cols("PK", 0, 256, "PK_0"))
+            lemma(*lpieces[0])
+            turn("Yl", cols("LK", 0, 256, "LK_0"))
+            lemma(*lpieces[1])
+            u_sum(0)
+        lp = cols("pM", 256, 512, "pM:l")
+        mm(lp, [(X("BLK"), cols("RLM", c0, c1, "RLM_%d" % t))])
+        x, sl = X("i0"), I("sl")
+        ts(x, pk, 0x4007, AND)
+        tt(X("KC"), lp, pk, A.add)
+        tt(X("keyS"), X("pY", (slice(None), slice(16, 32)), "pY:k"), x, A.subtract)
+        scan(X("SS"), X("D0"), X("keyS"), A.max, A.min)
+        ts(sl, final("SS"), 16.0, A.mult)
+        ts(sl, sl, 15, AND)
+        ts(F("sP"), sl, float(2 ** 20), A.mult, -65536.0, A.add)
+        if t:
+            for m0, m1 in cpieces:
+                conditions(m0, m1)
+            lemma(*lpieces[0])
+        keyed(X("key"), "pC", X("KC"))
+        scan(X("SB"), X("D0"), X("key"), A.max, A.min)
+        mb, mi = final("SB"), I("mi")
+        ts(X("bfl"), mb, CAP, A.is_lt)
+        ts(mi, mb, CAP + 49152.0, A.min)
+        ts(I("lim"), mi, 14, SHR, 3, AND)
+        ts(I("b"), mi, 7, AND)
+        ts(I("t2"), mi, 0x3FFF, AND)
+        ts(I("t1"), mi, 0x1FF0000, AND)
+        tt(F("bl"), I("b"), I("lim"), A.subtract)
+        ts(F("t2p"), I("t2"), 1.0, A.add)
+        ts(I("vb"), mi, 0x0F3FF8, AND)
+        tt(F("ov"), F("bl"), I("w"), A.is_ge)
+        ts(F("vb1"), I("vb"), 65536.0, A.add)
+        ts(F("tb"), mb, CAP, A.is_lt, 2 * CAP, A.mult)
+        ts(F("o14"), F("ov"), 16384.0, A.mult)
+        tt(F("vB"), F("vb1"), F("ov"), A.mult)
+        tt(F("z"), F("o14"), F("t2p"), A.max)
+        tt(F("nb"), F("z"), I("t1"), A.add)
+        if not last:
+            mm(cols("pM", 16, 32, "pM:w"), [(cols("RK", 0, 128), X("bfl"))])
+        for m0, m1 in lpieces[1 if t else 2:]:
+            lemma(m0, m1)
+        do("S", toks("DL", 0, HB), toks("AB", 0, HB),
+           [lambda: s_.activation(out=T.AB[:, 0:HB, :], in_=T.DL[:, 0:HB, :], func=AF.Abs)], cyc(256 * HB))
+        for kk in range(8):
+            bank = "pD%d" % (kk % 2)
+            calls = []
+            for j in range(2):
+                o = T[bank][:, HB:16, 16 * j:16 * j + 16]
+                calls.append(lambda o=o, r=rows_of(t, 2 * kk + j): p.matmul(o, T.ID[:], T.PL[:, HB:16, r], True, False))
+                calls.append(lambda o=o: p.matmul(o, T.NID[:], T.yv[:, 16 * HB:256], False, True))
+            do("P", ["ID", "NID", "yv"] + toks("PL", HB, 16), [bank], calls, 4 * 16 * (16 - HB) * 0.42e-3)
+            do("S", [bank], toks("AB%d" % kk, HB, 16),
+               [lambda kk=kk, bank=bank: s_.activation(out=T.AB[:, HB:16, 32 * kk:32 * kk + 32], in_=T[bank][:, HB:16, :], func=AF.Abs)],
+               cyc(32 * (16 - HB)))
+        sums(t, "AB", "pS", "SELS", "KB", 0, HB)
+        sums(1, "AB", "pS", "SELS", "KB", HB, 16, [x for kk in range(8) for x in toks("AB%d" % kk, HB, 16)])
+        if not last:
+            act(cols("RLM", c1, c1 + 256, "RLM_%d" % (t + 1)), X("RK"), AF.Copy, T.limf[:, t + 1:t + 2], extra=["limf"])
+        tt(I("uu"), F("u"), F("u"), A.mult)
+        ts(I("uu"), I("uu"), 5, SHR)
+        tt(I("fs"), I("uu"), F("v37"), A.add)
+        ts(I("fs"), I("fs"), 2047, AND)
+        ts(F("new8"), I("fs"), 8.0, A.mult, 65536.0, A.add)
+        if not last:
+            cp(I("w"), cols("pM", 16, 32, "pM:w"))
+            ts(I("w"), I("w"), 3, AND)
+        keyed(X("key"), "pL", lk)
+        scan(X("SG"), X("D0"), X("key"), A.max, A.min)
+        mg = final("SG")
+        tt(F("ng"), F("sP"), mg, A.add)
+        tt(F("q"), F("ng"), F("tb"), A.max)
+        tt(I("vc"), F("q"), F("nb"), A.min)
+        ts(I("gq"), F("q"), CAP + 16384.0, A.min)
+        ts(I("kc"), I("vc"), 20, SHR)
+        cp(first("EVC"), I("vc"))
+        cp(first("ERC"), I("kc"))
+        ts(I("al"), I("gq"), 3, SHR, 4095, AND)
+        update("ERC", "EVC", "RC", "eC", 0.0, pk, opk)
+        if not last:
+            ts(X("i1"), opk, 3, SHR, 4095, AND)
+            cp(cols("oC16", c0, c1, "oC16_%d" % t), X("i1"))
+            send("C16", t)
+            send("PK", t)
+        cp(cols("U16", 0, 16, "a16"), I("al"))
+        tt(F("x"), F("u32"), I("al"), A.mult)
+        ts(F("cg"), I("al"), 2048.0, A.is_ge, 2304.0, A.mult)
+        ts(I("h"), F("x"), 97.0 * t - 131072.0 - 31.0 / 64, A.add)
+        do("V", ["P", "Pz", "a16", "yv"], ["mn"],
+           [lambda: v.tensor_tensor(out=T.mn[:], in0=T.P[:, 0:2064].indirect(T.U16[:, 0:16]), in1=T.yv[:], op=A.min)], 0.4)
+        ts(I("h"), I("h"), 1792, AND)
+        tt(F("cg"), F("cg"), X("cb"), A.add)
+        tt(F("n"), I("h"), F("cg"), A.add)
+        cp(cols("U16", 16, 32, "n16"), F("n"))
+        do("V", ["P", "Pz", "a16", "yv"], ["dv"],
+           [lambda: v.tensor_tensor(out=T.dv[:], in0=T.P[:, 0:2064].indirect(T.U16[:, 0:16]), in1=T.yv[:], op=A.subtract)], 0.4)
+        do("V", ["mn", "n16"], ["P"],
+           [lambda: v.tensor_copy(out=T.P[:, 0:4352].indirect(T.U16[:, 16:32]), in_=T.mn[:])], 0.7)
+        act(X("yv"), X("dv"), AF.Abs)
+        if not last:
+            mm(X("pY", (slice(None), slice(0, 16))), [(X("ID"), X("yv"))])
+            u_sum(t + 1)
+        if last:
+            masks(opk, "Yp")
+            store("Y", "zp", cols("P", 0, 2048))
+            store("Y", "zy", X("yv"))
+            turn("Yp", X("i0"))
+            ts(X("i1"), X("i0"), 3, SHR, 4095, AND)
+            ts(X("i2"), X("i0"), 7, AND)
+            ts(X("f0"), X("i1"), 2048.0, A.is_ge)
+            ts(X("f2"), X("i1"), -2048.0, A.add)
+            ts(X("f0"), X("f0"), -4097.0, A.mult, 4096.0, A.add)
+            tt(X("h0"), X("f2"), X("i2"), A.max)
+            tt(X("f1"), X("i1"), X("f0"), A.min)
+            ts(X("i2"), X("i0"), 16, SHR, 15, AND)
+            store("Y", "zb", X("h0"))
+            store("Y", "zc", X("f1"))
+            cp(X("h1"), X("i2"))
+            store("Y", "zo", X("h1"))
+        do("V", whole("pS") + ["D0"], ["SC"],
+           [lambda: v.tensor_tensor_scan(out=T.SC[:], data0=T.D0[:], data1=T.pS[:, 0:256], initial=0.0, op0=A.max, op1=A.min)], cyc(256))
+        cp(I("ks"), final("SC"))
+        ts(I("gk"), I("gq"), 0x0F0000, AND)
+        ts(F("n8"), F("n"), 8.0, A.mult, 65536.0, A.add)
+        ts(I("ks"), I("ks"), 15, AND)
+        ts(F("gf"), F("q"), CAP, A.is_lt)
+        tt(F("vG"), F("n8"), I("gk"), A.add)
+        ts(F("k16"), I("ks"), 65536.0, A.mult)
+        ts(F("cf"), I("vc"), CAP, A.is_ge)
+        tt(F("vG"), F("vG"), F("gf"), A.mult)
+        tt(F("vC"), F("k16"), F("new8"), A.add)
+        tt(F("vG"), F("vG"), F("vB"), A.max)
+        tt(F("vC"), F("vC"), F("cf"), A.mult)
+        tt(I("vl"), F("vG"), F("vC"), A.max)
+        ts(I("rl"), I("vl"), 16, SHR)
+        cp(first("EVL"), I("vl"))
+        cp(first("ERL"), I("rl"))
+        update("ERL", "EVL", "RL", "eL", 1.0, lk, olk)
+        if not last:
+            ts(X("i2"), olk, 3, SHR, 2047, AND)
+            cp(cols("oL16", c0, c1, "oL16_%d" % t), X("i2"))
+            send("L16", t)
+            send("LK", t)
+
+    masks(X("zLK"), "Yl")
+    turn("Yl", X("i0"))
+    ts(X("i1"), X("i0"), 3, SHR, 2047, AND)
+    cp(X("f3"), X("i1"))
+    store("Y", "zl", X("f3"))
+    emit()
+    g.sync.wait_ge(T.sem.outs, stores[0])
+    g.wait_ge(T.sem.sent, sent[0])
+    for s in cnt:
+        g.wait_ge(T.sem[s], cnt[s])

@@ -3,48 +3,107 @@ from concourse.mybir import AluOpType as A, ActivationFunctionType as AF, AxisLi
 TV, HOP = 6, 5
 BIG = float(2 ** 26)
 CAP = float(2 ** 24)
-W = 256
+NONE = float(2 ** 24 + 2 ** 14 + 6)
+ROW0 = 160.0
+MN_ON_V = True
+SPAIRS = {"C": [4] * TV, "L": [4] * TV}
 SCRATCH = {
     "P": ("sbuf", [128, 4352], "bfloat16"), "NID": ("sbuf", [128, 128], "bfloat16"),
-    "PC": ("sbuf", [128, 16, 256], "bfloat16"), "PL": ("sbuf", [128, 16, 256], "bfloat16"),
-    "XC": ("sbuf", [128, 16, 256], "bfloat16"), "XL": ("sbuf", [128, 16, 256], "bfloat16"),
-    "DL": ("sbuf", [128, 16, 256], "bfloat16"), "AB": ("sbuf", [128, 16, 256], "bfloat16"),
-    "yv": ("sbuf", [128, 256], "bfloat16"), "dv": ("sbuf", [128, 256], "bfloat16"), "mn": ("sbuf", [128, 256], "bfloat16"),
+    "GC": ("sbuf", [128, 4096], "bfloat16"), "GL": ("sbuf", [128, 4096], "bfloat16"),
+    "XC": ("sbuf", [128, 2048, 2], "bfloat16"), "XL": ("sbuf", [128, 2048, 2], "bfloat16"),
+    "DL": ("sbuf", [128, 2048, 2], "bfloat16"), "AB": ("sbuf", [128, 2048, 2], "bfloat16"),
+    "y0": ("sbuf", [128, 512], "bfloat16"), "y1": ("sbuf", [128, 512], "bfloat16"), "pa": ("sbuf", [128, 256], "bfloat16"), "mn": ("sbuf", [128, 256], "bfloat16"),
     "C16": ("sbuf", [128, 256 * TV], "uint16"), "L16": ("sbuf", [128, 256 * TV], "uint16"),
     "PK": ("sbuf", [128, 256 * TV], "int32"), "LK": ("sbuf", [128, 256 * TV], "int32"),
-    "oC16": ("sbuf", [128, 256 * TV], "uint16"), "oL16": ("sbuf", [128, 256 * TV], "uint16"),
-    "oPK": ("sbuf", [128, 256 * TV], "int32"), "oLK": ("sbuf", [128, 256 * TV], "int32"),
+    "rPK": ("sbuf", [128, 256 * TV], "int32"), "rLK": ("sbuf", [128, 256 * TV], "int32"),
+    "VC": ("sbuf", [128, 16 * TV], "float32"), "VL": ("sbuf", [128, 16 * TV], "float32"),
+    "rVC": ("sbuf", [128, 16 * TV], "float32"), "rVL": ("sbuf", [128, 16 * TV], "float32"),
     "lemA": ("sbuf", [128, 256], "int32"), "conA": ("sbuf", [128, 256], "int32"), "limA": ("sbuf", [128, TV], "int32"),
     "orgA": ("sbuf", [128, 256], "bfloat16"), "cntA": ("sbuf", [128, 256], "bfloat16"),
     "f0": ("sbuf", [128, 256], "float32"), "f1": ("sbuf", [128, 256], "float32"), "f2": ("sbuf", [128, 256], "float32"),
-    "f3": ("sbuf", [128, 256], "float32"), "f4": ("sbuf", [128, 256], "float32"), "zPK": ("sbuf", [128, 256], "float32"), "zLK": ("sbuf", [128, 256], "float32"),
-    "i0": ("sbuf", [128, 256], "int32"), "i1": ("sbuf", [128, 256], "int32"),
-    "i2": ("sbuf", [128, 256], "int32"), "h0": ("sbuf", [128, 256], "bfloat16"), "h1": ("sbuf", [128, 256], "bfloat16"),
-    "KC": ("sbuf", [128, 256], "float32"), "key": ("sbuf", [128, 256], "float32"),
+    "f3": ("sbuf", [128, 256], "float32"), "f4": ("sbuf", [128, 256], "float32"),
+    "i0": ("sbuf", [128, 256], "int32"), "i1": ("sbuf", [128, 256], "int32"), "i2": ("sbuf", [128, 256], "int32"),
+    "i3": ("sbuf", [128, 256], "int32"), "h0": ("sbuf", [128, 256], "bfloat16"), "h1": ("sbuf", [128, 256], "bfloat16"),
+    "KC": ("sbuf", [128, 256], "float32"), "key": ("sbuf", [128, 256], "float32"), "keyL": ("sbuf", [128, 256], "float32"),
     "keyS": ("sbuf", [128, 256], "float32"), "SS": ("sbuf", [128, 256], "float32"),
     "SB": ("sbuf", [128, 256], "float32"), "SG": ("sbuf", [128, 256], "float32"), "SC": ("sbuf", [128, 256], "float32"),
     "RC": ("sbuf", [128, 256], "bfloat16"), "RL": ("sbuf", [128, 256], "bfloat16"),
     "eC": ("sbuf", [128, 256], "bfloat16"), "eL": ("sbuf", [128, 256], "bfloat16"),
     "EVC": ("sbuf", [128, 256], "float32"), "EVL": ("sbuf", [128, 256], "float32"),
     "ERC": ("sbuf", [128, 256], "bfloat16"), "ERL": ("sbuf", [128, 256], "bfloat16"),
-    "Yp": ("sbuf", [128, 16, 32], "float32"), "Yl": ("sbuf", [128, 16, 32], "float32"), "Z": ("sbuf", [128, 16, 32], "float32"),
+    "Ya": ("sbuf", [128, 288], "float32"), "Yb": ("sbuf", [128, 288], "float32"), "Yc": ("sbuf", [128, 288], "float32"),
+    "Za": ("sbuf", [128, 544], "float32"), "Zb": ("sbuf", [128, 544], "float32"), "Zc": ("sbuf", [128, 544], "float32"),
     "ones": ("sbuf", [128, 256], "bfloat16"), "ID": ("sbuf", [128, 128], "bfloat16"), "BT": ("sbuf", [128, 128], "bfloat16"),
-    "BLK": ("sbuf", [128, 128], "bfloat16"), "RK": ("sbuf", [128, 256], "bfloat16"), "mt": ("sbuf", [128, 128], "bfloat16"),
+    "BLK": ("sbuf", [128, 128], "bfloat16"), "RK": ("sbuf", [128, 256], "bfloat16"),
     "SELC": ("sbuf", [128, 2048], "bfloat16"), "SELS": ("sbuf", [128, 2048], "bfloat16"),
-    "THR": ("sbuf", [128, 256], "bfloat16"), "KI": ("sbuf", [128, 256], "float32"), "KB": ("sbuf", [128, 256], "bfloat16"),
+    "THR": ("sbuf", [128, 32, 4], "bfloat16"), "KI": ("sbuf", [128, 256], "float32"), "KB": ("sbuf", [128, 32, 8], "bfloat16"),
+    "K16": ("sbuf", [128, 256], "float32"), "K20": ("sbuf", [128, 256], "float32"),
     "D0": ("sbuf", [128, 256], "float32"), "D1": ("sbuf", [128, 256], "float32"), "D1h": ("sbuf", [128, 256], "bfloat16"),
     "fb": ("sbuf", [128, 256], "float32"), "RLM": ("sbuf", [128, 256 * TV], "bfloat16"), "limf": ("sbuf", [128, TV], "float32"),
-    "col": ("sbuf", [128, 8], "float32"), "cb": ("sbuf", [128, 16], "float32"), "kq": ("sbuf", [128, 16], "float32"),
-    "LF": ("sbuf", [128, 16 * 64], "float32"), "LI": ("sbuf", [128, 16 * 64], "int32"), "bfl": ("sbuf", [128, 16], "bfloat16"),
-    "U16": ("sbuf", [128, 32], "uint16"),
-    "pC": ("psum", [128, 512], "float32"), "pL": ("psum", [128, 512], "float32"), "pS": ("psum", [128, 512], "float32"),
-    "pM": ("psum", [128, 512], "float32"), "pY": ("psum", [128, 32, 16], "float32"), "pT": ("psum", [128, 512], "float32"),
-    "pD0": ("psum", [128, 16, 32], "float32"), "pD1": ("psum", [128, 16, 32], "float32"),
+    "col": ("sbuf", [128, 8], "float32"), "LF": ("sbuf", [128, 16 * 64], "float32"), "LI": ("sbuf", [128, 16 * 64], "int32"),
+    "bfl": ("sbuf", [128, 16], "bfloat16"), "U16": ("sbuf", [128, 32], "uint16"), "PM": ("sbuf", [128, 48], "uint16"),
+    "pC": ("psum", [128, 4, 16, 8], "float32"), "pL": ("psum", [128, 4, 16, 8], "float32"), "pS": ("psum", [128, 4, 16, 8], "float32"),
+    "pM": ("psum", [128, 512], "float32"), "pT": ("psum", [128, 512], "float32"),
+    "pD0": ("psum", [128, 512], "float32"), "pD1": ("psum", [128, 512], "float32"), "pD2": ("psum", [128, 512], "float32"),
 }
 _LOADS = ["prop", "lem", "con", "ex", "lim", "org", "cnt"]
-_KINDS = ["C16", "PK", "L16", "LK"]
+_KINDS = ["PK", "LK", "VC", "VL"]
 SEMAPHORES = (["qV", "qS", "qP", "qG", "sent", "outs"] + ["ld_" + n for n in _LOADS]
               + ["a%s_%d" % (k, t) for k in _KINDS for t in range(1, TV)])
+
+
+ORDER = []
+LAT, PASSES, JIT = 0.12, 60, 3.0
+
+
+def schedule(ops):
+    n = len(ops)
+    pred = [sorted(o["deps"]) for o in ops]
+    succ = [[] for _ in ops]
+    for i in range(n):
+        for d in pred[i]:
+            succ[d].append(i)
+
+    def place(order, before):
+        end, busy = [0.0] * n, {}
+        for i in order:
+            us, q = ops[i]["us"], ops[i]["q"]
+            s = max([end[d] + LAT for d in before[i]] + [0.0])
+            if q != "N":
+                line = busy.setdefault(q, [])
+                j = len(line)
+                while j and line[j - 1][1] > s:
+                    j -= 1
+                while j < len(line) and line[j][0] < s + us:
+                    s = max(s, line[j][1])
+                    j += 1
+                line.insert(j, (s, s + us))
+            end[i] = s + us
+        return end
+    def ranked(key, before, after):
+        left, heap, out = [len(b) for b in before], [], []
+        heap = sorted(((key[i], i) for i in range(n) if not left[i]), reverse=True)
+        while heap:
+            i = heap.pop()[1]
+            out.append(i)
+            for j in after[i]:
+                left[j] -= 1
+                if not left[j]:
+                    heap.append((key[j], j))
+            heap.sort(reverse=True)
+        return out
+    order, best, x = list(range(n)), None, 1
+    for ps in range(PASSES):
+        end = place(order, pred)
+        if best is None or max(end) < best[0] - 1e-9:
+            best = (max(end), sorted(range(n), key=lambda i: (end[i] - ops[i]["us"], i)), end)
+        key = []
+        for i in range(n):
+            x = (x * 1103515245 + 12345) % 2147483648
+            key.append(-best[2][i] + (JIT * x / 2147483648 if ps > 2 else 0.0))
+        back = place(ranked(key, succ, pred), succ)
+        order = sorted(range(n), key=lambda i: -back[i])
+    return best[1]
 
 
 def rank_program(g, core, T, topo):
@@ -66,7 +125,7 @@ def rank_program(g, core, T, topo):
             if seen[q].get(a, 0) < b:
                 seen[q][a] = b
 
-    banks = {"pC", "pL", "pS", "pM", "pY", "pT", "pD0", "pD1"}
+    banks = {"pC", "pL", "pS", "pM", "pT", "pD0", "pD1", "pD2"}
 
     def do(q, reads, writes, calls, us=0.06, kind="call"):
         i, deps = len(ops), set()
@@ -89,52 +148,18 @@ def rank_program(g, core, T, topo):
         return ops[-1]
 
     def emit():
-        lat, slack = 0.12, 0.1
-        n = len(ops)
-        succ, left = [[] for _ in ops], [len(o["deps"]) for o in ops]
-        for i, o in enumerate(ops):
-            for d in o["deps"]:
-                succ[d].append(i)
-        prio, start, end, rdy = [0.0] * n, [0.0] * n, [0.0] * n, [0.0] * n
-        for i in range(n - 1, -1, -1):
-            prio[i] = -i
-        free, pool = {q: 0.0 for q in "VSPGYN"}, {q: set() for q in "VSPGYN"}
-        for i in range(n):
-            if not left[i]:
-                pool[ops[i]["q"]].add(i)
-        done = []
-        while len(done) < n:
-            best = None
-            for q, c in pool.items():
-                if not c:
-                    continue
-                f = free[q] if q != "N" else 0.0
-                top = max(c, key=lambda i: (prio[i], -i))
-                lim = max(f, rdy[top]) + slack
-                fit = [i for i in c if q == "V" and i < top + 30 and max(f, rdy[i]) + ops[i]["us"] <= lim]
-                pick = min(fit, key=lambda i: (max(f, rdy[i]), -prio[i], i)) if fit and rdy[top] > f else top
-                s = max(f, rdy[pick])
-                if best is None or s < best[0]:
-                    best = (s, q, pick)
-            s, q, i = best
-            pool[q].discard(i)
-            start[i], end[i] = s, s + ops[i]["us"]
-            free[q] = end[i]
-            done.append(i)
-            for j in succ[i]:
-                left[j] -= 1
-                rdy[j] = max(rdy[j], end[i] + lat)
-                if not left[j]:
-                    pool[ops[j]["q"]].add(j)
-        for i in done:
+        if not ORDER:
+            ORDER.extend(schedule(ops))
+        for i in ORDER:
             o = ops[i]
             q = o["q"]
             if o["kind"] == "land":
                 continue
             deps = {}
             for d in o["deps"]:
-                a, b = ops[d]["sig"]
-                deps[a] = max(deps.get(a, 0), b)
+                if ops[d]["kind"] != "send":
+                    a, b = ops[d]["sig"]
+                    deps[a] = max(deps.get(a, 0), b)
             for a in sorted(deps, key=lambda a: a == "q" + q):
                 require(q, (a, deps[a]))
             if o["kind"] == "call":
@@ -174,30 +199,42 @@ def rank_program(g, core, T, topo):
     def cyc(n):
         return max(64, n) * 0.83e-3
 
+    def gcyc(n):
+        return 0.055 + n * 1.56 * 0.83e-3
+
     v, s_, p = g.vector, g.scalar, g.tensor
 
+    def by(win, off):
+        return (win[0].indirect(off[0]), [win[1], off[1]], 16 * off[2])
+
+    def toks(a):
+        return a[1] if isinstance(a[1], list) else [a[1]]
+
+    def cost(o, a, k=1.0):
+        return gcyc(a[2]) if isinstance(a[1], list) else cyc(o[2] * k)
+
     def tt(o, a, b, op):
-        do("V", [a[1], b[1]], [o[1]], [lambda: v.tensor_tensor(out=o[0], in0=a[0], in1=b[0], op=op)],
-           cyc(o[2] * (1 if {a[1].split(":")[0], b[1].split(":")[0]} & banks else 2)))
+        do("V", toks(a) + [b[1]], [o[1]], [lambda: v.tensor_tensor(out=o[0], in0=a[0], in1=b[0], op=op)],
+           cost(o, a, 1 if {toks(a)[0].split(":")[0], b[1].split(":")[0]} & banks else 2))
 
-    def ts(o, a, s1, op0, s2=None, op1=None, extra=()):
+    def ts(o, a, s1, op0, s2=None, op1=None, extra=(), k=1.0):
         kw = {"op1": op1} if op1 is not None else {}
-        do("V", [a[1]] + list(extra), [o[1]],
-           [lambda: v.tensor_scalar(out=o[0], in0=a[0], scalar1=s1, scalar2=s2, op0=op0, **kw)], cyc(o[2]))
+        do("V", toks(a) + list(extra), [o[1]],
+           [lambda: v.tensor_scalar(out=o[0], in0=a[0], scalar1=s1, scalar2=s2, op0=op0, **kw)], cost(o, a, k))
 
-    def cp(o, a):
-        do("V", [a[1]], [o[1]], [lambda: v.tensor_copy(out=o[0], in_=a[0])], cyc(o[2]))
+    def cp(o, a, k=1.0):
+        do("V", toks(a), [o[1]], [lambda: v.tensor_copy(out=o[0], in_=a[0])], cost(o, a, k))
 
-    def fill(o, c):
-        do("V", [], [o[1]], [lambda: v.memset(o[0], c)], 0.2 if o[1] != "SELC" else 0.9)
+    def fill(o, c, k=1.0):
+        do("V", [], [o[1]], [lambda: v.memset(o[0], c)], cyc(o[2] * k))
 
-    def scan(o, d0, d1, op0, op1):
-        do("V", [d0[1], d1[1]], [o[1]],
-           [lambda: v.tensor_tensor_scan(out=o[0], data0=d0[0], data1=d1[0], initial=0.0, op0=op0, op1=op1)], cyc(o[2]))
+    def scan(o, d0, d1, op0, op1, k=1.0):
+        do("V", [d0[1]] + toks(d1), [o[1]],
+           [lambda: v.tensor_tensor_scan(out=o[0], data0=d0[0], data1=d1[0], initial=0.0, op0=op0, op1=op1)], cyc(o[2] * k))
 
     def act(o, a, func, scale=1.0, bias=0.0, extra=()):
-        do("S", [a[1]] + list(extra), [o[1]], [lambda: s_.activation(out=o[0], in_=a[0], func=func, scale=scale, bias=bias)],
-           cyc(o[2]) if o[1] != "SELS" else 1.7)
+        do("S", toks(a) + list(extra), [o[1]], [lambda: s_.activation(out=o[0], in_=a[0], func=func, scale=scale, bias=bias)],
+           cost(o, a))
 
     def mm(o, pairs):
         reads = [t[1] for pr in pairs for t in pr]
@@ -214,7 +251,8 @@ def rank_program(g, core, T, topo):
         do("N", [], [dst[1]], [], 4.5 if name == "prop" else 2.3, "land")["sig"] = (s, 16)
     load("Y", "con", X("conA"))
     load("S", "prop", cols("P", 0, 2048))
-    load("Y", "ex", X("yv"))
+    load("Y", "ex", cols("y0", 0, 256))
+    act(cols("y0", 256, 512, "y0b"), cols("y0", 0, 256), AF.Copy)
     load("Y", "lem", X("lemA"))
     load("Y", "org", X("orgA"))
     load("Y", "cnt", X("cntA"))
@@ -225,76 +263,148 @@ def rank_program(g, core, T, topo):
 
     def iota(o, pat, base, cm):
         do("G", [], [o[1]], [lambda: g.iota(o[0], pat, base, cm, allow_small_or_imprecise_dtypes=True)], 0.13 + 2 * cyc(o[2]))
-    fill(X("ones"), 1.0)
+    iota(I("p"), [[0, 16]], 0, 1)
+    iota(I("pj"), [[1, 16]], 0, 0)
+    fill(X("ones"), 1.0, 0.5)
     one128 = cols("ones", 0, 128)
     sel(X("ID"), one128, [[-1, 128]], A.is_equal, 0.0, 0, 1)
     sel(X("BT"), one128, [[-16, 8], [0, 16]], A.is_ge, 0.0, 0, 1)
     sel(X("BLK"), X("BT"), [[16, 8], [0, 16]], A.is_ge, 0.0, 15, -1)
-    fill(cols("P", 2048, 2304, "Pz"), 0.0)
-    fill(X("THR"), 9.5 * BIG)
-    fill(X("SELC"), 0.0)
-    fill(X("EVC"), 0.0)
-    fill(X("EVL"), 0.0)
-    fill(X("ERC"), -1.0)
-    fill(X("ERL"), -1.0)
+    iota(cols("KI", 0, 256), [[0, 16], [1, 16]], 0, 0)
+    iota(X("KB"), [[1, 2], [0, 16], [2, 8]], 0, 0)
     fill(X("fb"), -float(2 ** 30))
     fill(X("SC"), 1.0)
+    sel(X("D0"), X("fb"), [[0, 16], [1, 16]], A.is_gt, NONE, 0, 0)
+    sel(X("D1"), X("SC"), [[0, 16], [1, 16]], A.is_gt, 0.0, 0, 0)
+    iota(X("K16"), [[0, 16], [4096, 16]], 0, 0)
+    fill(cols("P", 2048, 2304, "Pz"), 0.0, 0.5)
+    fill(X("THR", (slice(None), slice(None), slice(0, 2)), "THa", 64), 3.0 * BIG)
+    fill(X("THR", (slice(None), slice(None), slice(2, 4)), "THb", 64), 9.5 * BIG)
+    fill(X("SELC", None, None, 2048), 0.0, 0.5)
+    for b in ("EVC", "EVL"):
+        fill(X(b), 0.0)
+    for b in ("ERC", "ERL"):
+        fill(X(b), -1.0, 0.5)
+    for b in ("Ya", "Yb", "Yc"):
+        fill(X(b, (slice(None), slice(0, 16)), b + "0", 16), 0.0)
+        fill(X(b, (slice(None), slice(272, 288)), b + "1", 16), 0.0)
     fill(I("w"), 0)
-    emp = X("f0")
-    ts(emp, X("conA"), 0.0, A.is_lt)
-    ts(X("f1"), emp, 2049.0, A.mult)
-    tt(X("f1"), X("f1"), X("conA"), A.add)
-    cp(cols("C16", 0, 256, "C16_0"), X("f1"))
-    mm(X("pY", (slice(None), slice(0, 16))), [(X("ID"), X("yv"))])
-    cp(cols("L16", 0, 256, "L16_0"), X("lemA"))
+    perm, tm, tk = cols("PM", 0, 16, "perm"), cols("PM", 16, 32, "tm"), cols("PM", 32, 48, "tk")
+    ts(I("q"), I("p"), 15, AND)
+    ts(I("gq0"), I("p"), 4, SHR)
+    ts(F("q16"), I("q"), 16.0, A.mult)
+    tt(F("pv"), F("q16"), I("pj"), A.add)
+    cp(perm, F("pv"))
+    tt(I("o1"), I("q"), I("gq0"), A.add)
+    ts(I("o1"), I("o1"), 1, AND)
+    ts(F("o1"), I("o1"), 272.0, A.mult)
+    tt(F("o1"), F("o1"), F("pv"), A.add)
+    cp(tk, F("o1"))
+    ts(F("j16"), I("pj"), 16.0, A.mult)
+    tt(F("cb"), F("j16"), I("q"), A.add)
+    tt(I("o2"), I("pj"), I("gq0"), A.add)
+    ts(I("o2"), I("o2"), 1, AND)
+    ts(F("o2"), I("o2"), 272.0, A.mult)
+    tt(F("o2"), F("o2"), F("cb"), A.add)
+    cp(tm, F("o2"))
+    ts(F("cd8"), F("cb"), 8.0, A.mult, 18432.0, A.add)
+    cp(cols("col", 2, 3, "kq"), X("LI", (slice(None), slice(16 * lanes["LI"]["q"], 16 * lanes["LI"]["q"] + 1)), "LI:q", 1))
+    ts(cols("col", 3, 4, "k16"), cols("col", 2, 3, "kq"), 65536.0, A.mult)
+    ts(X("RK"), X("KI"), T.col[:, 2:3], A.is_equal, extra=["kq"])
     do("V", ["BLK"], ["SELC"],
        [(lambda i=i: v.tensor_scalar(out=T.SELC[:, 129 * i:128 * i + 128:16], in0=T.BLK[:, 0:128:16], scalar1=-BIG, scalar2=None,
                                      op0=A.mult)) for i in range(16)], 0.9)
+    act(X("SELS", None, None, 2048), X("SELC"), AF.Copy, -16.0 / BIG)
+    act(X("NID", None, None, 128), X("ID"), AF.Copy, -1.0)
+    act(X("K20"), X("K16"), AF.Copy, 256.0)
+    act(X("K16"), X("K16"), AF.Copy, 16.0)
+    act(X("D1h"), X("D1"), AF.Copy)
+    ts(cols("pT", 256, 512, "pT:k"), X("KI"), 0.0625, A.mult)
+    ts(X("limf", None, None, TV), X("limA"), 16384.0, A.mult)
+    for t in range(TV):
+        act(cols("RLM", 256 * t, 256 * t + 256, "RLM_%d" % t), X("RK"), AF.Copy, T.limf[:, t:t + 1], extra=["limf"])
+
+    def turn(y, z):
+        do("V", [y, y + "0", y + "1"], [z], [lambda: v.transpose(out=T[z][:, 0:256], in_=T[y][:, 16:272]),
+                                             lambda: v.transpose(out=T[z][:, 256:544], in_=T[y][:, 0:288])], cyc(544))
+        return X(z)
+
+    def mid(y):
+        return cols(y, 16, 272)
+
+    emp = X("f0")
+    ts(emp, X("conA"), 0.0, A.is_lt)
+    ts(X("f1"), emp, 2049.0, A.mult)
+    tt(mid("Ya"), X("f1"), X("conA"), A.add)
+    cp(cols("C16", 0, 256, "C16_0"), by(turn("Ya", "Za"), tk))
+    ts(mid("Yb"), X("lemA"), 8.0, A.mult)
+    ts(cols("L16", 0, 256, "L16_0"), by(turn("Yb", "Zb"), tk), 0.125, A.mult)
+    tt(cols("LK", 0, 256, "LK_0"), by(X("Zb"), tm), X("K16"), A.add)
+    pt = cols("pT", 0, 256, "pT:a")
+    act(pt, emp, AF.Identity, 7.0, 1.0)
+    act(X("f2"), X("orgA"), AF.Copy, 65536.0)
+    act(X("f3"), mid("Ya"), AF.Copy, 8.0)
+    tt(pt, pt, X("cntA"), A.mult)
+    tt(pt, pt, X("f2"), A.add)
+    tt(mid("Yc"), pt, X("f3"), A.add)
+    tt(cols("PK", 0, 256, "PK_0"), by(turn("Yc", "Zc"), tm), X("K20"), A.add)
 
     def selq(nm, q):
         return cols(nm, 128 * q, 128 * q + 128, nm)
-    yr = [X("yv", (slice(None), slice(q, 256, 16))) for q in range(16)]
+    pw = (T.P[:, 0:2064], ["P", "Pz"], 2064)
 
-    def gather(t, lst, dst, m, q="S"):
-        tok = "%s_%d" % (lst, t)
-        win = T.P[:, 0:2064].indirect(T[lst][:, 256 * t + 16 * m:256 * t + 16 * m + 16])
-        out = T[dst][:, m, :]
-        do(q, [tok, "P", "Pz"], ["%s:%d" % (dst, m)],
-           [(lambda: s_.activation(out=out, in_=win, func=AF.Copy)) if q == "S" else (lambda: v.tensor_copy(out=out, in_=win))], 0.39)
+    def names(lst, t, k0, k1):
+        off = cols(lst, 256 * t + 16 * k0, 256 * t + 16 * k1, "%s_%d" % (lst, t))
+        return (pw[0].indirect(off[0]), pw[1] + [off[1]], 256 * (k1 - k0))
 
-    def rows_of(t, k):
-        return slice(k, 256, 16) if t == 0 else slice(16 * k, 16 * k + 16)
+    def pair(buf, r):
+        return X(buf, (slice(None), slice(512 * (r // 2), 512 * (r // 2) + 512), r % 2), "%s:%d" % (buf, r), 512)
 
-    def lanes_of(t, q):
-        return slice(16 * q, 16 * q + 16) if t == 0 else slice(q, 256, 16)
+    turnb = [0]
 
-    def toks(b, m0, m1):
-        return ["%s:%d" % (b, m) for m in range(m0, m1)]
+    def differ(yv, src, r, dst, func, bias):
+        bank = X("pD%d" % (turnb[0] % 3), None, None, 512)
+        turnb[0] += 1
+        gs = cols(src, 512 * r, 512 * r + 512, "%s:%d" % (src, r))
+        do("P", ["ID", "NID", yv, yv + "b", gs[1]], [bank[1]],
+           [lambda: p.matmul(bank[0], T.NID[:], T[yv][:], True, False), lambda: p.matmul(bank[0], T.ID[:], gs[0], False, True)],
+           2 * 512 * 0.42e-3)
+        act(pair(dst, r), bank, func, 1.0, bias)
 
-    def compare(t, src, dst, op, m0, m1):
-        ms = slice(m0, m1)
-        do("V", toks(src, m0, m1) + ["pY"], toks(dst, m0, m1),
-           [(lambda k=k: v.tensor_tensor(out=T[dst][:, ms, rows_of(t, k)], in0=T[src][:, ms, rows_of(t, k)], in1=T.pY[:, ms, :], op=op))
-            for k in range(16)], 16 * cyc(16 * (m1 - m0)))
-
-    def sums(t, src, bank, sl, const, m0, m1, made=None):
-        ms, cs = slice(m0, m1), slice(16 * m0, 16 * m1)
-        out = T[bank][:, cs]
-        calls = [lambda: p.matmul(out, T.ID[:], T[const][:, cs], True, False)]
-        calls += [(lambda q=q: p.matmul(out, T[sl][:, 128 * q:128 * q + 128], T[src][:, ms, lanes_of(t, q)], False, q == 15)) for q in range(16)]
-        do("P", ["ID", const, sl] + (made or toks(src, m0, m1)), ["%s:%d" % (bank, m) for m in range(m0, m1)], calls,
-           17 * max(64, 16 * (m1 - m0)) * 0.42e-3)
+    def sums(src, bank, sl, const, ctok, b):
+        out = T[bank][:, 0:2, :, 2 * b:2 * b + 2]
+        calls = [lambda: p.matmul(out, T.ID[:], const, True, False)]
+        calls += [(lambda q=q: p.matmul(out, T[sl][:, 128 * q:128 * q + 128], T[src][:, 512 * b + q:512 * b + 512:16, :], False, q == 15))
+                  for q in range(16)]
+        do("P", ["ID", sl, "%s:%d" % (src, 2 * b), "%s:%d" % (src, 2 * b + 1)] + ctok, ["%s:%d" % (bank, b)], calls, 17 * 64 * 0.42e-3)
 
     def whole(bank):
-        return [("%s:%d" % (bank, m)) for m in range(16)]
+        return ["%s:%d" % (bank, b) for b in range(4)]
 
-    def keyed(o, bank, b):
-        do("V", whole(bank) + [b[1]], [o[1]], [lambda: v.tensor_tensor(out=o[0], in0=T[bank][:, 0:256], in1=b[0], op=A.max)], cyc(256))
+    def counts(t, kind):
+        lst, gb, xb, bank, ns = kind + "16", "G" + kind, "X" + kind, "p" + kind, SPAIRS[kind][t]
+        yv = "y%d" % (t % 2)
+        for r in range(ns + 1):
+            if r < ns:
+                act(cols(gb, 512 * r, 512 * r + 512, "%s:%d" % (gb, r)), names(lst, t, 2 * r, 2 * r + 2), AF.Copy)
+            if r:
+                differ(yv, gb, r - 1, xb, AF.Sign, -0.5)
+        for r in range(7, ns - 1, -1):
+            a, o = names(lst, t, 2 * r, 2 * r + 2), pair(xb if kind == "C" else "DL", r)
+            do("V", a[1] + [yv, yv + "b"], [o[1]],
+               [lambda a=a, o=o: v.tensor_tensor(out=o[0], in0=a[0], in1=T[yv][:], op=A.is_gt if kind == "C" else A.subtract)],
+               gcyc(512))
+            if kind == "L":
+                ts(pair("XL", r), o, 0.0, A.is_gt, k=0.5)
+        for b in range(4):
+            s = min(2, max(0, ns - 2 * b))
+            sums(xb, bank, "SELC", T.THR[:, :, 2 - s:4 - s], ["THa", "THb"], b)
 
-    cpieces = [(0, 8), (8, 16)]
-    HB = 4
-    lpieces = [(0, 4), (4, 8), (8, 12), (12, 16)]
-    VG = 3
+    def keyed(o, bank, b, c0):
+        do("V", whole(bank) + [b[1]], [o],
+           [(lambda e=e: v.tensor_tensor(out=T[o][:, e:256:2], in0=T[bank][:, e], in1=T[b[0]][:, c0 + e:c0 + 256:2], op=A.max))
+            for e in range(2)], cyc(256))
+
     dst = T.cores[(rank + HOP) % len(T.cores)]
     rid, pid = topo.addr(dst, core)
     msk = topo.mask(core, dst)
@@ -302,219 +412,143 @@ def rank_program(g, core, T, topo):
     sent = [0]
 
     def send(kind, t):
-        c = slice(256 * t, 256 * t + 256)
-        d = slice(256 * t + 256, 256 * t + 512)
+        n = 16 if kind[0] == "V" else 256
+        c = slice(n * t, n * t + n)
+        d = slice(n * t + n, n * t + 2 * n)
         a = "a%s_%d" % (kind, t + 1)
-        do("G", ["o%s_%d" % (kind, t)], ["net" + a],
-           lambda: g.remote_dma(T[kind][:, d], T["o" + kind][:, c], T.sem[a], T.sem.sent, pid, rid, msk), 0.8, "send")
-        do("N", ["net" + a], ["%s_%d" % (kind, t + 1)], [], 3.0, "land")["sig"] = (a, neng)
+        do("G", ["%s_%d" % (kind, t)], ["net" + a, "sends"],
+           lambda: g.remote_dma(T["r" + kind][:, d], T[kind][:, c], T.sem[a], T.sem.sent, pid, rid, msk), 0.8, "send")
+        do("W", ["net" + a], ["wire" + a], [], n / 116.0, "land")
+        do("N", ["wire" + a], ["r%s_%d" % (kind, t + 1)], [], 1.8, "land")["sig"] = (a, neng)
         sent[0] += neng
 
-    def masks(src, y):
-        for e in range(2):
-            act(X(y, (slice(None), slice(None), slice(16 * e, 16 * e + 16)), "%s%d" % (y, e)), src, AF.Copy, T.col[:, e:e + 1], extra=["col"])
+    def u_sum(yv):
+        pu = cols("pM", 0, 16, "pM:u")
+        mm(pu, [(selq("SELS", q), X(yv, (slice(None), slice(q, 256, 16)))) for q in range(16)])
+        act(F("u8"), pu, AF.Identity, 1.0 / 64, 8.0)
+        act(F("sq"), pu, AF.Square, 1.0 / 32, 296.0)
 
-    def turn(y, dst):
-        do("V", [y + "0", y + "1"], ["Z"], [(lambda m=m: v.transpose(out=T.Z[:, m, :], in_=T[y][:, m, :])) for m in range(16)], 0.85)
-        tt(dst, X("Z", (slice(None), slice(None), slice(0, 16))), X("Z", (slice(None), slice(None), slice(16, 32))), A.add)
-
-    def consts():
-        tt(cols("mt", 0, 64), cols("ID", 0, 64), cols("ID", 64, 128), A.add)
-        tt(cols("mt", 64, 96), cols("mt", 0, 32), cols("mt", 32, 64), A.add)
-        tt(cols("RK", 0, 16), cols("mt", 64, 80), cols("mt", 80, 96), A.add)
-        for w in (16, 32, 64, 128):
-            cp(cols("RK", w, 2 * w), cols("RK", 0, w))
-        tt(X("kq"), cols("RK", 0, 16), cols("KI", 0, 16), A.mult)
-        do("V", ["kq"], ["col"], [lambda: v.tensor_reduce(out=T.col[:, 2:3], in_=T.kq[:], axis=AX.X, op=A.add)])
-        do("V", ["BLK"], ["col"], [lambda: v.tensor_reduce(out=T.col[:, 0:1], in_=T.BLK[:, 0:128:32], axis=AX.X, op=A.add)])
-        ts(X("col", (slice(None), slice(1, 2))), X("col", (slice(None), slice(0, 1))), -1.0, A.mult, 1.0, A.add)
-        ts(X("col", (slice(None), slice(3, 4))), X("col", (slice(None), slice(2, 3))), float(2 ** 20), A.mult)
-        ts(X("col", (slice(None), slice(4, 5))), X("col", (slice(None), slice(2, 3))), 65536.0, A.mult, 65536.0, A.add)
-        ts(X("cb"), X("cb"), T.col[:, 2:3], A.add, extra=["col"])
-        ts(X("pY", (slice(None), slice(16, 32)), "pY:k"), X("KI"), 0.0625, A.mult)
-        ts(X("NID"), X("ID"), -1.0, A.mult)
-        cp(X("D1h"), X("D1"))
-        ts(X("limf"), X("limA"), 16384.0, A.mult)
-
-    def pack():
-        ts(X("f2"), X("f1"), 8.0, A.mult, T.col[:, 3:4], A.add, extra=["col"])
-        ts(X("f4"), X("orgA"), 65536.0, A.mult)
-        ts(X("f3"), emp, 7.0, A.mult, 1.0, A.add)
-        tt(X("f2"), X("f2"), X("f4"), A.add)
-        tt(X("f4"), X("f3"), X("cntA"), A.mult)
-        ts(X("f3"), X("lemA"), 8.0, A.mult, T.col[:, 4:5], A.add, extra=["col"])
-        tt(X("f2"), X("f2"), X("f4"), A.add)
-
-    iota(cols("KI", 0, 256), [[0, 16], [1, 16]], 0, 0)
-    iota(X("KB"), [[0, 16], [1, 16]], 0, 0)
-    iota(X("cb"), [[16, 16]], 0, 0)
-    sel(X("D0"), X("fb"), [[0, 16], [1, 16]], A.is_gt, float(2 ** 30), 0, 0)
-    sel(X("D1"), X("SC"), [[0, 16], [1, 16]], A.is_gt, 0.0, 0, 0)
-
-    def u_sum(t):
-        mm(cols("pM", 0, 16, "pM:u"), [(selq("SELS", q), yr[q]) for q in range(16)])
-        act(F("u"), cols("pM", 0, 16, "pM:u"), AF.Copy, 1.0 / 16)
-        act(F("u32"), cols("pM", 0, 16, "pM:u"), AF.Identity, 1.0 / 512, 1.0)
-        act(F("v37"), cols("pM", 0, 16, "pM:u"), AF.Identity, 37.0 / 16, float(t))
-
-    def update(e_row, e_val, R, e, at, old, new):
-        pa, pb = cols("pT", 0, 256, "pT:a"), cols("pT", 256, 512, "pT:b")
-        scan(X(R), X("D1h"), X(e_row), A.mult, A.add)
+    def update(kind, val, old, new):
+        e_row, e_val, R, e = "ER" + kind, "EV" + kind, "R" + kind, "e" + kind
+        pa = cols("pT", 0, 256, "pT:a")
+        ts(first(e_row), val, 2.0 ** (-20 if kind == "C" else -16), A.mult, ROW0 - 0.48, A.add)
+        cp(first(e_val), val)
+        scan(X(R), X("D1h"), X(e_row), A.mult, A.add, 0.5)
         scan(pa, X("D1"), X(e_val), A.mult, A.add)
-        ts(X(e), X(R), at, A.is_equal)
-        tt(pb, pa, old, A.subtract)
-        tt(pa, pb, X(e), A.mult)
+        ts(X(e), X(R), ROW0, A.is_equal, k=0.5)
+        tt(pa, pa, old, A.subtract)
+        tt(pa, pa, X(e), A.mult)
         tt(new, pa, old, A.add)
 
     stores = [0]
 
-    def store(q, name, src):
-        do(q, [src[1]], [], lambda: eng[q].dma_start(T[name][:], src[0]).then_inc(T.sem.outs, 16), 0.1, "store")
+    def store(q, name, src, us=2.3):
+        o = do(q, [src[1]], ["st" + name], lambda: eng[q].dma_start(T[name][:], src[0]).then_inc(T.sem.outs, 16), 0.1, "store")
+        do("N", ["st" + name], [], [], us, "land")
         stores[0] += 16
+
+    u_sum("y0")
 
     for t in range(TV):
         last = t == TV - 1
+        yv, yn = "y%d" % (t % 2), "y%d" % (1 - t % 2)
         c0, c1 = 256 * t, 256 * t + 256
         pk, lk = cols("PK", c0, c1, "PK_%d" % t), cols("LK", c0, c1, "LK_%d" % t)
-        opk, olk = cols("oPK", c0, c1, "oPK_%d" % t), cols("oLK", c0, c1, "oLK_%d" % t)
-        if last:
-            opk, olk = X("zPK"), X("zLK")
-        if t == 0:
-            consts()
-            ts(cols("RLM", 0, 256, "RLM_0"), X("RK"), T.limf[:, 0:1], A.mult, extra=["limf"])
-        for m in range(16):
-            gather(t, "C16", "PC", m, "V" if m < VG else "S")
-        def conditions(m0, m1):
-            compare(t, "PC", "XC", A.is_gt, m0, m1)
-            sums(t, "XC", "pC", "SELC", "THR", m0, m1)
-
-        def lemma(m0, m1):
-            if m0 < HB:
-                compare(t, "PL", "DL", A.subtract, m0, m1)
-                do("V", toks("DL", m0, m1), toks("XL", m0, m1),
-                   [lambda: v.tensor_scalar(out=T.XL[:, m0:m1, :], in0=T.DL[:, m0:m1, :], scalar1=0.0, scalar2=None, op0=A.is_gt)],
-                   cyc(128 * (m1 - m0)))
-            else:
-                compare(t, "PL", "XL", A.is_gt, m0, m1)
-            sums(t, "XL", "pL", "SELC", "THR", m0, m1)
-        for m in range(16 if t else 8):
-            gather(t, "L16", "PL", m)
-        if t == 0:
-            conditions(*cpieces[0])
-            pack()
-            masks(X("f2"), "Yp")
-            masks(X("f3"), "Yl")
-            for m in range(8, 16):
-                gather(t, "L16", "PL", m)
-            act(X("SELS"), X("SELC"), AF.Copy, -16.0 / BIG)
-            conditions(*cpieces[1])
-            turn("Yp", cols("PK", 0, 256, "PK_0"))
-            lemma(*lpieces[0])
-            turn("Yl", cols("LK", 0, 256, "LK_0"))
-            lemma(*lpieces[1])
-            u_sum(0)
+        vc, vl = cols("VC", 16 * t, 16 * t + 16, "VC_%d" % t), cols("VL", 16 * t, 16 * t + 16, "VL_%d" % t)
+        for kind, nm, word, tmp, top in (("C", "PK", pk, X("i1"), 4095), ("L", "LK", lk, X("i2"), 2047)):
+            if t:
+                update(kind, cols("rV" + kind, 16 * t, 16 * t + 16, "rV%s_%d" % (kind, t)),
+                       cols("r" + nm, c0, c1, "r%s_%d" % (nm, t)), word)
+                ts(tmp, by(word, perm), 3, SHR, top, AND)
+                cp(cols(kind + "16", c0, c1, "%s16_%d" % (kind, t)), tmp)
+            if not last:
+                send(nm, t)
+        counts(t, "C")
         lp = cols("pM", 256, 512, "pM:l")
         mm(lp, [(X("BLK"), cols("RLM", c0, c1, "RLM_%d" % t))])
         x, sl = X("i0"), I("sl")
         ts(x, pk, 0x4007, AND)
         tt(X("KC"), lp, pk, A.add)
-        tt(X("keyS"), X("pY", (slice(None), slice(16, 32)), "pY:k"), x, A.subtract)
+        tt(X("keyS"), cols("pT", 256, 512, "pT:k"), x, A.subtract)
         scan(X("SS"), X("D0"), X("keyS"), A.max, A.min)
         ts(sl, final("SS"), 16.0, A.mult)
         ts(sl, sl, 15, AND)
-        ts(F("sP"), sl, float(2 ** 20), A.mult, -65536.0, A.add)
-        if t:
-            for m0, m1 in cpieces:
-                conditions(m0, m1)
-            lemma(*lpieces[0])
-        keyed(X("key"), "pC", X("KC"))
+        ts(F("sP"), sl, float(2 ** 20), A.mult)
+        keyed("key", "pC", ("KC", "KC"), 0)
         scan(X("SB"), X("D0"), X("key"), A.max, A.min)
         mb, mi = final("SB"), I("mi")
-        ts(X("bfl"), mb, CAP, A.is_lt)
-        ts(mi, mb, CAP + 49152.0, A.min)
+        cp(mi, mb)
+        ts(X("bfl", None, None, 16), mb, CAP, A.is_lt)
+        ts(F("tb"), mb, CAP, A.is_lt, NONE, A.mult)
         ts(I("lim"), mi, 14, SHR, 3, AND)
         ts(I("b"), mi, 7, AND)
         ts(I("t2"), mi, 0x3FFF, AND)
         ts(I("t1"), mi, 0x1FF0000, AND)
+        ts(I("vb"), mi, 0x0F3FF8, AND)
         tt(F("bl"), I("b"), I("lim"), A.subtract)
         ts(F("t2p"), I("t2"), 1.0, A.add)
-        ts(I("vb"), mi, 0x0F3FF8, AND)
         tt(F("ov"), F("bl"), I("w"), A.is_ge)
-        ts(F("vb1"), I("vb"), 65536.0, A.add)
-        ts(F("tb"), mb, CAP, A.is_lt, 2 * CAP, A.mult)
         ts(F("o14"), F("ov"), 16384.0, A.mult)
-        tt(F("vB"), F("vb1"), F("ov"), A.mult)
+        ts(F("nov"), F("ov"), -NONE, A.mult, NONE, A.add)
         tt(F("z"), F("o14"), F("t2p"), A.max)
+        tt(F("vB"), F("nov"), I("vb"), A.max)
         tt(F("nb"), F("z"), I("t1"), A.add)
         if not last:
             mm(cols("pM", 16, 32, "pM:w"), [(cols("RK", 0, 128), X("bfl"))])
-        for m0, m1 in lpieces[1 if t else 2:]:
-            lemma(m0, m1)
-        do("S", toks("DL", 0, HB), toks("AB", 0, HB),
-           [lambda: s_.activation(out=T.AB[:, 0:HB, :], in_=T.DL[:, 0:HB, :], func=AF.Abs)], cyc(256 * HB))
-        for kk in range(8):
-            bank = "pD%d" % (kk % 2)
-            calls = []
-            for j in range(2):
-                o = T[bank][:, HB:16, 16 * j:16 * j + 16]
-                calls.append(lambda o=o, r=rows_of(t, 2 * kk + j): p.matmul(o, T.ID[:], T.PL[:, HB:16, r], True, False))
-                calls.append(lambda o=o: p.matmul(o, T.NID[:], T.yv[:, 16 * HB:256], False, True))
-            do("P", ["ID", "NID", "yv"] + toks("PL", HB, 16), [bank], calls, 4 * 16 * (16 - HB) * 0.42e-3)
-            do("S", [bank], toks("AB%d" % kk, HB, 16),
-               [lambda kk=kk, bank=bank: s_.activation(out=T.AB[:, HB:16, 32 * kk:32 * kk + 32], in_=T[bank][:, HB:16, :], func=AF.Abs)],
-               cyc(32 * (16 - HB)))
-        sums(t, "AB", "pS", "SELS", "KB", 0, HB)
-        sums(1, "AB", "pS", "SELS", "KB", HB, 16, [x for kk in range(8) for x in toks("AB%d" % kk, HB, 16)])
-        if not last:
-            act(cols("RLM", c1, c1 + 256, "RLM_%d" % (t + 1)), X("RK"), AF.Copy, T.limf[:, t + 1:t + 2], extra=["limf"])
-        tt(I("uu"), F("u"), F("u"), A.mult)
-        ts(I("uu"), I("uu"), 5, SHR)
-        tt(I("fs"), I("uu"), F("v37"), A.add)
-        ts(I("fs"), I("fs"), 2047, AND)
-        ts(F("new8"), I("fs"), 8.0, A.mult, 65536.0, A.add)
-        if not last:
             cp(I("w"), cols("pM", 16, 32, "pM:w"))
             ts(I("w"), I("w"), 3, AND)
-        keyed(X("key"), "pL", lk)
-        scan(X("SG"), X("D0"), X("key"), A.max, A.min)
-        mg = final("SG")
-        tt(F("ng"), F("sP"), mg, A.add)
-        tt(F("q"), F("ng"), F("tb"), A.max)
-        tt(I("vc"), F("q"), F("nb"), A.min)
-        ts(I("gq"), F("q"), CAP + 16384.0, A.min)
-        ts(I("kc"), I("vc"), 20, SHR)
-        cp(first("EVC"), I("vc"))
-        cp(first("ERC"), I("kc"))
-        ts(I("al"), I("gq"), 3, SHR, 4095, AND)
-        update("ERC", "EVC", "RC", "eC", 0.0, pk, opk)
-        if not last:
-            ts(X("i1"), opk, 3, SHR, 4095, AND)
-            cp(cols("oC16", c0, c1, "oC16_%d" % t), X("i1"))
-            send("C16", t)
-            send("PK", t)
-        cp(cols("U16", 0, 16, "a16"), I("al"))
-        tt(F("x"), F("u32"), I("al"), A.mult)
-        ts(F("cg"), I("al"), 2048.0, A.is_ge, 2304.0, A.mult)
-        ts(I("h"), F("x"), 97.0 * t - 131072.0 - 31.0 / 64, A.add)
-        do("V", ["P", "Pz", "a16", "yv"], ["mn"],
-           [lambda: v.tensor_tensor(out=T.mn[:], in0=T.P[:, 0:2064].indirect(T.U16[:, 0:16]), in1=T.yv[:], op=A.min)], 0.4)
-        ts(I("h"), I("h"), 1792, AND)
-        tt(F("cg"), F("cg"), X("cb"), A.add)
-        tt(F("n"), I("h"), F("cg"), A.add)
-        cp(cols("U16", 16, 32, "n16"), F("n"))
-        do("V", ["P", "Pz", "a16", "yv"], ["dv"],
-           [lambda: v.tensor_tensor(out=T.dv[:], in0=T.P[:, 0:2064].indirect(T.U16[:, 0:16]), in1=T.yv[:], op=A.subtract)], 0.4)
-        do("V", ["mn", "n16"], ["P"],
-           [lambda: v.tensor_copy(out=T.P[:, 0:4352].indirect(T.U16[:, 16:32]), in_=T.mn[:])], 0.7)
-        act(X("yv"), X("dv"), AF.Abs)
-        if not last:
-            mm(X("pY", (slice(None), slice(0, 16))), [(X("ID"), X("yv"))])
-            u_sum(t + 1)
+        ts(I("fs"), F("sq"), 8.0 * t - 296.0 * 296.0, A.add)
+        ts(I("fs"), I("fs"), 16376, AND)
+        tt(F("nw"), I("fs"), F("tb"), A.subtract)
+        counts(t, "L")
+        ns = SPAIRS["L"][t]
+        for r in range(7, ns - 1, -1):
+            act(pair("AB", r), pair("DL", r), AF.Abs)
+        for r in range(ns):
+            differ(yv, "GL", r, "AB", AF.Abs, 0.0)
+        for b in (3, 2, 1, 0):
+            sums("AB", "pS", "SELS", T.KB[:, :, 2 * b:2 * b + 2], ["KB"], b)
+        keyed("keyL", "pL", ("LK", lk[1]), c0)
+        scan(X("SG"), X("D0"), X("keyL"), A.max, A.min)
+        gq = I("gq")
+        tt(gq, final("SG"), F("tb"), A.max)
+        tt(F("ng"), F("sP"), gq, A.add)
+        tt(vc, F("ng"), F("nb"), A.min)
+        ts(I("al"), gq, 3, SHR, 4095, AND)
         if last:
-            masks(opk, "Yp")
-            store("Y", "zp", cols("P", 0, 2048))
-            store("Y", "zy", X("yv"))
-            turn("Yp", X("i0"))
+            update("C", vc, pk, mid("Ya"))
+        else:
+            send("VC", t)
+        a16, n16 = cols("U16", 0, 16, "a16"), cols("U16", 16, 32, "n16")
+        cp(a16, I("al"))
+        tt(F("x"), F("u8"), I("al"), A.mult)
+        ts(F("gf"), gq, CAP, A.is_lt, 18432.0, A.mult)
+        ts(I("h"), F("x"), 776.0 * t - 2.0 ** 20 - 0.375, A.add)
+        tt(F("cg"), F("cd8"), F("gf"), A.subtract)
+        ts(I("h"), I("h"), 14336, AND)
+        tt(F("n8"), I("h"), F("cg"), A.add)
+        ts(n16, F("n8"), 0.125, A.mult)
+        pa = (pw[0].indirect(a16[0]), pw[1] + ["a16"], 256)
+        y, y2 = cols(yv, 0, 256), cols(yn, 0, 256)
+        act(X("pa"), pa, AF.Copy)
+        dy = X("pC", (slice(None), slice(2, 4)), "pC:y")
+        mm(dy, [(X("ID"), X("pa")), (X("NID"), y)])
+        act(y2, dy, AF.Abs)
+        if MN_ON_V or last:
+            tt(X("mn"), pa, y, A.min)
+        else:
+            dm = X("pL", (slice(None), slice(2, 4)), "pL:m")
+            mm(dm, [(X("ID"), X("pa")), (X("ID"), y), (X("NID"), y2)])
+            act(X("mn"), dm, AF.Copy, 0.5)
+        do("V", ["mn", "n16"], ["P"],
+           [lambda: v.tensor_copy(out=T.P[:, 0:4352].indirect(T.U16[:, 16:32]), in_=T.mn[:])], 0.85)
+        if not last:
+            act(cols(yn, 256, 512, yn + "b"), dy, AF.Abs)
+            u_sum(yn)
+        if last:
+            store("Y", "zp", cols("P", 0, 2048), 4.5)
+            store("Y", "zy", y2)
+            cp(X("i0"), by(turn("Ya", "Za"), tm))
             ts(X("i1"), X("i0"), 3, SHR, 4095, AND)
             ts(X("i2"), X("i0"), 7, AND)
             ts(X("f0"), X("i1"), 2048.0, A.is_ge)
@@ -522,40 +556,29 @@ def rank_program(g, core, T, topo):
             ts(X("f0"), X("f0"), -4097.0, A.mult, 4096.0, A.add)
             tt(X("h0"), X("f2"), X("i2"), A.max)
             tt(X("f1"), X("i1"), X("f0"), A.min)
-            ts(X("i2"), X("i0"), 16, SHR, 15, AND)
+            ts(X("i3"), X("i0"), 16, SHR, 15, AND)
             store("Y", "zb", X("h0"))
             store("Y", "zc", X("f1"))
-            cp(X("h1"), X("i2"))
+            cp(X("h1"), X("i3"))
             store("Y", "zo", X("h1"))
-        do("V", whole("pS") + ["D0"], ["SC"],
-           [lambda: v.tensor_tensor_scan(out=T.SC[:], data0=T.D0[:], data1=T.pS[:, 0:256], initial=0.0, op0=A.max, op1=A.min)], cyc(256))
-        cp(I("ks"), final("SC"))
-        ts(I("gk"), I("gq"), 0x0F0000, AND)
-        ts(F("n8"), F("n"), 8.0, A.mult, 65536.0, A.add)
-        ts(I("ks"), I("ks"), 15, AND)
-        ts(F("gf"), F("q"), CAP, A.is_lt)
+        do("S", whole("pS"), ["f4"],
+           [(lambda e=e: s_.activation(out=T.f4[:, e:256:2], in_=T.pS[:, e], func=AF.Copy)) for e in range(2)], cyc(256))
+        scan(X("SC"), X("D0"), X("f4"), A.max, A.min)
+        ts(I("gk"), gq, 0x10F0000, AND)
+        ts(F("gB"), gq, -1.0, A.mult, float(2 ** 22), A.add)
         tt(F("vG"), F("n8"), I("gk"), A.add)
-        ts(F("k16"), I("ks"), 65536.0, A.mult)
-        ts(F("cf"), I("vc"), CAP, A.is_ge)
-        tt(F("vG"), F("vG"), F("gf"), A.mult)
-        tt(F("vC"), F("k16"), F("new8"), A.add)
-        tt(F("vG"), F("vG"), F("vB"), A.max)
-        tt(F("vC"), F("vC"), F("cf"), A.mult)
-        tt(I("vl"), F("vG"), F("vC"), A.max)
-        ts(I("rl"), I("vl"), 16, SHR)
-        cp(first("EVL"), I("vl"))
-        cp(first("ERL"), I("rl"))
-        update("ERL", "EVL", "RL", "eL", 1.0, lk, olk)
-        if not last:
-            ts(X("i2"), olk, 3, SHR, 2047, AND)
-            cp(cols("oL16", c0, c1, "oL16_%d" % t), X("i2"))
-            send("L16", t)
-            send("LK", t)
+        tt(F("vX"), F("vB"), F("gB"), A.max)
+        ts(I("ks"), final("SC"), 65536.0, A.mult, -2.0 ** 31, A.add)
+        ts(I("ks"), I("ks"), 0xF0000, AND)
+        tt(F("vC"), I("ks"), F("nw"), A.add)
+        tt(F("vC"), F("vC"), F("vX"), A.max)
+        tt(vl, F("vC"), F("vG"), A.min)
+        if last:
+            update("L", vl, lk, mid("Yb"))
+        else:
+            send("VL", t)
 
-    masks(X("zLK"), "Yl")
-    turn("Yl", X("i0"))
-    ts(X("i1"), X("i0"), 3, SHR, 2047, AND)
-    cp(X("f3"), X("i1"))
+    ts(X("f3"), by(turn("Yb", "Zb"), tm), T.col[:, 3:4], A.subtract, 0.125, A.mult, extra=["k16"])
     store("Y", "zl", X("f3"))
     emit()
     g.sync.wait_ge(T.sem.outs, stores[0])

@@ -6,7 +6,7 @@ CAP = float(2 ** 24)
 NONE = float(2 ** 24 + 2 ** 14 + 6)
 ROW0 = 160.0
 MN_ON_V = True
-SPAIRS = {"C": [4] * TV, "L": [4] * TV}
+SPAIRS = {"C": [4] + [6] * (TV - 1), "L": [4] * TV}
 SCRATCH = {
     "P": ("sbuf", [128, 4352], "bfloat16"), "NID": ("sbuf", [128, 128], "bfloat16"),
     "GC": ("sbuf", [128, 4096], "bfloat16"), "GL": ("sbuf", [128, 4096], "bfloat16"),
@@ -16,8 +16,8 @@ SCRATCH = {
     "C16": ("sbuf", [128, 256 * TV], "uint16"), "L16": ("sbuf", [128, 256 * TV], "uint16"),
     "PK": ("sbuf", [128, 256 * TV], "int32"), "LK": ("sbuf", [128, 256 * TV], "int32"),
     "rPK": ("sbuf", [128, 256 * TV], "int32"), "rLK": ("sbuf", [128, 256 * TV], "int32"),
-    "VC": ("sbuf", [128, 16 * TV], "float32"), "VL": ("sbuf", [128, 16 * TV], "float32"),
-    "rVC": ("sbuf", [128, 16 * TV], "float32"), "rVL": ("sbuf", [128, 16 * TV], "float32"),
+    "VC": ("sbuf", [128, 16 * TV], "int32"), "VL": ("sbuf", [128, 16 * TV], "float32"),
+    "rVC": ("sbuf", [128, 16 * TV], "int32"), "rVL": ("sbuf", [128, 16 * TV], "float32"),
     "lemA": ("sbuf", [128, 256], "int32"), "conA": ("sbuf", [128, 256], "int32"), "limA": ("sbuf", [128, TV], "int32"),
     "orgA": ("sbuf", [128, 256], "bfloat16"), "cntA": ("sbuf", [128, 256], "bfloat16"),
     "f0": ("sbuf", [128, 256], "float32"), "f1": ("sbuf", [128, 256], "float32"), "f2": ("sbuf", [128, 256], "float32"),
@@ -28,7 +28,9 @@ SCRATCH = {
     "keyS": ("sbuf", [128, 256], "float32"), "SS": ("sbuf", [128, 256], "float32"),
     "SB": ("sbuf", [128, 256], "float32"), "SG": ("sbuf", [128, 256], "float32"), "SC": ("sbuf", [128, 256], "float32"),
     "RC": ("sbuf", [128, 256], "bfloat16"), "RL": ("sbuf", [128, 256], "bfloat16"),
-    "eC": ("sbuf", [128, 256], "bfloat16"), "eL": ("sbuf", [128, 256], "bfloat16"),
+    "eC": ("sbuf", [128, 16, 8, 2], "bfloat16"), "eL": ("sbuf", [128, 256], "bfloat16"), "e2": ("sbuf", [128, 16, 8, 2], "bfloat16"),
+    "ER2": ("sbuf", [128, 256], "bfloat16"), "R2": ("sbuf", [128, 256], "bfloat16"), "x17": ("sbuf", [128, 256], "bfloat16"),
+    "HI": ("sbuf", [128, 128], "bfloat16"), "LO": ("sbuf", [128, 128], "bfloat16"),
     "EVC": ("sbuf", [128, 256], "float32"), "EVL": ("sbuf", [128, 256], "float32"),
     "ERC": ("sbuf", [128, 256], "bfloat16"), "ERL": ("sbuf", [128, 256], "bfloat16"),
     "Ya": ("sbuf", [128, 288], "float32"), "Yb": ("sbuf", [128, 288], "float32"), "Yc": ("sbuf", [128, 288], "float32"),
@@ -41,7 +43,7 @@ SCRATCH = {
     "D0": ("sbuf", [128, 256], "float32"), "D1": ("sbuf", [128, 256], "float32"), "D1h": ("sbuf", [128, 256], "bfloat16"),
     "fb": ("sbuf", [128, 256], "float32"), "RLM": ("sbuf", [128, 256 * TV], "bfloat16"), "limf": ("sbuf", [128, TV], "float32"),
     "col": ("sbuf", [128, 8], "float32"), "LF": ("sbuf", [128, 16 * 64], "float32"), "LI": ("sbuf", [128, 16 * 64], "int32"),
-    "bfl": ("sbuf", [128, 16], "bfloat16"), "U16": ("sbuf", [128, 32], "uint16"), "PM": ("sbuf", [128, 48], "uint16"),
+    "bfl": ("sbuf", [128, 16], "bfloat16"), "U16": ("sbuf", [128, 48], "uint16"), "PM": ("sbuf", [128, 48], "uint16"),
     "pC": ("psum", [128, 4, 16, 8], "float32"), "pL": ("psum", [128, 4, 16, 8], "float32"), "pS": ("psum", [128, 4, 16, 8], "float32"),
     "pM": ("psum", [128, 512], "float32"), "pT": ("psum", [128, 512], "float32"),
     "pD0": ("psum", [128, 512], "float32"), "pD1": ("psum", [128, 512], "float32"), "pD2": ("psum", [128, 512], "float32"),
@@ -53,7 +55,8 @@ SEMAPHORES = (["qV", "qS", "qP", "qG", "sent", "outs"] + ["ld_" + n for n in _LO
 
 
 ORDER = []
-LAT, PASSES, JIT = 0.12, 60, 3.0
+LAT, PASSES, JIT = 0.21, 2500, 1.0
+TTG, NET, SEED = 1.0, 1.2, 1
 
 
 def schedule(ops):
@@ -92,18 +95,21 @@ def schedule(ops):
                     heap.append((key[j], j))
             heap.sort(reverse=True)
         return out
-    order, best, x = list(range(n)), None, 1
+    order, best, x = list(range(n)), None, SEED
     for ps in range(PASSES):
         end = place(order, pred)
-        if best is None or max(end) < best[0] - 1e-9:
-            best = (max(end), sorted(range(n), key=lambda i: (end[i] - ops[i]["us"], i)), end)
-        key = []
-        for i in range(n):
+        if best is None or max(end) <= best[0]:
+            best = (max(end), end)
+        shift = {}
+        for c in sorted({o["at"] for o in ops}):
             x = (x * 1103515245 + 12345) % 2147483648
-            key.append(-best[2][i] + (JIT * x / 2147483648 if ps > 2 else 0.0))
-        back = place(ranked(key, succ, pred), succ)
-        order = sorted(range(n), key=lambda i: -back[i])
-    return best[1]
+            shift[c] = JIT * ((x >> 8) % 2001 / 1000.0 - 1.0) if (x >> 20) % 16 == 0 and ps > 2 else 0.0
+        if ps % 2:
+            order = ranked([best[1][i] - ops[i]["us"] + shift[ops[i]["at"]] for i in range(n)], pred, succ)
+        else:
+            back = place(ranked([shift[ops[i]["at"]] - best[1][i] for i in range(n)], succ, pred), succ)
+            order = sorted(range(n), key=lambda i: -back[i])
+    return sorted(range(n), key=lambda i: (best[1][i] - ops[i]["us"], i))
 
 
 def rank_program(g, core, T, topo):
@@ -125,6 +131,7 @@ def rank_program(g, core, T, topo):
             if seen[q].get(a, 0) < b:
                 seen[q][a] = b
 
+    since = [-5000]
     banks = {"pC", "pL", "pS", "pM", "pT", "pD0", "pD1", "pD2"}
 
     def do(q, reads, writes, calls, us=0.06, kind="call"):
@@ -144,7 +151,7 @@ def rank_program(g, core, T, topo):
         for t in reads:
             read.setdefault(t, set()).add(i)
         deps.discard(i)
-        ops.append({"q": q, "deps": deps, "calls": calls, "us": us, "kind": kind})
+        ops.append({"q": q, "deps": deps, "calls": calls, "us": us, "kind": kind, "at": i - since[0]})
         return ops[-1]
 
     def emit():
@@ -283,7 +290,9 @@ def rank_program(g, core, T, topo):
     fill(X("SELC", None, None, 2048), 0.0, 0.5)
     for b in ("EVC", "EVL"):
         fill(X(b), 0.0)
-    for b in ("ERC", "ERL"):
+    act(X("HI", None, None, 128), X("ID"), AF.Copy, 32 * BIG)
+    act(X("LO", None, None, 128), X("ID"), AF.Copy, -64 * BIG)
+    for b in ("ERC", "ERL", "ER2"):
         fill(X(b), -1.0, 0.5)
     for b in ("Ya", "Yb", "Yc"):
         fill(X(b, (slice(None), slice(0, 16)), b + "0", 16), 0.0)
@@ -371,12 +380,16 @@ def rank_program(g, core, T, topo):
            2 * 512 * 0.42e-3)
         act(pair(dst, r), bank, func, 1.0, bias)
 
-    def sums(src, bank, sl, const, ctok, b):
+    def sums(src, bank, sl, const, ctok, b, late=False):
         out = T[bank][:, 0:2, :, 2 * b:2 * b + 2]
         calls = [lambda: p.matmul(out, T.ID[:], const, True, False)]
+        if late:
+            calls += [(lambda e=e, w=w, m=m: p.matmul(T[bank][:, e, :, 2 * b:2 * b + 2], T[w][:], T[m][:, :, 2 * b:2 * b + 2, e], False, False))
+                      for e in range(2) for w, m in (("HI", "eC"), ("LO", "e2"))]
+            ctok = ctok + ["HI", "LO", "eC", "e2"]
         calls += [(lambda q=q: p.matmul(out, T[sl][:, 128 * q:128 * q + 128], T[src][:, 512 * b + q:512 * b + 512:16, :], False, q == 15))
                   for q in range(16)]
-        do("P", ["ID", sl, "%s:%d" % (src, 2 * b), "%s:%d" % (src, 2 * b + 1)] + ctok, ["%s:%d" % (bank, b)], calls, 17 * 64 * 0.42e-3)
+        do("P", ["ID", sl, "%s:%d" % (src, 2 * b), "%s:%d" % (src, 2 * b + 1)] + ctok, ["%s:%d" % (bank, b)], calls, len(calls) * 64 * 0.42e-3)
 
     def whole(bank):
         return ["%s:%d" % (bank, b) for b in range(4)]
@@ -393,12 +406,12 @@ def rank_program(g, core, T, topo):
             a, o = names(lst, t, 2 * r, 2 * r + 2), pair(xb if kind == "C" else "DL", r)
             do("V", a[1] + [yv, yv + "b"], [o[1]],
                [lambda a=a, o=o: v.tensor_tensor(out=o[0], in0=a[0], in1=T[yv][:], op=A.is_gt if kind == "C" else A.subtract)],
-               gcyc(512))
+               gcyc(512) * TTG)
             if kind == "L":
                 ts(pair("XL", r), o, 0.0, A.is_gt, k=0.5)
         for b in range(4):
             s = min(2, max(0, ns - 2 * b))
-            sums(xb, bank, "SELC", T.THR[:, :, 2 - s:4 - s], ["THa", "THb"], b)
+            sums(xb, bank, "SELC", T.THR[:, :, 2 - s:4 - s], ["THa", "THb"], b, kind == "C" and t > 0)
 
     def keyed(o, bank, b, c0):
         do("V", whole(bank) + [b[1]], [o],
@@ -419,7 +432,7 @@ def rank_program(g, core, T, topo):
         do("G", ["%s_%d" % (kind, t)], ["net" + a, "sends"],
            lambda: g.remote_dma(T["r" + kind][:, d], T[kind][:, c], T.sem[a], T.sem.sent, pid, rid, msk), 0.8, "send")
         do("W", ["net" + a], ["wire" + a], [], n / 116.0, "land")
-        do("N", ["wire" + a], ["r%s_%d" % (kind, t + 1)], [], 1.8, "land")["sig"] = (a, neng)
+        do("N", ["wire" + a], ["r%s_%d" % (kind, t + 1)], [], NET, "land")["sig"] = (a, neng)
         sent[0] += neng
 
     def u_sum(yv):
@@ -440,6 +453,17 @@ def rank_program(g, core, T, topo):
         tt(pa, pa, X(e), A.mult)
         tt(new, pa, old, A.add)
 
+    def late_row(val, yv):
+        l17, p17 = cols("U16", 32, 48, "l17"), cols("pM", 32, 48, "pM:x")
+        ts(I("n17"), val, 3, SHR, 4095, AND)
+        cp(l17, I("n17"))
+        tt(X("x17"), (pw[0].indirect(l17[0]), pw[1] + ["l17"], 256), cols(yv, 0, 256), A.is_gt)
+        mm(p17, [(X("ID"), X("THR", (slice(None), slice(0, 16), 2), "THb"))]
+           + [(selq("SELC", q), X("x17", (slice(None), slice(q, 256, 16)))) for q in range(16)])
+        tt(first("ER2"), p17, first("ERC"), A.max)
+        scan(X("R2"), X("D1h"), X("ER2"), A.mult, A.add, 0.5)
+        ts(X("e2"), X("R2"), ROW0, A.is_equal, k=0.5)
+
     stores = [0]
 
     def store(q, name, src, us=2.3):
@@ -451,16 +475,20 @@ def rank_program(g, core, T, topo):
 
     for t in range(TV):
         last = t == TV - 1
+        since[0] = len(ops) - (2000 if t == 0 else 1000 if last else 0)
         yv, yn = "y%d" % (t % 2), "y%d" % (1 - t % 2)
         c0, c1 = 256 * t, 256 * t + 256
         pk, lk = cols("PK", c0, c1, "PK_%d" % t), cols("LK", c0, c1, "LK_%d" % t)
         vc, vl = cols("VC", 16 * t, 16 * t + 16, "VC_%d" % t), cols("VL", 16 * t, 16 * t + 16, "VL_%d" % t)
         for kind, nm, word, tmp, top in (("C", "PK", pk, X("i1"), 4095), ("L", "LK", lk, X("i2"), 2047)):
             if t:
-                update(kind, cols("rV" + kind, 16 * t, 16 * t + 16, "rV%s_%d" % (kind, t)),
-                       cols("r" + nm, c0, c1, "r%s_%d" % (nm, t)), word)
-                ts(tmp, by(word, perm), 3, SHR, top, AND)
+                val = cols("rV" + kind, 16 * t, 16 * t + 16, "rV%s_%d" % (kind, t))
+                old = cols("r" + nm, c0, c1, "r%s_%d" % (nm, t))
+                update(kind, val, old, word)
+                ts(tmp, by(old if kind == "C" else word, perm), 3, SHR, top, AND)
                 cp(cols(kind + "16", c0, c1, "%s16_%d" % (kind, t)), tmp)
+                if kind == "C":
+                    late_row(val, yv)
             if not last:
                 send(nm, t)
         counts(t, "C")

@@ -5,10 +5,12 @@ BIG = float(2 ** 26)
 CAP = float(2 ** 24)
 NONE = float(2 ** 24 + 2 ** 14 + 6)
 ROW0 = 160.0
-MN_ON_V = True
-SPAIRS = {"C": [4] + [6] * (TV - 1), "L": [4] * TV}
+MN_ON_V = [True] * (TV - 1) + [False]
+DUP_ON_G, EARLY = False, "C"
+RELU, SPLIT, WIDE = [0] * TV, 1, 2
+SPAIRS = {"C": [4] + [7] * (TV - 1), "L": [4] + [3] * (TV - 1)}
 SCRATCH = {
-    "P": ("sbuf", [128, 4352], "bfloat16"), "NID": ("sbuf", [128, 128], "bfloat16"),
+    "P": ("sbuf", [128, 4368], "bfloat16"), "NID": ("sbuf", [128, 128], "bfloat16"),
     "GC": ("sbuf", [128, 4096], "bfloat16"), "GL": ("sbuf", [128, 4096], "bfloat16"),
     "XC": ("sbuf", [128, 2048, 2], "bfloat16"), "XL": ("sbuf", [128, 2048, 2], "bfloat16"),
     "DL": ("sbuf", [128, 2048, 2], "bfloat16"), "AB": ("sbuf", [128, 2048, 2], "bfloat16"),
@@ -16,8 +18,8 @@ SCRATCH = {
     "C16": ("sbuf", [128, 256 * TV], "uint16"), "L16": ("sbuf", [128, 256 * TV], "uint16"),
     "PK": ("sbuf", [128, 256 * TV], "int32"), "LK": ("sbuf", [128, 256 * TV], "int32"),
     "rPK": ("sbuf", [128, 256 * TV], "int32"), "rLK": ("sbuf", [128, 256 * TV], "int32"),
-    "VC": ("sbuf", [128, 16 * TV], "int32"), "VL": ("sbuf", [128, 16 * TV], "float32"),
-    "rVC": ("sbuf", [128, 16 * TV], "int32"), "rVL": ("sbuf", [128, 16 * TV], "float32"),
+    "VC": ("sbuf", [128, 16 * TV], "int32"), "VL": ("sbuf", [128, 16 * TV], "int32"),
+    "rVC": ("sbuf", [128, 16 * TV], "int32"), "rVL": ("sbuf", [128, 16 * TV], "int32"),
     "lemA": ("sbuf", [128, 256], "int32"), "conA": ("sbuf", [128, 256], "int32"), "limA": ("sbuf", [128, TV], "int32"),
     "orgA": ("sbuf", [128, 256], "bfloat16"), "cntA": ("sbuf", [128, 256], "bfloat16"),
     "f0": ("sbuf", [128, 256], "float32"), "f1": ("sbuf", [128, 256], "float32"), "f2": ("sbuf", [128, 256], "float32"),
@@ -25,10 +27,16 @@ SCRATCH = {
     "i0": ("sbuf", [128, 256], "int32"), "i1": ("sbuf", [128, 256], "int32"), "i2": ("sbuf", [128, 256], "int32"),
     "i3": ("sbuf", [128, 256], "int32"), "h0": ("sbuf", [128, 256], "bfloat16"), "h1": ("sbuf", [128, 256], "bfloat16"),
     "KC": ("sbuf", [128, 256], "float32"), "key": ("sbuf", [128, 256], "float32"), "keyL": ("sbuf", [128, 256], "float32"),
-    "keyS": ("sbuf", [128, 256], "float32"), "SS": ("sbuf", [128, 256], "float32"),
-    "SB": ("sbuf", [128, 256], "float32"), "SG": ("sbuf", [128, 256], "float32"), "SC": ("sbuf", [128, 256], "float32"),
+    "DS": ("sbuf", [128, 256], "float32"), "SS": ("sbuf", [128, 256], "float32"),
+    "SB": ("sbuf", [128, 256], "int32"), "SG": ("sbuf", [128, 256], "int32"), "SC": ("sbuf", [128, 256], "float32"),
     "RC": ("sbuf", [128, 256], "bfloat16"), "RL": ("sbuf", [128, 256], "bfloat16"),
-    "eC": ("sbuf", [128, 16, 8, 2], "bfloat16"), "eL": ("sbuf", [128, 256], "bfloat16"), "e2": ("sbuf", [128, 16, 8, 2], "bfloat16"),
+    "eC": ("sbuf", [128, 16, 8, 2], "bfloat16"), "eL": ("sbuf", [128, 16, 8, 2], "bfloat16"),
+    "UX": ("sbuf", [128, 32], "float32"), "AX": ("sbuf", [128, 32 * TV], "int32"), "HX": ("sbuf", [128, 32], "int32"),
+    "QA": ("sbuf", [128, 64], "float32"), "QB": ("sbuf", [128, 64], "int32"), "QC": ("sbuf", [128, 64], "float32"),
+    "NA": ("sbuf", [128, 64], "int32"), "NB": ("sbuf", [128, 64], "int32"), "NC": ("sbuf", [128, 64], "float32"),
+    "HA": ("sbuf", [128, 64], "float32"), "HB": ("sbuf", [128, 64], "int32"), "HC": ("sbuf", [128, 64], "float32"),
+    "DG": ("sbuf", [128, 256], "float32"), "KI16": ("sbuf", [128, 128], "bfloat16"), "FAR": ("sbuf", [128, 128], "bfloat16"),
+    "d17": ("sbuf", [128, 256], "bfloat16"), "g17": ("sbuf", [128, 256], "bfloat16"), "a17": ("sbuf", [128, 256], "bfloat16"), "e2": ("sbuf", [128, 16, 8, 2], "bfloat16"),
     "ER2": ("sbuf", [128, 256], "bfloat16"), "R2": ("sbuf", [128, 256], "bfloat16"), "x17": ("sbuf", [128, 256], "bfloat16"),
     "HI": ("sbuf", [128, 128], "bfloat16"), "LO": ("sbuf", [128, 128], "bfloat16"),
     "EVC": ("sbuf", [128, 256], "float32"), "EVL": ("sbuf", [128, 256], "float32"),
@@ -37,13 +45,13 @@ SCRATCH = {
     "Za": ("sbuf", [128, 544], "float32"), "Zb": ("sbuf", [128, 544], "float32"), "Zc": ("sbuf", [128, 544], "float32"),
     "ones": ("sbuf", [128, 256], "bfloat16"), "ID": ("sbuf", [128, 128], "bfloat16"), "BT": ("sbuf", [128, 128], "bfloat16"),
     "BLK": ("sbuf", [128, 128], "bfloat16"), "RK": ("sbuf", [128, 256], "bfloat16"),
-    "SELC": ("sbuf", [128, 2048], "bfloat16"), "SELS": ("sbuf", [128, 2048], "bfloat16"),
+    "SELC": ("sbuf", [128, 2048], "bfloat16"),
     "THR": ("sbuf", [128, 32, 4], "bfloat16"), "KI": ("sbuf", [128, 256], "float32"), "KB": ("sbuf", [128, 32, 8], "bfloat16"),
     "K16": ("sbuf", [128, 256], "float32"), "K20": ("sbuf", [128, 256], "float32"),
     "D0": ("sbuf", [128, 256], "float32"), "D1": ("sbuf", [128, 256], "float32"), "D1h": ("sbuf", [128, 256], "bfloat16"),
     "fb": ("sbuf", [128, 256], "float32"), "RLM": ("sbuf", [128, 256 * TV], "bfloat16"), "limf": ("sbuf", [128, TV], "float32"),
     "col": ("sbuf", [128, 8], "float32"), "LF": ("sbuf", [128, 16 * 64], "float32"), "LI": ("sbuf", [128, 16 * 64], "int32"),
-    "bfl": ("sbuf", [128, 16], "bfloat16"), "U16": ("sbuf", [128, 48], "uint16"), "PM": ("sbuf", [128, 48], "uint16"),
+    "bfl": ("sbuf", [128, 16], "bfloat16"), "U16": ("sbuf", [128, 80], "uint16"), "PM": ("sbuf", [128, 48], "uint16"),
     "pC": ("psum", [128, 4, 16, 8], "float32"), "pL": ("psum", [128, 4, 16, 8], "float32"), "pS": ("psum", [128, 4, 16, 8], "float32"),
     "pM": ("psum", [128, 512], "float32"), "pT": ("psum", [128, 512], "float32"),
     "pD0": ("psum", [128, 512], "float32"), "pD1": ("psum", [128, 512], "float32"), "pD2": ("psum", [128, 512], "float32"),
@@ -55,61 +63,91 @@ SEMAPHORES = (["qV", "qS", "qP", "qG", "sent", "outs"] + ["ld_" + n for n in _LO
 
 
 ORDER = []
-LAT, PASSES, JIT = 0.21, 2500, 1.0
-TTG, NET, SEED = 1.0, 1.2, 1
+LAT, PASSES, JIT = 0.21, 8000, 0.4
+TTG, NET, SEED, WARM, FEW = 1.0, 1.2, 3, 0.3, 3
+MILE, SLOW, BACK, SLOWNET, FARW = 0.3, 0.4, 4, 2.0, 0.5
 
 
 def schedule(ops):
     n = len(ops)
-    pred = [sorted(o["deps"]) for o in ops]
-    succ = [[] for _ in ops]
+    us, queue, pred, above = [o["us"] for o in ops], [o["q"] for o in ops], [], []
+    slow = [o["us"] * o["slow"] for o in ops]
+    wide = [o["us"] * (SLOWNET if o["q"] in "NWG" and o["kind"] != "call" and o["deps"] else 1.0) for o in ops]
+    for o in ops:
+        far = 0
+        for d in o["deps"]:
+            far |= above[d]
+        pred.append(sorted(d for d in o["deps"] if not far >> d & 1))
+        above.append(far | sum(1 << d for d in pred[-1]))
+    succ, same = [[] for _ in ops], {}
     for i in range(n):
+        same.setdefault(ops[i]["at"], []).append(i)
         for d in pred[i]:
             succ[d].append(i)
+    same = [same[c] for c in sorted(same)]
 
     def place(order, before):
-        end, busy = [0.0] * n, {}
+        end, busy = [0.0] * n, {q: [] for q in queue}
         for i in order:
-            us, q = ops[i]["us"], ops[i]["q"]
-            s = max([end[d] + LAT for d in before[i]] + [0.0])
-            if q != "N":
-                line = busy.setdefault(q, [])
-                j = len(line)
+            s = 0.0
+            for d in before[i]:
+                if end[d] > s:
+                    s = end[d]
+            s += LAT
+            if queue[i] != "N":
+                line = busy[queue[i]]
+                j = m = len(line)
                 while j and line[j - 1][1] > s:
                     j -= 1
-                while j < len(line) and line[j][0] < s + us:
-                    s = max(s, line[j][1])
+                while j < m and line[j][0] < s + us[i]:
+                    if line[j][1] > s:
+                        s = line[j][1]
                     j += 1
-                line.insert(j, (s, s + us))
-            end[i] = s + us
+                line.insert(j, (s, s + us[i]))
+            end[i] = s + us[i]
         return end
-    def ranked(key, before, after):
-        left, heap, out = [len(b) for b in before], [], []
-        heap = sorted(((key[i], i) for i in range(n) if not left[i]), reverse=True)
-        while heap:
-            i = heap.pop()[1]
-            out.append(i)
-            for j in after[i]:
-                left[j] -= 1
-                if not left[j]:
-                    heap.append((key[j], j))
-            heap.sort(reverse=True)
-        return out
-    order, best, x = list(range(n)), None, SEED
+
+    def replay(order, slow):
+        out, free = [0.0] * n, {q: 0.0 for q in queue}
+        for i in order:
+            s = 0.0
+            for d in pred[i]:
+                if out[d] > s:
+                    s = out[d]
+            s += LAT
+            if queue[i] != "N":
+                s = max(s, free[queue[i]])
+                free[queue[i]] = s + slow[i]
+            out[i] = s + slow[i]
+        return max(out)
+    marks = [i for i in range(n) if us[i] == 0.85]
+    order, best, top, x = list(range(n)), None, None, SEED
     for ps in range(PASSES):
         end = place(order, pred)
-        if best is None or max(end) <= best[0]:
-            best = (max(end), end)
-        shift = {}
-        for c in sorted({o["at"] for o in ops}):
+        base = max(end) + MILE * sum(end[i] for i in marks)
+        if best is None or base < best[2] + 1.0:
+            order = sorted(range(n), key=lambda i: end[i] - us[i])
+            span = base + SLOW * replay(order, slow) + FARW * replay(order, wide)
+            if best is None or span <= best[0] + WARM * (1.0 - ps / PASSES) * ((x >> 4) % 64) / 64.0:
+                best = (span, end, base)
+        if top is None or best[0] < top[0]:
+            top = best
+        back = ps % BACK == 0
+        key = [-e for e in best[1]] if back else [e - u for e, u in zip(best[1], us)]
+        for _ in range(FEW if ps > 2 else 0):
             x = (x * 1103515245 + 12345) % 2147483648
-            shift[c] = JIT * ((x >> 8) % 2001 / 1000.0 - 1.0) if (x >> 20) % 16 == 0 and ps > 2 else 0.0
-        if ps % 2:
-            order = ranked([best[1][i] - ops[i]["us"] + shift[ops[i]["at"]] for i in range(n)], pred, succ)
-        else:
-            back = place(ranked([shift[ops[i]["at"]] - best[1][i] for i in range(n)], succ, pred), succ)
-            order = sorted(range(n), key=lambda i: -back[i])
-    return sorted(range(n), key=lambda i: (best[1][i] - ops[i]["us"], i))
+            for i in same[(x >> 8) % len(same)]:
+                key[i] += JIT * 2 ** (ps % 5) * ((x >> 3) % 2001 / 1000.0 - 1.0)
+        before = succ if back else pred
+        for i in (range(n) if back else range(n - 1, -1, -1)):
+            for d in before[i]:
+                if key[d] > key[i] - us[d] - LAT:
+                    key[d] = key[i] - us[d] - LAT
+        order = sorted(range(n), key=lambda i: key[i])
+        if back:
+            key = place(order, succ)
+            order = sorted(range(n), key=lambda i: -key[i])
+    return sorted(range(n), key=lambda i: (top[1][i] - us[i], i))
 
 
 def rank_program(g, core, T, topo):
@@ -131,6 +169,7 @@ def rank_program(g, core, T, topo):
             if seen[q].get(a, 0) < b:
                 seen[q][a] = b
 
+    gathers = {0.85}
     since = [-5000]
     banks = {"pC", "pL", "pS", "pM", "pT", "pD0", "pD1", "pD2"}
 
@@ -151,7 +190,8 @@ def rank_program(g, core, T, topo):
         for t in reads:
             read.setdefault(t, set()).add(i)
         deps.discard(i)
-        ops.append({"q": q, "deps": deps, "calls": calls, "us": us, "kind": kind, "at": i - since[0]})
+        ops.append({"q": q, "deps": deps, "calls": calls, "us": us, "kind": kind, "at": i - since[0],
+                    "slow": 1.3 if q in "NWGY" else 1.9 if us in gathers else 1.4})
         return ops[-1]
 
     def emit():
@@ -203,10 +243,22 @@ def rank_program(g, core, T, topo):
     def final(name):
         return X(name, (slice(None), slice(15, 256, 16)), None, 16)
 
+    def odd(name):
+        return X(name, (slice(None), slice(1, 32, 2)), name + "1", 16)
+
+    def nth(name, j):
+        return X(name, (slice(None), slice(j, 64, 4)), name + str(j), 16)
+
+    def scan4(name, op0, op1):
+        do("V", [name + z + str(j) for z in "AB" for j in range(4)], [name + "C" + str(j) for j in range(4)],
+           [lambda: v.tensor_tensor_scan(out=T[name + "C"][:], data0=T[name + "A"][:], data1=T[name + "B"][:], initial=0.0,
+                                         op0=op0, op1=op1)], cyc(64))
+
     def cyc(n):
         return max(64, n) * 0.83e-3
 
     def gcyc(n):
+        gathers.add(0.055 + n * 1.56 * 0.83e-3)
         return 0.055 + n * 1.56 * 0.83e-3
 
     v, s_, p = g.vector, g.scalar, g.tensor
@@ -257,7 +309,7 @@ def rank_program(g, core, T, topo):
         eng[q].dma_start(dst[0], T[name][:]).then_inc(T.sem[s], 16)
         do("N", [], [dst[1]], [], 4.5 if name == "prop" else 2.3, "land")["sig"] = (s, 16)
     load("Y", "con", X("conA"))
-    load("S", "prop", cols("P", 0, 2048))
+    load("S", "prop", cols("P", 16, 2064))
     load("Y", "ex", cols("y0", 0, 256))
     act(cols("y0", 256, 512, "y0b"), cols("y0", 0, 256), AF.Copy)
     load("Y", "lem", X("lemA"))
@@ -278,26 +330,34 @@ def rank_program(g, core, T, topo):
     sel(X("BT"), one128, [[-16, 8], [0, 16]], A.is_ge, 0.0, 0, 1)
     sel(X("BLK"), X("BT"), [[16, 8], [0, 16]], A.is_ge, 0.0, 15, -1)
     iota(cols("KI", 0, 256), [[0, 16], [1, 16]], 0, 0)
-    iota(X("KB"), [[1, 2], [0, 16], [2, 8]], 0, 0)
+    iota(X("KB"), [[1, 2], [0, 16], [2, 8]], int(ROW0), 0)
     fill(X("fb"), -float(2 ** 30))
     fill(X("SC"), 1.0)
     sel(X("D0"), X("fb"), [[0, 16], [1, 16]], A.is_gt, NONE, 0, 0)
     sel(X("D1"), X("SC"), [[0, 16], [1, 16]], A.is_gt, 0.0, 0, 0)
     iota(X("K16"), [[0, 16], [4096, 16]], 0, 0)
-    fill(cols("P", 2048, 2304, "Pz"), 0.0, 0.5)
+    fill(cols("P", 2064, 2080, "Pz"), 0.0, 0.5)
+    fill(cols("P", 0, 16, "Py"), 0.0, 0.5)
     fill(X("THR", (slice(None), slice(None), slice(0, 2)), "THa", 64), 3.0 * BIG)
     fill(X("THR", (slice(None), slice(None), slice(2, 4)), "THb", 64), 9.5 * BIG)
     fill(X("SELC", None, None, 2048), 0.0, 0.5)
     for b in ("EVC", "EVL"):
-        fill(X(b), 0.0)
+        iota(X(b), [[0, 256]], 0, 0)
     act(X("HI", None, None, 128), X("ID"), AF.Copy, 32 * BIG)
     act(X("LO", None, None, 128), X("ID"), AF.Copy, -64 * BIG)
     for b in ("ERC", "ERL", "ER2"):
-        fill(X(b), -1.0, 0.5)
+        iota(X(b), [[0, 256]], -1, 0)
     for b in ("Ya", "Yb", "Yc"):
         fill(X(b, (slice(None), slice(0, 16)), b + "0", 16), 0.0)
         fill(X(b, (slice(None), slice(272, 288)), b + "1", 16), 0.0)
     fill(I("w"), 0)
+    fill(X("UX", (slice(None), slice(0, 32, 2)), None, 16), 0.0)
+    for nm, c, c0 in (("QA", 0.0, -2.0 ** 30), ("NA", 1, -2 ** 30), ("NB", -2 ** 30, None), ("HA", 1.0, 0.0)):
+        do("V", [], [nm + str(j) for j in range(4)], [lambda nm=nm, c=c: v.memset(T[nm][:], c)], cyc(64))
+        if c0 is not None:
+            fill(nth(nm, 0), c0)
+    iota(X("AX", None, None, 32 * TV), [[32 * 97, TV], [0, 32]], 0, 0)
+    act(X("DG"), X("D0"), AF.Copy)
     perm, tm, tk = cols("PM", 0, 16, "perm"), cols("PM", 16, 32, "tm"), cols("PM", 32, 48, "tk")
     ts(I("q"), I("p"), 15, AND)
     ts(I("gq0"), I("p"), 4, SHR)
@@ -316,22 +376,23 @@ def rank_program(g, core, T, topo):
     ts(F("o2"), I("o2"), 272.0, A.mult)
     tt(F("o2"), F("o2"), F("cb"), A.add)
     cp(tm, F("o2"))
-    ts(F("cd8"), F("cb"), 8.0, A.mult, 18432.0, A.add)
+    ts(nth("HB", 1), F("cb"), 8.0, A.mult, 18432.0, A.add)
     cp(cols("col", 2, 3, "kq"), X("LI", (slice(None), slice(16 * lanes["LI"]["q"], 16 * lanes["LI"]["q"] + 1)), "LI:q", 1))
-    ts(cols("col", 3, 4, "k16"), cols("col", 2, 3, "kq"), 65536.0, A.mult)
+    ts(cols("col", 3, 4, "k16"), cols("col", 2, 3, "kq"), -8192.0, A.mult)
+    ts(cols("col", 4, 5, "kb"), cols("col", 2, 3, "kq"), -16.0, A.mult, ROW0 - 0.48, A.add)
     ts(X("RK"), X("KI"), T.col[:, 2:3], A.is_equal, extra=["kq"])
-    do("V", ["BLK"], ["SELC"],
-       [(lambda i=i: v.tensor_scalar(out=T.SELC[:, 129 * i:128 * i + 128:16], in0=T.BLK[:, 0:128:16], scalar1=-BIG, scalar2=None,
-                                     op0=A.mult)) for i in range(16)], 0.9)
-    act(X("SELS", None, None, 2048), X("SELC"), AF.Copy, -16.0 / BIG)
+    do("S", ["BLK"], ["SELC"],
+       [(lambda i=i: s_.activation(out=T.SELC[:, 129 * i:128 * i + 128:16], in_=T.BLK[:, 0:128:16], func=AF.Copy, scale=-BIG))
+        for i in range(16)], 0.86)
+    act(X("KB"), X("KB"), AF.Copy, -BIG / 16)
     act(X("NID", None, None, 128), X("ID"), AF.Copy, -1.0)
     act(X("K20"), X("K16"), AF.Copy, 256.0)
     act(X("K16"), X("K16"), AF.Copy, 16.0)
     act(X("D1h"), X("D1"), AF.Copy)
-    ts(cols("pT", 256, 512, "pT:k"), X("KI"), 0.0625, A.mult)
+    act(X("DS"), X("D1"), AF.Identity, 65536.0625, -65536.0)
     ts(X("limf", None, None, TV), X("limA"), 16384.0, A.mult)
     for t in range(TV):
-        act(cols("RLM", 256 * t, 256 * t + 256, "RLM_%d" % t), X("RK"), AF.Copy, T.limf[:, t:t + 1], extra=["limf"])
+        act(cols("RLM", 128 * t, 128 * t + 128, "RLM_%d" % t), X("BLK"), AF.Copy, T.limf[:, t:t + 1], extra=["limf"])
 
     def turn(y, z):
         do("V", [y, y + "0", y + "1"], [z], [lambda: v.transpose(out=T[z][:, 0:256], in_=T[y][:, 16:272]),
@@ -341,30 +402,29 @@ def rank_program(g, core, T, topo):
     def mid(y):
         return cols(y, 16, 272)
 
-    emp = X("f0")
-    ts(emp, X("conA"), 0.0, A.is_lt)
-    ts(X("f1"), emp, 2049.0, A.mult)
-    tt(mid("Ya"), X("f1"), X("conA"), A.add)
-    cp(cols("C16", 0, 256, "C16_0"), by(turn("Ya", "Za"), tk))
+    cp(mid("Ya"), X("conA"))
+    ts(cols("C16", 0, 256, "C16_0"), by(turn("Ya", "Za"), tk), 16.0, A.add)
     ts(mid("Yb"), X("lemA"), 8.0, A.mult)
     ts(cols("L16", 0, 256, "L16_0"), by(turn("Yb", "Zb"), tk), 0.125, A.mult)
     tt(cols("LK", 0, 256, "LK_0"), by(X("Zb"), tm), X("K16"), A.add)
-    pt = cols("pT", 0, 256, "pT:a")
-    act(pt, emp, AF.Identity, 7.0, 1.0)
-    act(X("f2"), X("orgA"), AF.Copy, 65536.0)
-    act(X("f3"), mid("Ya"), AF.Copy, 8.0)
-    tt(pt, pt, X("cntA"), A.mult)
-    tt(pt, pt, X("f2"), A.add)
-    tt(mid("Yc"), pt, X("f3"), A.add)
+    pt, px = cols("pT", 0, 256, "pT:a"), cols("pM", 256, 512, "pM:l")
+    act(X("h0"), mid("Ya"), AF.Relu, -16384.0)
+    act(pt, X("h0"), AF.Identity, 7.0 / 16384, 1.0)
+    act(X("h1"), X("orgA"), AF.Copy, 65536.0)
+    act(X("f3"), mid("Ya"), AF.Relu, 8.0)
+    tt(X("mn"), pt, X("cntA"), A.mult)
+    mm(px, [(X("ID"), X("h0")), (X("ID"), X("h1")), (X("ID"), X("mn"))])
+    tt(mid("Yc"), px, X("f3"), A.add)
     tt(cols("PK", 0, 256, "PK_0"), by(turn("Yc", "Zc"), tm), X("K20"), A.add)
 
     def selq(nm, q):
         return cols(nm, 128 * q, 128 * q + 128, nm)
-    pw = (T.P[:, 0:2064], ["P", "Pz"], 2064)
+    pw = (T.P[:, 16:2080], ["P", "Pz"], 2064)
 
     def names(lst, t, k0, k1):
         off = cols(lst, 256 * t + 16 * k0, 256 * t + 16 * k1, "%s_%d" % (lst, t))
-        return (pw[0].indirect(off[0]), pw[1] + [off[1]], 256 * (k1 - k0))
+        win = T.P[:, 0:2080] if (lst, t) == ("C16", 0) else pw[0]
+        return (win.indirect(off[0]), pw[1] + ["Py", off[1]], 256 * (k1 - k0))
 
     def pair(buf, r):
         return X(buf, (slice(None), slice(512 * (r // 2), 512 * (r // 2) + 512), r % 2), "%s:%d" % (buf, r), 512)
@@ -375,21 +435,29 @@ def rank_program(g, core, T, topo):
         bank = X("pD%d" % (turnb[0] % 3), None, None, 512)
         turnb[0] += 1
         gs = cols(src, 512 * r, 512 * r + 512, "%s:%d" % (src, r))
-        do("P", ["ID", "NID", yv, yv + "b", gs[1]], [bank[1]],
-           [lambda: p.matmul(bank[0], T.NID[:], T[yv][:], True, False), lambda: p.matmul(bank[0], T.ID[:], gs[0], False, True)],
-           2 * 512 * 0.42e-3)
+        do("P", ["ID", "NID", yv, gs[1]], [bank[1]],
+           [lambda: p.matmul(bank[0], T.ID[:], gs[0], True, False),
+            lambda: p.matmul(T[bank[1]][:, 0:256], T.NID[:], T[yv][:, 0:256], False, False),
+            lambda: p.matmul(T[bank[1]][:, 256:512], T.NID[:], T[yv][:, 0:256], False, True)], 2 * 512 * 0.42e-3)
         act(pair(dst, r), bank, func, 1.0, bias)
 
-    def sums(src, bank, sl, const, ctok, b, late=False):
+    def sums(src, bank, sl, const, ctok, b, late=(), more=()):
         out = T[bank][:, 0:2, :, 2 * b:2 * b + 2]
         calls = [lambda: p.matmul(out, T.ID[:], const, True, False)]
-        if late:
-            calls += [(lambda e=e, w=w, m=m: p.matmul(T[bank][:, e, :, 2 * b:2 * b + 2], T[w][:], T[m][:, :, 2 * b:2 * b + 2, e], False, False))
-                      for e in range(2) for w, m in (("HI", "eC"), ("LO", "e2"))]
-            ctok = ctok + ["HI", "LO", "eC", "e2"]
+        calls += [(lambda e=e, w=w, m=m: p.matmul(T[bank][:, e, :, 2 * b:2 * b + 2], T[w][:], T[m][:, :, 2 * b:2 * b + 2, e], False, False))
+                  for e in range(2) for w, m in late]
+        ctok = ctok + [z for wm in late for z in wm]
+        if more:
+            j = slice(more[0] % 2, 2)
+            calls += [(lambda q=q: p.matmul(T[bank][:, 0:2, :, more[0]:2 * b + 2], T[sl][:, 128 * q:128 * q + 128],
+                                            T.DL[:, 512 * b + q:512 * b + 512:16, j], False, False)) for q in range(16)]
+            ctok = ctok + ["DL:%d" % r for r in more]
+        if (bank, b) == ("pL", 3):
+            calls.append(lambda: p.matmul(T.pL[:, 1, :, 7], T.HI[:], T.bfl[:], False, False))
+            ctok = ctok + ["HI", "bfl"]
         calls += [(lambda q=q: p.matmul(out, T[sl][:, 128 * q:128 * q + 128], T[src][:, 512 * b + q:512 * b + 512:16, :], False, q == 15))
                   for q in range(16)]
-        do("P", ["ID", sl, "%s:%d" % (src, 2 * b), "%s:%d" % (src, 2 * b + 1)] + ctok, ["%s:%d" % (bank, b)], calls, len(calls) * 64 * 0.42e-3)
+        do("P", ["ID", sl, ] + ["%s:%d%s" % (src, r, z) for r in (2 * b, 2 * b + 1) for z in ("", "+")] + ctok, ["%s:%d" % (bank, b)], calls, len(calls) * 64 * 0.42e-3)
 
     def whole(bank):
         return ["%s:%d" % (bank, b) for b in range(4)]
@@ -398,12 +466,22 @@ def rank_program(g, core, T, topo):
         lst, gb, xb, bank, ns = kind + "16", "G" + kind, "X" + kind, "p" + kind, SPAIRS[kind][t]
         yv = "y%d" % (t % 2)
         for r in range(ns + 1):
-            if r < ns:
-                act(cols(gb, 512 * r, 512 * r + 512, "%s:%d" % (gb, r)), names(lst, t, 2 * r, 2 * r + 2), AF.Copy)
+            if r < ns and r % WIDE == 0:
+                e = min(ns, r + WIDE)
+                a = names(lst, t, 2 * r, 2 * e)
+                do("S", a[1], ["%s:%d" % (gb, z) for z in range(r, e)],
+                   [lambda a=a, r=r, e=e: s_.activation(out=T[gb][:, 512 * r:512 * e], in_=a[0], func=AF.Copy)], gcyc(a[2]))
             if r:
                 differ(yv, gb, r - 1, xb, AF.Sign, -0.5)
         for r in range(7, ns - 1, -1):
             a, o = names(lst, t, 2 * r, 2 * r + 2), pair(xb if kind == "C" else "DL", r)
+            if kind == "C" and t and r >= 8 - SPLIT:
+                for e in range(2):
+                    a = names(lst, t, 2 * r + e, 2 * r + e + 1)
+                    c = slice(512 * (r // 2) + 256 * e, 512 * (r // 2) + 256 * e + 256)
+                    do("V", a[1] + [yv], [o[1] + "+" * e],
+                       [lambda a=a, c=c, r=r: v.tensor_tensor(out=T.XC[:, c, r % 2], in0=a[0], in1=T[yv][:, 0:256], op=A.is_gt)], gcyc(256))
+                continue
             do("V", a[1] + [yv, yv + "b"], [o[1]],
                [lambda a=a, o=o: v.tensor_tensor(out=o[0], in0=a[0], in1=T[yv][:], op=A.is_gt if kind == "C" else A.subtract)],
                gcyc(512) * TTG)
@@ -411,7 +489,8 @@ def rank_program(g, core, T, topo):
                 ts(pair("XL", r), o, 0.0, A.is_gt, k=0.5)
         for b in range(4):
             s = min(2, max(0, ns - 2 * b))
-            sums(xb, bank, "SELC", T.THR[:, :, 2 - s:4 - s], ["THa", "THb"], b, kind == "C" and t > 0)
+            sums(xb, bank, "SELC", T.THR[:, :, 2 - s:4 - s], ["THa", "THb"], b,
+                 [] if not t or kind not in EARLY else [("HI", "eC"), ("LO", "e2")] if kind == "C" else [("HI", "eL")])
 
     def keyed(o, bank, b, c0):
         do("V", whole(bank) + [b[1]], [o],
@@ -429,7 +508,7 @@ def rank_program(g, core, T, topo):
         c = slice(n * t, n * t + n)
         d = slice(n * t + n, n * t + 2 * n)
         a = "a%s_%d" % (kind, t + 1)
-        do("G", ["%s_%d" % (kind, t)], ["net" + a, "sends"],
+        do("G", ["%s_%d" % (kind, t)], ["net" + a],
            lambda: g.remote_dma(T["r" + kind][:, d], T[kind][:, c], T.sem[a], T.sem.sent, pid, rid, msk), 0.8, "send")
         do("W", ["net" + a], ["wire" + a], [], n / 116.0, "land")
         do("N", ["wire" + a], ["r%s_%d" % (kind, t + 1)], [], NET, "land")["sig"] = (a, neng)
@@ -437,9 +516,9 @@ def rank_program(g, core, T, topo):
 
     def u_sum(yv):
         pu = cols("pM", 0, 16, "pM:u")
-        mm(pu, [(selq("SELS", q), X(yv, (slice(None), slice(q, 256, 16)))) for q in range(16)])
-        act(F("u8"), pu, AF.Identity, 1.0 / 64, 8.0)
-        act(F("sq"), pu, AF.Square, 1.0 / 32, 296.0)
+        mm(pu, [(selq("SELC", q), X(yv, (slice(None), slice(q, 256, 16)))) for q in range(16)])
+        act(odd("UX"), pu, AF.Identity, -1.0 / BIG, 32.0)
+        act(F("sq"), pu, AF.Square, -0.5 / BIG, 296.0)
 
     def update(kind, val, old, new):
         e_row, e_val, R, e = "ER" + kind, "EV" + kind, "R" + kind, "e" + kind
@@ -464,6 +543,21 @@ def rank_program(g, core, T, topo):
         scan(X("R2"), X("D1h"), X("ER2"), A.mult, A.add, 0.5)
         ts(X("e2"), X("R2"), ROW0, A.is_equal, k=0.5)
 
+    def late_lemma(val, yv):
+        l17, pc, ps = cols("U16", 48, 64, "m17"), cols("pM", 48, 64, "pM:c"), cols("pM", 64, 80, "pM:s")
+        ts(I("m17"), val, 3, SHR, 2047, AND)
+        cp(l17, I("m17"))
+        tt(X("d17"), (pw[0].indirect(l17[0]), pw[1] + ["m17"], 256), cols(yv, 0, 256), A.subtract)
+        ts(X("g17"), X("d17"), 0.0, A.is_gt, k=0.5)
+        act(X("a17"), X("d17"), AF.Abs)
+        ts(F("far"), val, -float(2 ** 23), A.add)
+        mm(pc, [(X("ID"), X("THR", (slice(None), slice(0, 16), 2), "THb"))]
+           + [(selq("SELC", q), X("g17", (slice(None), slice(q, 256, 16)))) for q in range(16)])
+        tt(F("k17"), pc, val, A.max)
+        mm(ps, [(X("KI16"), first("ERL"))] + [(selq("SELC", q), X("a17", (slice(None), slice(q, 256, 16)))) for q in range(16)])
+        act(F("s0"), ps, AF.Copy, -16.0 / BIG)
+        tt(F("s17"), F("s0"), F("far"), A.max)
+
     stores = [0]
 
     def store(q, name, src, us=2.3):
@@ -485,129 +579,139 @@ def rank_program(g, core, T, topo):
                 val = cols("rV" + kind, 16 * t, 16 * t + 16, "rV%s_%d" % (kind, t))
                 old = cols("r" + nm, c0, c1, "r%s_%d" % (nm, t))
                 update(kind, val, old, word)
-                ts(tmp, by(old if kind == "C" else word, perm), 3, SHR, top, AND)
+                ts(tmp, by(old if kind in EARLY else word, perm), 3, SHR, top, AND)
                 cp(cols(kind + "16", c0, c1, "%s16_%d" % (kind, t)), tmp)
-                if kind == "C":
-                    late_row(val, yv)
+                if kind in EARLY:
+                    (late_row if kind == "C" else late_lemma)(val, yv)
             if not last:
                 send(nm, t)
         counts(t, "C")
         lp = cols("pM", 256, 512, "pM:l")
-        mm(lp, [(X("BLK"), cols("RLM", c0, c1, "RLM_%d" % t))])
+        mm(lp, [(cols("RLM", 128 * t, 128 * t + 128, "RLM_%d" % t), X("RK"))])
         x, sl = X("i0"), I("sl")
         ts(x, pk, 0x4007, AND)
         tt(X("KC"), lp, pk, A.add)
-        tt(X("keyS"), cols("pT", 256, 512, "pT:k"), x, A.subtract)
-        scan(X("SS"), X("D0"), X("keyS"), A.max, A.min)
-        ts(sl, final("SS"), 16.0, A.mult)
+        scan(X("SS"), X("DS"), x, A.add, A.max)
+        ts(sl, final("SS"), -16.0, A.mult, -1.0, A.add)
         ts(sl, sl, 15, AND)
         ts(F("sP"), sl, float(2 ** 20), A.mult)
         keyed("key", "pC", ("KC", "KC"), 0)
         scan(X("SB"), X("D0"), X("key"), A.max, A.min)
-        mb, mi = final("SB"), I("mi")
-        cp(mi, mb)
+        mb = mi = final("SB")
+        tb = final("DG")
         ts(X("bfl", None, None, 16), mb, CAP, A.is_lt)
-        ts(F("tb"), mb, CAP, A.is_lt, NONE, A.mult)
+        ts(tb, mb, CAP, A.is_lt, NONE, A.mult)
         ts(I("lim"), mi, 14, SHR, 3, AND)
         ts(I("b"), mi, 7, AND)
-        ts(I("t2"), mi, 0x3FFF, AND)
-        ts(I("t1"), mi, 0x1FF0000, AND)
-        ts(I("vb"), mi, 0x0F3FF8, AND)
+        ts(nth("NB", 0), mi, 0x3FFF, AND)
+        ts(nth("NA", 2), mi, 0x1FF0000, AND)
+        ts(nth("QB", 2), mi, 0x0F3FF8, AND)
         tt(F("bl"), I("b"), I("lim"), A.subtract)
-        ts(F("t2p"), I("t2"), 1.0, A.add)
         tt(F("ov"), F("bl"), I("w"), A.is_ge)
-        ts(F("o14"), F("ov"), 16384.0, A.mult)
-        ts(F("nov"), F("ov"), -NONE, A.mult, NONE, A.add)
-        tt(F("z"), F("o14"), F("t2p"), A.max)
-        tt(F("vB"), F("nov"), I("vb"), A.max)
-        tt(F("nb"), F("z"), I("t1"), A.add)
+        ts(nth("NB", 1), F("ov"), 16384.0, A.mult)
+        ts(nth("QB", 1), F("ov"), -NONE, A.mult, NONE, A.add)
+        scan4("N", A.add, A.max)
         if not last:
             mm(cols("pM", 16, 32, "pM:w"), [(cols("RK", 0, 128), X("bfl"))])
             cp(I("w"), cols("pM", 16, 32, "pM:w"))
             ts(I("w"), I("w"), 3, AND)
         ts(I("fs"), F("sq"), 8.0 * t - 296.0 * 296.0, A.add)
         ts(I("fs"), I("fs"), 16376, AND)
-        tt(F("nw"), I("fs"), F("tb"), A.subtract)
+        tt(nth("QA", 1), I("fs"), tb, A.subtract)
         counts(t, "L")
+        late = t and "L" in EARLY
         ns = SPAIRS["L"][t]
         for r in range(7, ns - 1, -1):
-            act(pair("AB", r), pair("DL", r), AF.Abs)
+            if r < 8 - RELU[t]:
+                act(pair("AB", r), pair("DL", r), AF.Abs)
+            else:
+                ts(pair("AB", r), pair("DL", r), -2.0, A.mult, 0.0, A.max, k=0.5)
         for r in range(ns):
             differ(yv, "GL", r, "AB", AF.Abs, 0.0)
         for b in (3, 2, 1, 0):
-            sums("AB", "pS", "SELS", T.KB[:, :, 2 * b:2 * b + 2], ["KB"], b)
+            sums("AB", "pS", "SELC", T.KB[:, :, 2 * b:2 * b + 2], ["KB"], b, [("FAR", "eL")] if late else [], [r for r in (2 * b, 2 * b + 1) if r >= 8 - RELU[t]])
         keyed("keyL", "pL", ("LK", lk[1]), c0)
-        scan(X("SG"), X("D0"), X("keyL"), A.max, A.min)
-        gq = I("gq")
-        tt(gq, final("SG"), F("tb"), A.max)
+        scan(X("SG"), X("DG"), X("keyL"), A.max, A.min)
+        gq = final("SG")
+        if late:
+            tt(F("k17"), F("k17"), tb, A.max)
+            tt(I("gq"), gq, F("k17"), A.min)
+            gq = I("gq")
         tt(F("ng"), F("sP"), gq, A.add)
-        tt(vc, F("ng"), F("nb"), A.min)
-        ts(I("al"), gq, 3, SHR, 4095, AND)
+        tt(vc, F("ng"), nth("NC", 2), A.min)
         if last:
             update("C", vc, pk, mid("Ya"))
         else:
             send("VC", t)
         a16, n16 = cols("U16", 0, 16, "a16"), cols("U16", 16, 32, "n16")
-        cp(a16, I("al"))
-        tt(F("x"), F("u8"), I("al"), A.mult)
-        ts(F("gf"), gq, CAP, A.is_lt, 18432.0, A.mult)
-        ts(I("h"), F("x"), 776.0 * t - 2.0 ** 20 - 0.375, A.add)
-        tt(F("cg"), F("cd8"), F("gf"), A.subtract)
-        ts(I("h"), I("h"), 14336, AND)
-        tt(F("n8"), I("h"), F("cg"), A.add)
-        ts(n16, F("n8"), 0.125, A.mult)
-        pa = (pw[0].indirect(a16[0]), pw[1] + ["a16"], 256)
         y, y2 = cols(yv, 0, 256), cols(yn, 0, 256)
+        al, ax = X("AX", (slice(None), slice(32 * t, 32 * t + 32, 2)), None, 16), cols("AX", 32 * t, 32 * t + 32)
+        ts(al, gq, 3, SHR, 4095, AND)
+        ts(nth("HB", 2), gq, CAP, A.is_lt, -18432.0, A.mult)
+        ts(nth("HB", 3), gq, 0x10F0000, AND)
+        cp(a16, al)
+        do("V", ["UX", "UX1", "AX"], ["HX"],
+           [lambda ax=ax: v.tensor_tensor_scan(out=T.HX[:], data0=T.UX[:], data1=ax[0], initial=0.0, op0=A.mult, op1=A.add)], cyc(32))
+        ts(nth("HB", 0), X("HX", (slice(None), slice(1, 32, 2)), None, 16), 2, SHR, 14336, AND)
+        scan4("H", A.mult, A.add)
+        ts(n16, nth("HC", 2), 0.125, A.mult)
+        pa = (pw[0].indirect(a16[0]), pw[1] + ["a16"], 256)
         act(X("pa"), pa, AF.Copy)
         dy = X("pC", (slice(None), slice(2, 4)), "pC:y")
         mm(dy, [(X("ID"), X("pa")), (X("NID"), y)])
         act(y2, dy, AF.Abs)
-        if MN_ON_V or last:
+        if MN_ON_V[t]:
             tt(X("mn"), pa, y, A.min)
         else:
             dm = X("pL", (slice(None), slice(2, 4)), "pL:m")
             mm(dm, [(X("ID"), X("pa")), (X("ID"), y), (X("NID"), y2)])
             act(X("mn"), dm, AF.Copy, 0.5)
         do("V", ["mn", "n16"], ["P"],
-           [lambda: v.tensor_copy(out=T.P[:, 0:4352].indirect(T.U16[:, 16:32]), in_=T.mn[:])], 0.85)
+           [lambda: v.tensor_copy(out=T.P[:, 16:4368].indirect(T.U16[:, 16:32]), in_=T.mn[:])], 0.85)
         if not last:
-            act(cols(yn, 256, 512, yn + "b"), dy, AF.Abs)
+            if DUP_ON_G:
+                sel(cols(yn, 256, 512, yn + "b"), y2, [[0, 256]], A.is_ge, 0.0, 0, 0)
+            else:
+                act(cols(yn, 256, 512, yn + "b"), dy, AF.Abs)
             u_sum(yn)
         if last:
-            store("Y", "zp", cols("P", 0, 2048), 4.5)
+            store("Y", "zp", cols("P", 16, 2064), 4.5)
             store("Y", "zy", y2)
-            cp(X("i0"), by(turn("Ya", "Za"), tm))
+            turned = by(turn("Ya", "Za"), tm)
+            cp(X("i0"), turned)
+            act(X("h1"), turned, AF.Identity, 2.0 ** -16, T.col[:, 4:5], extra=["kb"])
+            act(X("h1"), X("h1"), AF.Identity, 1.0, -ROW0)
+            store("S", "zo", X("h1"))
             ts(X("i1"), X("i0"), 3, SHR, 4095, AND)
             ts(X("i2"), X("i0"), 7, AND)
-            ts(X("f0"), X("i1"), 2048.0, A.is_ge)
-            ts(X("f2"), X("i1"), -2048.0, A.add)
-            ts(X("f0"), X("f0"), -4097.0, A.mult, 4096.0, A.add)
-            tt(X("h0"), X("f2"), X("i2"), A.max)
-            tt(X("f1"), X("i1"), X("f0"), A.min)
-            ts(X("i3"), X("i0"), 16, SHR, 15, AND)
+            pe, pf = cols("pD0", 0, 256), cols("pD1", 0, 256)
+            ts(pe, X("i1"), -2048.0, A.add)
+            tt(X("h0"), pe, X("i2"), A.max)
             store("Y", "zb", X("h0"))
+            ts(pf, X("i1"), 2048.0, A.is_lt, 4096.0, A.mult)
+            act(pf, pf, AF.Identity, 1.0, -1.0)
+            tt(X("f1"), pf, X("i1"), A.min)
             store("Y", "zc", X("f1"))
-            cp(X("h1"), X("i3"))
-            store("Y", "zo", X("h1"))
         do("S", whole("pS"), ["f4"],
-           [(lambda e=e: s_.activation(out=T.f4[:, e:256:2], in_=T.pS[:, e], func=AF.Copy)) for e in range(2)], cyc(256))
+           [(lambda e=e: s_.activation(out=T.f4[:, e:256:2], in_=T.pS[:, e], func=AF.Copy, scale=-16.0 / BIG))
+            for e in range(2)], cyc(256))
         scan(X("SC"), X("D0"), X("f4"), A.max, A.min)
-        ts(I("gk"), gq, 0x10F0000, AND)
-        ts(F("gB"), gq, -1.0, A.mult, float(2 ** 22), A.add)
-        tt(F("vG"), F("n8"), I("gk"), A.add)
-        tt(F("vX"), F("vB"), F("gB"), A.max)
-        ts(I("ks"), final("SC"), 65536.0, A.mult, -2.0 ** 31, A.add)
-        ts(I("ks"), I("ks"), 0xF0000, AND)
-        tt(F("vC"), I("ks"), F("nw"), A.add)
-        tt(F("vC"), F("vC"), F("vX"), A.max)
-        tt(vl, F("vC"), F("vG"), A.min)
+        ts(nth("QB", 3), gq, -1.0, A.mult, float(2 ** 22), A.add)
+        ms = final("SC")
+        if late:
+            tt(F("ms"), ms, F("s17"), A.min)
+            ms = F("ms")
+        ts(I("ks"), ms, 65536.0, A.mult, -2.0 ** 31, A.add)
+        ts(nth("QB", 0), I("ks"), 0xF0000, AND)
+        scan4("Q", A.add, A.max)
+        tt(vl, nth("QC", 3), nth("HC", 3), A.min)
         if last:
             update("L", vl, lk, mid("Yb"))
         else:
             send("VL", t)
 
-    ts(X("f3"), by(turn("Yb", "Zb"), tm), T.col[:, 3:4], A.subtract, 0.125, A.mult, extra=["k16"])
-    store("Y", "zl", X("f3"))
+    act(X("f3"), by(turn("Yb", "Zb"), tm), AF.Identity, 0.125, T.col[:, 3:4], extra=["k16"])
+    store("S", "zl", X("f3"))
     emit()
     g.sync.wait_ge(T.sem.outs, stores[0])
     g.wait_ge(T.sem.sent, sent[0])

from concourse.mybir import AluOpType as A, ActivationFunctionType as AF, AxisListType as AX

TV, HOP = 6, 5
BIG = float(2 ** 26)
CAP = float(2 ** 24)
NONE = float(2 ** 24 + 2 ** 14 + 6)
ROW0 = 160.0
MN_ON_V = [True] * (TV - 1) + [False]
DUP_ON_G, EARLY = False, "C"
RELU, SPLIT, WIDE = [0] * TV, 1, 2
SPAIRS = {"C": [4] + [7] * (TV - 1), "L": [4] + [3] * (TV - 1)}
SCRATCH = {
    "P": ("sbuf", [128, 4368], "bfloat16"), "NID": ("sbuf", [128, 128], "bfloat16"),
    "GC": ("sbuf", [128, 4096], "bfloat16"), "GL": ("sbuf", [128, 4096], "bfloat16"),
    "XC": ("sbuf", [128, 2048, 2], "bfloat16"), "XL": ("sbuf", [128, 2048, 2], "bfloat16"),
    "DL": ("sbuf", [128, 2048, 2], "bfloat16"), "AB": ("sbuf", [128, 2048, 2], "bfloat16"),
    "y0": ("sbuf", [128, 512], "bfloat16"), "y1": ("sbuf", [128, 512], "bfloat16"), "pa": ("sbuf", [128, 256], "bfloat16"), "mn": ("sbuf", [128, 256], "bfloat16"),
    "C16": ("sbuf", [128, 256 * TV], "uint16"), "L16": ("sbuf", [128, 256 * TV], "uint16"),
    "PK": ("sbuf", [128, 256 * TV], "int32"), "LK": ("sbuf", [128, 256 * TV], "int32"),
    "rPK": ("sbuf", [128, 256 * TV], "int32"), "rLK": ("sbuf", [128, 256 * TV], "int32"),
    "VC": ("sbuf", [128, 16 * TV], "int32"), "VL": ("sbuf", [128, 16 * TV], "int32"),
    "rVC": ("sbuf", [128, 16 * TV], "int32"), "rVL": ("sbuf", [128, 16 * TV], "int32"),
    "lemA": ("sbuf", [128, 256], "int32"), "conA": ("sbuf", [128, 256], "int32"), "limA": ("sbuf", [128, TV], "int32"),
    "orgA": ("sbuf", [128, 256], "bfloat16"), "cntA": ("sbuf", [128, 256], "bfloat16"),
    "f0": ("sbuf", [128, 256], "float32"), "f1": ("sbuf", [128, 256], "float32"), "f2": ("sbuf", [128, 256], "float32"),
    "f3": ("sbuf", [128, 256], "float32"), "f4": ("sbuf", [128, 256], "float32"),
    "i0": ("sbuf", [128, 256], "int32"), "i1": ("sbuf", [128, 256], "int32"), "i2": ("sbuf", [128, 256], "int32"),
    "i3": ("sbuf", [128, 256], "int32"), "h0": ("sbuf", [128, 256], "bfloat16"), "h1": ("sbuf", [128, 256], "bfloat16"),
    "KC": ("sbuf", [128, 256], "float32"), "key": ("sbuf", [128, 256], "float32"), "keyL": ("sbuf", [128, 256], "float32"),
    "DS": ("sbuf", [128, 256], "float32"), "SS": ("sbuf", [128, 256], "float32"),
    "SB": ("sbuf", [128, 256], "int32"), "SG": ("sbuf", [128, 256], "int32"), "SC": ("sbuf", [128, 256], "float32"),
    "RC": ("sbuf", [128, 256], "bfloat16"), "RL": ("sbuf", [128, 256], "bfloat16"),
    "eC": ("sbuf", [128, 16, 8, 2], "bfloat16"), "eL": ("sbuf", [128, 16, 8, 2], "bfloat16"),
    "UX": ("sbuf", [128, 32], "float32"), "AX": ("sbuf", [128, 32 * TV], "int32"), "HX": ("sbuf", [128, 32], "int32"),
    "QA": ("sbuf", [128, 64], "float32"), "QB": ("sbuf", [128, 64], "int32"), "QC": ("sbuf", [128, 64], "float32"),
    "NA": ("sbuf", [128, 64], "int32"), "NB": ("sbuf", [128, 64], "int32"), "NC": ("sbuf", [128, 64], "float32"),
    "HA": ("sbuf", [128, 64], "float32"), "HB": ("sbuf", [128, 64], "int32"), "HC": ("sbuf", [128, 64], "float32"),
    "DG": ("sbuf", [128, 256], "float32"), "KI16": ("sbuf", [128, 128], "bfloat16"), "FAR": ("sbuf", [128, 128], "bfloat16"),
    "d17": ("sbuf", [128, 256], "bfloat16"), "g17": ("sbuf", [128, 256], "bfloat16"), "a17": ("sbuf", [128, 256], "bfloat16"), "e2": ("sbuf", [128, 16, 8, 2], "bfloat16"),
    "ER2": ("sbuf", [128, 256], "bfloat16"), "R2": ("sbuf", [128, 256], "bfloat16"), "x17": ("sbuf", [128, 256], "bfloat16"),
    "HI": ("sbuf", [128, 128], "bfloat16"), "LO": ("sbuf", [128, 128], "bfloat16"),
    "EVC": ("sbuf", [128, 256], "float32"), "EVL": ("sbuf", [128, 256], "float32"),
    "ERC": ("sbuf", [128, 256], "bfloat16"), "ERL": ("sbuf", [128, 256], "bfloat16"),
    "Ya": ("sbuf", [128, 288], "float32"), "Yb": ("sbuf", [128, 288], "float32"), "Yc": ("sbuf", [128, 288], "float32"),
    "Za": ("sbuf", [128, 544], "float32"), "Zb": ("sbuf", [128, 544], "float32"), "Zc": ("sbuf", [128, 544], "float32"),
    "ones": ("sbuf", [128, 256], "bfloat16"), "ID": ("sbuf", [128, 128], "bfloat16"), "BT": ("sbuf", [128, 128], "bfloat16"),
    "BLK": ("sbuf", [128, 128], "bfloat16"), "RK": ("sbuf", [128, 256], "bfloat16"),
    "SELC": ("sbuf", [128, 2048], "bfloat16"),
    "THR": ("sbuf", [128, 32, 4], "bfloat16"), "KI": ("sbuf", [128, 256], "float32"), "KB": ("sbuf", [128, 32, 8], "bfloat16"),
    "K16": ("sbuf", [128, 256], "float32"), "K20": ("sbuf", [128, 256], "float32"),
    "D0": ("sbuf", [128, 256], "float32"), "D1": ("sbuf", [128, 256], "float32"), "D1h": ("sbuf", [128, 256], "bfloat16"),
    "fb": ("sbuf", [128, 256], "float32"), "RLM": ("sbuf", [128, 256 * TV], "bfloat16"), "limf": ("sbuf", [128, TV], "float32"),
    "col": ("sbuf", [128, 8], "float32"), "LF": ("sbuf", [128, 16 * 64], "float32"), "LI": ("sbuf", [128, 16 * 64], "int32"),
    "bfl": ("sbuf", [128, 16], "bfloat16"), "U16": ("sbuf", [128, 80], "uint16"), "PM": ("sbuf", [128, 48], "uint16"),
    "pC": ("psum", [128, 4, 16, 8], "float32"), "pL": ("psum", [128, 4, 16, 8], "float32"), "pS": ("psum", [128, 4, 16, 8], "float32"),
    "pM": ("psum", [128, 512], "float32"), "pT": ("psum", [128, 512], "float32"),
    "pD0": ("psum", [128, 512], "float32"), "pD1": ("psum", [128, 512], "float32"), "pD2": ("psum", [128, 512], "float32"),
}
_LOADS = ["prop", "lem", "con", "ex", "lim", "org", "cnt"]
_KINDS = ["PK", "LK", "VC", "VL"]
SEMAPHORES = (["qV", "qS", "qP", "qG", "sent", "outs"] + ["ld_" + n for n in _LOADS]
              + ["a%s_%d" % (k, t) for k in _KINDS for t in range(1, TV)])


ORDER = []
LAT, PASSES, JIT = 0.21, 8000, 0.4
TTG, NET, SEED, WARM, FEW = 1.0, 1.2, 3, 0.3, 3
MILE, SLOW, BACK, SLOWNET, FARW = 0.3, 0.4, 4, 2.0, 0.5


def schedule(ops):
    n = len(ops)
    us, queue, pred, above = [o["us"] for o in ops], [o["q"] for o in ops], [], []
    slow = [o["us"] * o["slow"] for o in ops]
    wide = [o["us"] * (SLOWNET if o["q"] in "NWG" and o["kind"] != "call" and o["deps"] else 1.0) for o in ops]
    for o in ops:
        far = 0
        for d in o["deps"]:
            far |= above[d]
        pred.append(sorted(d for d in o["deps"] if not far >> d & 1))
        above.append(far | sum(1 << d for d in pred[-1]))
    succ, same = [[] for _ in ops], {}
    for i in range(n):
        same.setdefault(ops[i]["at"], []).append(i)
        for d in pred[i]:
            succ[d].append(i)
    same = [same[c] for c in sorted(same)]

    def place(order, before):
        end, busy = [0.0] * n, {q: [] for q in queue}
        for i in order:
            s = 0.0
            for d in before[i]:
                if end[d] > s:
                    s = end[d]
            s += LAT
            if queue[i] != "N":
                line = busy[queue[i]]
                j = m = len(line)
                while j and line[j - 1][1] > s:
                    j -= 1
                while j < m and line[j][0] < s + us[i]:
                    if line[j][1] > s:
                        s = line[j][1]
                    j += 1
                line.insert(j, (s, s + us[i]))
            end[i] = s + us[i]
        return end

    def replay(order, slow):
        out, free = [0.0] * n, {q: 0.0 for q in queue}
        for i in order:
            s = 0.0
            for d in pred[i]:
                if out[d] > s:
                    s = out[d]
            s += LAT
            if queue[i] != "N":
                s = max(s, free[queue[i]])
                free[queue[i]] = s + slow[i]
            out[i] = s + slow[i]
        return max(out)
    marks = [i for i in range(n) if us[i] == 0.85]
    order, best, top, x = list(range(n)), None, None, SEED
    for ps in range(PASSES):
        end = place(order, pred)
        base = max(end) + MILE * sum(end[i] for i in marks)
        if best is None or base < best[2] + 1.0:
            order = sorted(range(n), key=lambda i: end[i] - us[i])
            span = base + SLOW * replay(order, slow) + FARW * replay(order, wide)
            if best is None or span <= best[0] + WARM * (1.0 - ps / PASSES) * ((x >> 4) % 64) / 64.0:
                best = (span, end, base)
        if top is None or best[0] < top[0]:
            top = best
        back = ps % BACK == 0
        key = [-e for e in best[1]] if back else [e - u for e, u in zip(best[1], us)]
        for _ in range(FEW if ps > 2 else 0):
            x = (x * 1103515245 + 12345) % 2147483648
            for i in same[(x >> 8) % len(same)]:
                key[i] += JIT * 2 ** (ps % 5) * ((x >> 3) % 2001 / 1000.0 - 1.0)
        before = succ if back else pred
        for i in (range(n) if back else range(n - 1, -1, -1)):
            for d in before[i]:
                if key[d] > key[i] - us[d] - LAT:
                    key[d] = key[i] - us[d] - LAT
        order = sorted(range(n), key=lambda i: key[i])
        if back:
            key = place(order, succ)
            order = sorted(range(n), key=lambda i: -key[i])
    return sorted(range(n), key=lambda i: (top[1][i] - us[i], i))


def rank_program(g, core, T, topo):
    rank = T.rank_of(core)
    if rank is None:
        return
    eng = {"V": g.vector, "S": g.scalar, "P": g.tensor, "G": g, "Y": g.sync}
    cnt = {}
    seen = {q: {} for q in eng}
    snap = {}
    ops, wrote, read, run = [], {}, {}, {}

    def require(q, dep):
        s, n = dep
        if seen[q].get(s, 0) >= n:
            return
        eng[q].wait_ge(T.sem[s], n)
        for a, b in list(snap.get(dep, {}).items()) + [dep]:
            if seen[q].get(a, 0) < b:
                seen[q][a] = b

    gathers = {0.85}
    since = [-5000]
    banks = {"pC", "pL", "pS", "pM", "pT", "pD0", "pD1", "pD2"}

    def do(q, reads, writes, calls, us=0.06, kind="call"):
        i, deps = len(ops), set()
        for t in reads + writes:
            deps |= wrote.get(t, set())
        for t in writes:
            deps |= read.get(t, set())
        for b in {t.split(":")[0] for t in reads + writes} & banks:
            r = run.setdefault(b, [q, [], []])
            if r[0] != q:
                run[b] = r = [q, [], r[1]]
            r[1].append(i)
            deps |= set(r[2])
        for t in writes:
            wrote[t], read[t] = {i}, set()
        for t in reads:
            read.setdefault(t, set()).add(i)
        deps.discard(i)
        ops.append({"q": q, "deps": deps, "calls": calls, "us": us, "kind": kind, "at": i - since[0],
                    "slow": 1.3 if q in "NWGY" else 1.9 if us in gathers else 1.4})
        return ops[-1]

    def emit():
        if not ORDER:
            ORDER.extend(schedule(ops))
        for i in ORDER:
            o = ops[i]
            q = o["q"]
            if o["kind"] == "land":
                continue
            deps = {}
            for d in o["deps"]:
                if ops[d]["kind"] != "send":
                    a, b = ops[d]["sig"]
                    deps[a] = max(deps.get(a, 0), b)
            for a in sorted(deps, key=lambda a: a == "q" + q):
                require(q, (a, deps[a]))
            if o["kind"] == "call":
                a = "q" + q
                for c in o["calls"]:
                    c().then_inc(T.sem[a], 1)
                    cnt[a] = cnt.get(a, 0) + 1
                o["sig"] = (a, cnt[a])
                snap[o["sig"]] = dict(seen[q])
            else:
                o["calls"]()

    def X(name, idx=None, tok=None, n=256):
        return (T[name][:] if idx is None else T[name][idx], tok or name, n)

    def cols(name, a, b, tok=None):
        return X(name, (slice(None), slice(a, b)), tok, b - a)

    lanes = {"LF": {}, "LI": {}}

    def lane(buf, n):
        j = lanes[buf].setdefault(n, len(lanes[buf]))
        return cols(buf, 16 * j, 16 * j + 16, buf + ":" + n)

    def F(n):
        return lane("LF", n)

    def I(n):
        return lane("LI", n)

    def first(name):
        return X(name, (slice(None), slice(0, 256, 16)), None, 16)

    def final(name):
        return X(name, (slice(None), slice(15, 256, 16)), None, 16)

    def odd(name):
        return X(name, (slice(None), slice(1, 32, 2)), name + "1", 16)

    def nth(name, j):
        return X(name, (slice(None), slice(j, 64, 4)), name + str(j), 16)

    def scan4(name, op0, op1):
        do("V", [name + z + str(j) for z in "AB" for j in range(4)], [name + "C" + str(j) for j in range(4)],
           [lambda: v.tensor_tensor_scan(out=T[name + "C"][:], data0=T[name + "A"][:], data1=T[name + "B"][:], initial=0.0,
                                         op0=op0, op1=op1)], cyc(64))

    def cyc(n):
        return max(64, n) * 0.83e-3

    def gcyc(n):
        gathers.add(0.055 + n * 1.56 * 0.83e-3)
        return 0.055 + n * 1.56 * 0.83e-3

    v, s_, p = g.vector, g.scalar, g.tensor

    def by(win, off):
        return (win[0].indirect(off[0]), [win[1], off[1]], 16 * off[2])

    def toks(a):
        return a[1] if isinstance(a[1], list) else [a[1]]

    def cost(o, a, k=1.0):
        return gcyc(a[2]) if isinstance(a[1], list) else cyc(o[2] * k)

    def tt(o, a, b, op):
        do("V", toks(a) + [b[1]], [o[1]], [lambda: v.tensor_tensor(out=o[0], in0=a[0], in1=b[0], op=op)],
           cost(o, a, 1 if {toks(a)[0].split(":")[0], b[1].split(":")[0]} & banks else 2))

    def ts(o, a, s1, op0, s2=None, op1=None, extra=(), k=1.0):
        kw = {"op1": op1} if op1 is not None else {}
        do("V", toks(a) + list(extra), [o[1]],
           [lambda: v.tensor_scalar(out=o[0], in0=a[0], scalar1=s1, scalar2=s2, op0=op0, **kw)], cost(o, a, k))

    def cp(o, a, k=1.0):
        do("V", toks(a), [o[1]], [lambda: v.tensor_copy(out=o[0], in_=a[0])], cost(o, a, k))

    def fill(o, c, k=1.0):
        do("V", [], [o[1]], [lambda: v.memset(o[0], c)], cyc(o[2] * k))

    def scan(o, d0, d1, op0, op1, k=1.0):
        do("V", [d0[1]] + toks(d1), [o[1]],
           [lambda: v.tensor_tensor_scan(out=o[0], data0=d0[0], data1=d1[0], initial=0.0, op0=op0, op1=op1)], cyc(o[2] * k))

    def act(o, a, func, scale=1.0, bias=0.0, extra=()):
        do("S", toks(a) + list(extra), [o[1]], [lambda: s_.activation(out=o[0], in_=a[0], func=func, scale=scale, bias=bias)],
           cost(o, a))

    def mm(o, pairs):
        reads = [t[1] for pr in pairs for t in pr]
        n = len(pairs)
        do("P", reads, [o[1]], [(lambda i=i, l=l, r=r: p.matmul(o[0], l[0], r[0], i == 0, i == n - 1)) for i, (l, r) in enumerate(pairs)],
           n * max(64, o[2]) * 0.42e-3)

    SHR, AND = A.logical_shift_right, A.bitwise_and

    def load(q, name, dst):
        s = "ld_" + name
        cnt[s] = 16
        eng[q].dma_start(dst[0], T[name][:]).then_inc(T.sem[s], 16)
        do("N", [], [dst[1]], [], 4.5 if name == "prop" else 2.3, "land")["sig"] = (s, 16)
    load("Y", "con", X("conA"))
    load("S", "prop", cols("P", 16, 2064))
    load("Y", "ex", cols("y0", 0, 256))
    act(cols("y0", 256, 512, "y0b"), cols("y0", 0, 256), AF.Copy)
    load("Y", "lem", X("lemA"))
    load("Y", "org", X("orgA"))
    load("Y", "cnt", X("cntA"))
    load("Y", "lim", X("limA"))

    def sel(o, a, pat, cmp, fillv, base, cm):
        do("G", [a[1]], [o[1]], [lambda: g.affine_select(o[0], a[0], pat, cmp, fillv, base, cm)], 0.17 + 2 * cyc(o[2]))

    def iota(o, pat, base, cm):
        do("G", [], [o[1]], [lambda: g.iota(o[0], pat, base, cm, allow_small_or_imprecise_dtypes=True)], 0.13 + 2 * cyc(o[2]))
    iota(I("p"), [[0, 16]], 0, 1)
    iota(I("pj"), [[1, 16]], 0, 0)
    fill(X("ones"), 1.0, 0.5)
    one128 = cols("ones", 0, 128)
    sel(X("ID"), one128, [[-1, 128]], A.is_equal, 0.0, 0, 1)
    sel(X("BT"), one128, [[-16, 8], [0, 16]], A.is_ge, 0.0, 0, 1)
    sel(X("BLK"), X("BT"), [[16, 8], [0, 16]], A.is_ge, 0.0, 15, -1)
    iota(cols("KI", 0, 256), [[0, 16], [1, 16]], 0, 0)
    iota(X("KB"), [[1, 2], [0, 16], [2, 8]], int(ROW0), 0)
    fill(X("fb"), -float(2 ** 30))
    fill(X("SC"), 1.0)
    sel(X("D0"), X("fb"), [[0, 16], [1, 16]], A.is_gt, NONE, 0, 0)
    sel(X("D1"), X("SC"), [[0, 16], [1, 16]], A.is_gt, 0.0, 0, 0)
    iota(X("K16"), [[0, 16], [4096, 16]], 0, 0)
    fill(cols("P", 2064, 2080, "Pz"), 0.0, 0.5)
    fill(cols("P", 0, 16, "Py"), 0.0, 0.5)
    fill(X("THR", (slice(None), slice(None), slice(0, 2)), "THa", 64), 3.0 * BIG)
    fill(X("THR", (slice(None), slice(None), slice(2, 4)), "THb", 64), 9.5 * BIG)
    fill(X("SELC", None, None, 2048), 0.0, 0.5)
    for b in ("EVC", "EVL"):
        iota(X(b), [[0, 256]], 0, 0)
    act(X("HI", None, None, 128), X("ID"), AF.Copy, 32 * BIG)
    act(X("LO", None, None, 128), X("ID"), AF.Copy, -64 * BIG)
    for b in ("ERC", "ERL", "ER2"):
        iota(X(b), [[0, 256]], -1, 0)
    for b in ("Ya", "Yb", "Yc"):
        fill(X(b, (slice(None), slice(0, 16)), b + "0", 16), 0.0)
        fill(X(b, (slice(None), slice(272, 288)), b + "1", 16), 0.0)
    fill(I("w"), 0)
    fill(X("UX", (slice(None), slice(0, 32, 2)), None, 16), 0.0)
    for nm, c, c0 in (("QA", 0.0, -2.0 ** 30), ("NA", 1, -2 ** 30), ("NB", -2 ** 30, None), ("HA", 1.0, 0.0)):
        do("V", [], [nm + str(j) for j in range(4)], [lambda nm=nm, c=c: v.memset(T[nm][:], c)], cyc(64))
        if c0 is not None:
            fill(nth(nm, 0), c0)
    iota(X("AX", None, None, 32 * TV), [[32 * 97, TV], [0, 32]], 0, 0)
    act(X("DG"), X("D0"), AF.Copy)
    perm, tm, tk = cols("PM", 0, 16, "perm"), cols("PM", 16, 32, "tm"), cols("PM", 32, 48, "tk")
    ts(I("q"), I("p"), 15, AND)
    ts(I("gq0"), I("p"), 4, SHR)
    ts(F("q16"), I("q"), 16.0, A.mult)
    tt(F("pv"), F("q16"), I("pj"), A.add)
    cp(perm, F("pv"))
    tt(I("o1"), I("q"), I("gq0"), A.add)
    ts(I("o1"), I("o1"), 1, AND)
    ts(F("o1"), I("o1"), 272.0, A.mult)
    tt(F("o1"), F("o1"), F("pv"), A.add)
    cp(tk, F("o1"))
    ts(F("j16"), I("pj"), 16.0, A.mult)
    tt(F("cb"), F("j16"), I("q"), A.add)
    tt(I("o2"), I("pj"), I("gq0"), A.add)
    ts(I("o2"), I("o2"), 1, AND)
    ts(F("o2"), I("o2"), 272.0, A.mult)
    tt(F("o2"), F("o2"), F("cb"), A.add)
    cp(tm, F("o2"))
    ts(nth("HB", 1), F("cb"), 8.0, A.mult, 18432.0, A.add)
    cp(cols("col", 2, 3, "kq"), X("LI", (slice(None), slice(16 * lanes["LI"]["q"], 16 * lanes["LI"]["q"] + 1)), "LI:q", 1))
    ts(cols("col", 3, 4, "k16"), cols("col", 2, 3, "kq"), -8192.0, A.mult)
    ts(cols("col", 4, 5, "kb"), cols("col", 2, 3, "kq"), -16.0, A.mult, ROW0 - 0.48, A.add)
    ts(X("RK"), X("KI"), T.col[:, 2:3], A.is_equal, extra=["kq"])
    do("S", ["BLK"], ["SELC"],
       [(lambda i=i: s_.activation(out=T.SELC[:, 129 * i:128 * i + 128:16], in_=T.BLK[:, 0:128:16], func=AF.Copy, scale=-BIG))
        for i in range(16)], 0.86)
    act(X("KB"), X("KB"), AF.Copy, -BIG / 16)
    act(X("NID", None, None, 128), X("ID"), AF.Copy, -1.0)
    act(X("K20"), X("K16"), AF.Copy, 256.0)
    act(X("K16"), X("K16"), AF.Copy, 16.0)
    act(X("D1h"), X("D1"), AF.Copy)
    act(X("DS"), X("D1"), AF.Identity, 65536.0625, -65536.0)
    ts(X("limf", None, None, TV), X("limA"), 16384.0, A.mult)
    for t in range(TV):
        act(cols("RLM", 128 * t, 128 * t + 128, "RLM_%d" % t), X("BLK"), AF.Copy, T.limf[:, t:t + 1], extra=["limf"])

    def turn(y, z):
        do("V", [y, y + "0", y + "1"], [z], [lambda: v.transpose(out=T[z][:, 0:256], in_=T[y][:, 16:272]),
                                             lambda: v.transpose(out=T[z][:, 256:544], in_=T[y][:, 0:288])], cyc(544))
        return X(z)

    def mid(y):
        return cols(y, 16, 272)

    cp(mid("Ya"), X("conA"))
    ts(cols("C16", 0, 256, "C16_0"), by(turn("Ya", "Za"), tk), 16.0, A.add)
    ts(mid("Yb"), X("lemA"), 8.0, A.mult)
    ts(cols("L16", 0, 256, "L16_0"), by(turn("Yb", "Zb"), tk), 0.125, A.mult)
    tt(cols("LK", 0, 256, "LK_0"), by(X("Zb"), tm), X("K16"), A.add)
    pt, px = cols("pT", 0, 256, "pT:a"), cols("pM", 256, 512, "pM:l")
    act(X("h0"), mid("Ya"), AF.Relu, -16384.0)
    act(pt, X("h0"), AF.Identity, 7.0 / 16384, 1.0)
    act(X("h1"), X("orgA"), AF.Copy, 65536.0)
    act(X("f3"), mid("Ya"), AF.Relu, 8.0)
    tt(X("mn"), pt, X("cntA"), A.mult)
    mm(px, [(X("ID"), X("h0")), (X("ID"), X("h1")), (X("ID"), X("mn"))])
    tt(mid("Yc"), px, X("f3"), A.add)
    tt(cols("PK", 0, 256, "PK_0"), by(turn("Yc", "Zc"), tm), X("K20"), A.add)

    def selq(nm, q):
        return cols(nm, 128 * q, 128 * q + 128, nm)
    pw = (T.P[:, 16:2080], ["P", "Pz"], 2064)

    def names(lst, t, k0, k1):
        off = cols(lst, 256 * t + 16 * k0, 256 * t + 16 * k1, "%s_%d" % (lst, t))
        win = T.P[:, 0:2080] if (lst, t) == ("C16", 0) else pw[0]
        return (win.indirect(off[0]), pw[1] + ["Py", off[1]], 256 * (k1 - k0))

    def pair(buf, r):
        return X(buf, (slice(None), slice(512 * (r // 2), 512 * (r // 2) + 512), r % 2), "%s:%d" % (buf, r), 512)

    turnb = [0]

    def differ(yv, src, r, dst, func, bias):
        bank = X("pD%d" % (turnb[0] % 3), None, None, 512)
        turnb[0] += 1
        gs = cols(src, 512 * r, 512 * r + 512, "%s:%d" % (src, r))
        do("P", ["ID", "NID", yv, gs[1]], [bank[1]],
           [lambda: p.matmul(bank[0], T.ID[:], gs[0], True, False),
            lambda: p.matmul(T[bank[1]][:, 0:256], T.NID[:], T[yv][:, 0:256], False, False),
            lambda: p.matmul(T[bank[1]][:, 256:512], T.NID[:], T[yv][:, 0:256], False, True)], 2 * 512 * 0.42e-3)
        act(pair(dst, r), bank, func, 1.0, bias)

    def sums(src, bank, sl, const, ctok, b, late=(), more=()):
        out = T[bank][:, 0:2, :, 2 * b:2 * b + 2]
        calls = [lambda: p.matmul(out, T.ID[:], const, True, False)]
        calls += [(lambda e=e, w=w, m=m: p.matmul(T[bank][:, e, :, 2 * b:2 * b + 2], T[w][:], T[m][:, :, 2 * b:2 * b + 2, e], False, False))
                  for e in range(2) for w, m in late]
        ctok = ctok + [z for wm in late for z in wm]
        if more:
            j = slice(more[0] % 2, 2)
            calls += [(lambda q=q: p.matmul(T[bank][:, 0:2, :, more[0]:2 * b + 2], T[sl][:, 128 * q:128 * q + 128],
                                            T.DL[:, 512 * b + q:512 * b + 512:16, j], False, False)) for q in range(16)]
            ctok = ctok + ["DL:%d" % r for r in more]
        if (bank, b) == ("pL", 3):
            calls.append(lambda: p.matmul(T.pL[:, 1, :, 7], T.HI[:], T.bfl[:], False, False))
            ctok = ctok + ["HI", "bfl"]
        calls += [(lambda q=q: p.matmul(out, T[sl][:, 128 * q:128 * q + 128], T[src][:, 512 * b + q:512 * b + 512:16, :], False, q == 15))
                  for q in range(16)]
        do("P", ["ID", sl, ] + ["%s:%d%s" % (src, r, z) for r in (2 * b, 2 * b + 1) for z in ("", "+")] + ctok, ["%s:%d" % (bank, b)], calls, len(calls) * 64 * 0.42e-3)

    def whole(bank):
        return ["%s:%d" % (bank, b) for b in range(4)]

    def counts(t, kind):
        lst, gb, xb, bank, ns = kind + "16", "G" + kind, "X" + kind, "p" + kind, SPAIRS[kind][t]
        yv = "y%d" % (t % 2)
        for r in range(ns + 1):
            if r < ns and r % WIDE == 0:
                e = min(ns, r + WIDE)
                a = names(lst, t, 2 * r, 2 * e)
                do("S", a[1], ["%s:%d" % (gb, z) for z in range(r, e)],
                   [lambda a=a, r=r, e=e: s_.activation(out=T[gb][:, 512 * r:512 * e], in_=a[0], func=AF.Copy)], gcyc(a[2]))
            if r:
                differ(yv, gb, r - 1, xb, AF.Sign, -0.5)
        for r in range(7, ns - 1, -1):
            a, o = names(lst, t, 2 * r, 2 * r + 2), pair(xb if kind == "C" else "DL", r)
            if kind == "C" and t and r >= 8 - SPLIT:
                for e in range(2):
                    a = names(lst, t, 2 * r + e, 2 * r + e + 1)
                    c = slice(512 * (r // 2) + 256 * e, 512 * (r // 2) + 256 * e + 256)
                    do("V", a[1] + [yv], [o[1] + "+" * e],
                       [lambda a=a, c=c, r=r: v.tensor_tensor(out=T.XC[:, c, r % 2], in0=a[0], in1=T[yv][:, 0:256], op=A.is_gt)], gcyc(256))
                continue
            do("V", a[1] + [yv, yv + "b"], [o[1]],
               [lambda a=a, o=o: v.tensor_tensor(out=o[0], in0=a[0], in1=T[yv][:], op=A.is_gt if kind == "C" else A.subtract)],
               gcyc(512) * TTG)
            if kind == "L":
                ts(pair("XL", r), o, 0.0, A.is_gt, k=0.5)
        for b in range(4):
            s = min(2, max(0, ns - 2 * b))
            sums(xb, bank, "SELC", T.THR[:, :, 2 - s:4 - s], ["THa", "THb"], b,
                 [] if not t or kind not in EARLY else [("HI", "eC"), ("LO", "e2")] if kind == "C" else [("HI", "eL")])

    def keyed(o, bank, b, c0):
        do("V", whole(bank) + [b[1]], [o],
           [(lambda e=e: v.tensor_tensor(out=T[o][:, e:256:2], in0=T[bank][:, e], in1=T[b[0]][:, c0 + e:c0 + 256:2], op=A.max))
            for e in range(2)], cyc(256))

    dst = T.cores[(rank + HOP) % len(T.cores)]
    rid, pid = topo.addr(dst, core)
    msk = topo.mask(core, dst)
    neng = len(topo.engines(core, dst))
    sent = [0]

    def send(kind, t):
        n = 16 if kind[0] == "V" else 256
        c = slice(n * t, n * t + n)
        d = slice(n * t + n, n * t + 2 * n)
        a = "a%s_%d" % (kind, t + 1)
        do("G", ["%s_%d" % (kind, t)], ["net" + a],
           lambda: g.remote_dma(T["r" + kind][:, d], T[kind][:, c], T.sem[a], T.sem.sent, pid, rid, msk), 0.8, "send")
        do("W", ["net" + a], ["wire" + a], [], n / 116.0, "land")
        do("N", ["wire" + a], ["r%s_%d" % (kind, t + 1)], [], NET, "land")["sig"] = (a, neng)
        sent[0] += neng

    def u_sum(yv):
        pu = cols("pM", 0, 16, "pM:u")
        mm(pu, [(selq("SELC", q), X(yv, (slice(None), slice(q, 256, 16)))) for q in range(16)])
        act(odd("UX"), pu, AF.Identity, -1.0 / BIG, 32.0)
        act(F("sq"), pu, AF.Square, -0.5 / BIG, 296.0)

    def update(kind, val, old, new):
        e_row, e_val, R, e = "ER" + kind, "EV" + kind, "R" + kind, "e" + kind
        pa = cols("pT", 0, 256, "pT:a")
        ts(first(e_row), val, 2.0 ** (-20 if kind == "C" else -16), A.mult, ROW0 - 0.48, A.add)
        cp(first(e_val), val)
        scan(X(R), X("D1h"), X(e_row), A.mult, A.add, 0.5)
        scan(pa, X("D1"), X(e_val), A.mult, A.add)
        ts(X(e), X(R), ROW0, A.is_equal, k=0.5)
        tt(pa, pa, old, A.subtract)
        tt(pa, pa, X(e), A.mult)
        tt(new, pa, old, A.add)

    def late_row(val, yv):
        l17, p17 = cols("U16", 32, 48, "l17"), cols("pM", 32, 48, "pM:x")
        ts(I("n17"), val, 3, SHR, 4095, AND)
        cp(l17, I("n17"))
        tt(X("x17"), (pw[0].indirect(l17[0]), pw[1] + ["l17"], 256), cols(yv, 0, 256), A.is_gt)
        mm(p17, [(X("ID"), X("THR", (slice(None), slice(0, 16), 2), "THb"))]
           + [(selq("SELC", q), X("x17", (slice(None), slice(q, 256, 16)))) for q in range(16)])
        tt(first("ER2"), p17, first("ERC"), A.max)
        scan(X("R2"), X("D1h"), X("ER2"), A.mult, A.add, 0.5)
        ts(X("e2"), X("R2"), ROW0, A.is_equal, k=0.5)

    def late_lemma(val, yv):
        l17, pc, ps = cols("U16", 48, 64, "m17"), cols("pM", 48, 64, "pM:c"), cols("pM", 64, 80, "pM:s")
        ts(I("m17"), val, 3, SHR, 2047, AND)
        cp(l17, I("m17"))
        tt(X("d17"), (pw[0].indirect(l17[0]), pw[1] + ["m17"], 256), cols(yv, 0, 256), A.subtract)
        ts(X("g17"), X("d17"), 0.0, A.is_gt, k=0.5)
        act(X("a17"), X("d17"), AF.Abs)
        ts(F("far"), val, -float(2 ** 23), A.add)
        mm(pc, [(X("ID"), X("THR", (slice(None), slice(0, 16), 2), "THb"))]
           + [(selq("SELC", q), X("g17", (slice(None), slice(q, 256, 16)))) for q in range(16)])
        tt(F("k17"), pc, val, A.max)
        mm(ps, [(X("KI16"), first("ERL"))] + [(selq("SELC", q), X("a17", (slice(None), slice(q, 256, 16)))) for q in range(16)])
        act(F("s0"), ps, AF.Copy, -16.0 / BIG)
        tt(F("s17"), F("s0"), F("far"), A.max)

    stores = [0]

    def store(q, name, src, us=2.3):
        o = do(q, [src[1]], ["st" + name], lambda: eng[q].dma_start(T[name][:], src[0]).then_inc(T.sem.outs, 16), 0.1, "store")
        do("N", ["st" + name], [], [], us, "land")
        stores[0] += 16

    u_sum("y0")

    for t in range(TV):
        last = t == TV - 1
        since[0] = len(ops) - (2000 if t == 0 else 1000 if last else 0)
        yv, yn = "y%d" % (t % 2), "y%d" % (1 - t % 2)
        c0, c1 = 256 * t, 256 * t + 256
        pk, lk = cols("PK", c0, c1, "PK_%d" % t), cols("LK", c0, c1, "LK_%d" % t)
        vc, vl = cols("VC", 16 * t, 16 * t + 16, "VC_%d" % t), cols("VL", 16 * t, 16 * t + 16, "VL_%d" % t)
        for kind, nm, word, tmp, top in (("C", "PK", pk, X("i1"), 4095), ("L", "LK", lk, X("i2"), 2047)):
            if t:
                val = cols("rV" + kind, 16 * t, 16 * t + 16, "rV%s_%d" % (kind, t))
                old = cols("r" + nm, c0, c1, "r%s_%d" % (nm, t))
                update(kind, val, old, word)
                ts(tmp, by(old if kind in EARLY else word, perm), 3, SHR, top, AND)
                cp(cols(kind + "16", c0, c1, "%s16_%d" % (kind, t)), tmp)
                if kind in EARLY:
                    (late_row if kind == "C" else late_lemma)(val, yv)
            if not last:
                send(nm, t)
        counts(t, "C")
        lp = cols("pM", 256, 512, "pM:l")
        mm(lp, [(cols("RLM", 128 * t, 128 * t + 128, "RLM_%d" % t), X("RK"))])
        x, sl = X("i0"), I("sl")
        ts(x, pk, 0x4007, AND)
        tt(X("KC"), lp, pk, A.add)
        scan(X("SS"), X("DS"), x, A.add, A.max)
        ts(sl, final("SS"), -16.0, A.mult, -1.0, A.add)
        ts(sl, sl, 15, AND)
        ts(F("sP"), sl, float(2 ** 20), A.mult)
        keyed("key", "pC", ("KC", "KC"), 0)
        scan(X("SB"), X("D0"), X("key"), A.max, A.min)
        mb = mi = final("SB")
        tb = final("DG")
        ts(X("bfl", None, None, 16), mb, CAP, A.is_lt)
        ts(tb, mb, CAP, A.is_lt, NONE, A.mult)
        ts(I("lim"), mi, 14, SHR, 3, AND)
        ts(I("b"), mi, 7, AND)
        ts(nth("NB", 0), mi, 0x3FFF, AND)
        ts(nth("NA", 2), mi, 0x1FF0000, AND)
        ts(nth("QB", 2), mi, 0x0F3FF8, AND)
        tt(F("bl"), I("b"), I("lim"), A.subtract)
        tt(F("ov"), F("bl"), I("w"), A.is_ge)
        ts(nth("NB", 1), F("ov"), 16384.0, A.mult)
        ts(nth("QB", 1), F("ov"), -NONE, A.mult, NONE, A.add)
        scan4("N", A.add, A.max)
        if not last:
            mm(cols("pM", 16, 32, "pM:w"), [(cols("RK", 0, 128), X("bfl"))])
            cp(I("w"), cols("pM", 16, 32, "pM:w"))
            ts(I("w"), I("w"), 3, AND)
        ts(I("fs"), F("sq"), 8.0 * t - 296.0 * 296.0, A.add)
        ts(I("fs"), I("fs"), 16376, AND)
        tt(nth("QA", 1), I("fs"), tb, A.subtract)
        counts(t, "L")
        late = t and "L" in EARLY
        ns = SPAIRS["L"][t]
        for r in range(7, ns - 1, -1):
            if r < 8 - RELU[t]:
                act(pair("AB", r), pair("DL", r), AF.Abs)
            else:
                ts(pair("AB", r), pair("DL", r), -2.0, A.mult, 0.0, A.max, k=0.5)
        for r in range(ns):
            differ(yv, "GL", r, "AB", AF.Abs, 0.0)
        for b in (3, 2, 1, 0):
            sums("AB", "pS", "SELC", T.KB[:, :, 2 * b:2 * b + 2], ["KB"], b, [("FAR", "eL")] if late else [], [r for r in (2 * b, 2 * b + 1) if r >= 8 - RELU[t]])
        keyed("keyL", "pL", ("LK", lk[1]), c0)
        scan(X("SG"), X("DG"), X("keyL"), A.max, A.min)
        gq = final("SG")
        if late:
            tt(F("k17"), F("k17"), tb, A.max)
            tt(I("gq"), gq, F("k17"), A.min)
            gq = I("gq")
        tt(F("ng"), F("sP"), gq, A.add)
        tt(vc, F("ng"), nth("NC", 2), A.min)
        if last:
            update("C", vc, pk, mid("Ya"))
        else:
            send("VC", t)
        a16, n16 = cols("U16", 0, 16, "a16"), cols("U16", 16, 32, "n16")
        y, y2 = cols(yv, 0, 256), cols(yn, 0, 256)
        al, ax = X("AX", (slice(None), slice(32 * t, 32 * t + 32, 2)), None, 16), cols("AX", 32 * t, 32 * t + 32)
        ts(al, gq, 3, SHR, 4095, AND)
        ts(nth("HB", 2), gq, CAP, A.is_lt, -18432.0, A.mult)
        ts(nth("HB", 3), gq, 0x10F0000, AND)
        cp(a16, al)
        do("V", ["UX", "UX1", "AX"], ["HX"],
           [lambda ax=ax: v.tensor_tensor_scan(out=T.HX[:], data0=T.UX[:], data1=ax[0], initial=0.0, op0=A.mult, op1=A.add)], cyc(32))
        ts(nth("HB", 0), X("HX", (slice(None), slice(1, 32, 2)), None, 16), 2, SHR, 14336, AND)
        scan4("H", A.mult, A.add)
        ts(n16, nth("HC", 2), 0.125, A.mult)
        pa = (pw[0].indirect(a16[0]), pw[1] + ["a16"], 256)
        act(X("pa"), pa, AF.Copy)
        dy = X("pC", (slice(None), slice(2, 4)), "pC:y")
        mm(dy, [(X("ID"), X("pa")), (X("NID"), y)])
        act(y2, dy, AF.Abs)
        if MN_ON_V[t]:
            tt(X("mn"), pa, y, A.min)
        else:
            dm = X("pL", (slice(None), slice(2, 4)), "pL:m")
            mm(dm, [(X("ID"), X("pa")), (X("ID"), y), (X("NID"), y2)])
            act(X("mn"), dm, AF.Copy, 0.5)
        do("V", ["mn", "n16"], ["P"],
           [lambda: v.tensor_copy(out=T.P[:, 16:4368].indirect(T.U16[:, 16:32]), in_=T.mn[:])], 0.85)
        if not last:
            if DUP_ON_G:
                sel(cols(yn, 256, 512, yn + "b"), y2, [[0, 256]], A.is_ge, 0.0, 0, 0)
            else:
                act(cols(yn, 256, 512, yn + "b"), dy, AF.Abs)
            u_sum(yn)
        if last:
            store("Y", "zp", cols("P", 16, 2064), 4.5)
            store("Y", "zy", y2)
            turned = by(turn("Ya", "Za"), tm)
            cp(X("i0"), turned)
            act(X("h1"), turned, AF.Identity, 2.0 ** -16, T.col[:, 4:5], extra=["kb"])
            act(X("h1"), X("h1"), AF.Identity, 1.0, -ROW0)
            store("S", "zo", X("h1"))
            ts(X("i1"), X("i0"), 3, SHR, 4095, AND)
            ts(X("i2"), X("i0"), 7, AND)
            pe, pf = cols("pD0", 0, 256), cols("pD1", 0, 256)
            ts(pe, X("i1"), -2048.0, A.add)
            tt(X("h0"), pe, X("i2"), A.max)
            store("Y", "zb", X("h0"))
            ts(pf, X("i1"), 2048.0, A.is_lt, 4096.0, A.mult)
            act(pf, pf, AF.Identity, 1.0, -1.0)
            tt(X("f1"), pf, X("i1"), A.min)
            store("Y", "zc", X("f1"))
        do("S", whole("pS"), ["f4"],
           [(lambda e=e: s_.activation(out=T.f4[:, e:256:2], in_=T.pS[:, e], func=AF.Copy, scale=-16.0 / BIG))
            for e in range(2)], cyc(256))
        scan(X("SC"), X("D0"), X("f4"), A.max, A.min)
        ts(nth("QB", 3), gq, -1.0, A.mult, float(2 ** 22), A.add)
        ms = final("SC")
        if late:
            tt(F("ms"), ms, F("s17"), A.min)
            ms = F("ms")
        ts(I("ks"), ms, 65536.0, A.mult, -2.0 ** 31, A.add)
        ts(nth("QB", 0), I("ks"), 0xF0000, AND)
        scan4("Q", A.add, A.max)
        tt(vl, nth("QC", 3), nth("HC", 3), A.min)
        if last:
            update("L", vl, lk, mid("Yb"))
        else:
            send("VL", t)

    act(X("f3"), by(turn("Yb", "Zb"), tm), AF.Identity, 0.125, T.col[:, 3:4], extra=["k16"])
    store("S", "zl", X("f3"))
    emit()
    g.sync.wait_ge(T.sem.outs, stores[0])
    g.wait_ge(T.sem.sent, sent[0])
    for s in cnt:
        g.wait_ge(T.sem[s], cnt[s])
